import numpy as np
import ml_dtypes


def mxq(x, axis, fmt="e4m3"):
    dtype, down = {"e4m3": (ml_dtypes.float8_e4m3fn, 7), "e5m2": (ml_dtypes.float8_e5m2, 14)}[fmt]
    v = np.moveaxis(np.asarray(x, np.float32).astype(ml_dtypes.bfloat16).astype(np.float64), axis, -1)
    blocks = v.reshape(v.shape[:-1] + (-1, 32))
    amax = np.abs(blocks).max(-1, keepdims=True)
    byte = np.maximum(np.where(amax > 0, np.frexp(amax)[1] - 1 + 127, 0) - down, 1)
    scale = np.exp2(byte - 127.0)
    codes = (blocks / scale).astype(np.float32).astype(dtype).astype(np.float64)
    return np.moveaxis((codes * scale).reshape(v.shape), -1, axis)


WIDE = False


def mx_kscale(k):
    if not WIDE:
        return np.ones(k)
    levels = np.array([10, -10, 5, -5, 0])
    if k % 512:
        return np.exp2(np.random.permutation(np.resize(levels, k // 32))).repeat(32)
    a = np.empty((k // 512, 16))
    for p in range(k // 512):
        a[p, :8] = np.random.permutation(np.resize(levels, 8))
        for g in range(8):
            far = levels[np.abs(levels - a[p, g]) >= 10]
            a[p, g + 8] = far[np.random.randint(len(far))]
    return np.exp2(a.ravel()).repeat(32)


def f64(x):
    return np.asarray(x).astype(np.float64)


def striped(idx):
    return np.tile(idx.reshape(-1, 16).T, (8, 1)).astype(np.uint16)


def unstriped(offs):
    return offs[:16].T.reshape(-1).astype(np.int64)


def pack_weight(w):
    k, n = w.shape
    w = f64(np.asarray(w, np.float32).astype(ml_dtypes.bfloat16)).reshape(k // 32, 32, n)
    amax = np.abs(w).max(1)
    byte = np.clip(np.where(amax > 0, np.frexp(amax)[1] - 1 + 127 - 7, 1), 1, 254)
    scaled = (w * np.exp2(127.0 - byte)[:, None, :]).reshape(k, n).astype(np.float32)
    words = np.ascontiguousarray(scaled.reshape(k // 512, 128, 4, n).transpose(0, 1, 3, 2)).astype(ml_dtypes.float8_e4m3fn).view(np.uint8)
    return words, np.ascontiguousarray(byte.astype(np.uint8).reshape(k // 512, 16, n))


def unpack_weight(words, scales):
    g, p, n, _ = words.shape
    vals = np.ascontiguousarray(words).view(ml_dtypes.float8_e4m3fn).astype(np.float64) * np.repeat(np.exp2(scales.astype(np.float64) - 127.0), 8, axis=1)[..., None]
    return vals.transpose(0, 1, 3, 2).reshape(g * 512, n)


def planes(y):
    n, m = y.shape
    v = y.astype(np.float32).astype(ml_dtypes.bfloat16).astype(np.float64).reshape(n // 32, 32, m)
    top = np.abs(v).max(1)
    byte = np.clip(np.where(top > 0, np.frexp(top)[1] - 1 + 127 - 7, 1), 1, 254)
    codes = (v * np.exp2(127.0 - byte)[:, None, :]).reshape(n, m).astype(np.float32).astype(ml_dtypes.float8_e4m3fn).view(np.uint8)
    words = codes.reshape(n // 512, 128, 4, m).transpose(0, 1, 3, 2)
    return np.ascontiguousarray(words), np.ascontiguousarray(byte.astype(np.uint8).reshape(n // 512, 16, m))


def gelu(v):
    return 0.5 * v * (1.0 + np.tanh(np.sqrt(2.0 / np.pi) * (v + 0.044715 * v**3)))


K, T, S, D, V, H = 1024, 4096, 1024, 3, 512, 512
P = 2 ** 7


def setup_inputs():
    n = np.random.standard_normal
    s = mx_kscale(K)[:, None]
    u = mx_kscale(H)
    near = np.random.permutation(S)
    packed_xT = pack_weight(n((K, T)) * s)
    return {
        "x_words": packed_xT[0],
        "x_scales": packed_xT[1],
        "w1": (n((K, H)) / np.sqrt(K) / s * u).astype(np.float32),
        "w2": (n((H, H)) / np.sqrt(H) / u[:, None]).astype(np.float32),
        "gate": (np.tile(np.random.uniform(0.2, 1.0, (D, 1, V)) / np.sqrt(D), (1, P, 1))).astype(np.float32),
        "turn": (np.random.uniform(0.5, 1.5, (H, 1)) * u[:, None]).astype(np.float32),
        "offs": striped(np.random.permutation(T)[:S]),
        "cen": striped(np.random.permutation(S)[:V]),
        "pos1": striped(near[:V]),
        "pos2": striped(near[V:]),
        "pos3": striped(np.random.permutation(S)[:V]),
    }


def reference(x_words, x_scales, w1, w2, gate, turn, offs, cen, pos1, pos2, pos3):
    xq = unpack_weight(x_words, x_scales)[:, unstriped(offs)]
    h = gelu(mxq(f64(w1), 0, "e4m3").T @ xq)
    z = 0.9 * (h[:, unstriped(pos1)] * f64(gate)[0, :1] + h[:, unstriped(pos2)] * f64(gate)[1, :1] + h[:, unstriped(pos3)] * f64(gate)[2, :1]) + 0.1 * h[:, unstriped(cen)]
    y = mxq(f64(w2), 0, "e4m3").T @ mxq(z, 0, "e4m3")
    out_0 = 0.6 * z + 0.4 * (f64(turn) * y)
    return (out_0,) + planes(out_0)

@@ -1,0 +1,302 @@
+from contextlib import ExitStack
+
+import concourse.mybir as mybir
+from concourse.masks import make_identity
+
+K, T, S, D, V, H = 1024, 4096, 1024, 3, 512, 512
+FLOPS = 2 * K * H * S + 2 * H * H * V
+
+F32 = mybir.dt.float32
+BF16 = mybir.dt.bfloat16
+I32 = mybir.dt.int32
+U32 = mybir.dt.uint32
+U16 = mybir.dt.uint16
+U8 = mybir.dt.uint8
+FP8X4 = mybir.dt.float8_e4m3fn_x4
+MULT = mybir.AluOpType.mult
+ADD = mybir.AluOpType.add
+COPY = mybir.ActivationFunctionType.Copy
+GELU = mybir.ActivationFunctionType.Gelu_apprx_tanh
+
+P = 128
+PACK = 4
+K_PASS = P * PACK
+PASSES = K // K_PASS
+BANK = 512
+STRIPE = 16
+ROW_BLOCKS = H // P
+CHUNKS = V // P
+W1_LOADS = ((0, 1), (1, 2), (2, 4))
+
+
+def tile_picked_zgcnii_gelu_po_kernel(
+    tc, x_words, x_scales, w1, w2, gate, turn, offs, cen, pos1, pos2, pos3, out_0, out_1, out_2
+):
+    nc = tc.nc
+    with ExitStack() as ctx:
+        keep = ctx.enter_context(tc.tile_pool(name="keep", bufs=1))
+        ring = ctx.enter_context(tc.tile_pool(name="ring", bufs=2))
+        sums = ctx.enter_context(tc.psum_pool(name="sums", bufs=1))
+        work = ctx.enter_context(tc.psum_pool(name="work", bufs=4))
+
+        def load_list(name, dram):
+            tile = keep.tile(list(dram.shape), U16, name=name)
+            nc.sync.dma_start(tile[:], dram)
+            return tile
+
+        w1_raw = {}
+
+        def load_w1(first, last):
+            for g in range(PASSES):
+                raw = keep.tile([P, PACK, (last - first) * P], F32, name="w1_raw_%d_%d" % (first, g))
+                rows = w1[g * K_PASS : (g + 1) * K_PASS, first * P : last * P]
+                nc.sync.dma_start(out=raw[:], in_=rows.rearrange("(p j) c -> p j c", j=PACK))
+                for a in range(first, last):
+                    w1_raw[a, g] = raw[:, :, (a - first) * P : (a - first + 1) * P]
+
+        def load_x(g):
+            tile = keep.tile([P, T], I32, name="x_table_%d" % g, align_bytes=64)
+            nc.sync.dma_start(out=tile[:], in_=x_words[g].rearrange("p n r -> p (n r)").bitcast(I32))
+            return tile
+
+        scale_table = keep.tile([P, T], U8, align_bytes=64)
+        nc.vector.memset(scale_table[:].bitcast(I32), 0)
+        load_w1(*W1_LOADS[0])
+        offs_t = load_list("offs_t", offs)
+        gate_cols = keep.tile([P, D, PACK], F32)
+        nc.sync.dma_start(out=gate_cols[:], in_=gate[:, 0, :].rearrange("d (p e) -> p d e", e=PACK))
+        x_table = [load_x(0)]
+        for q in range(4):
+            nc.sync.dma_start(
+                out=scale_table[32 * q : 32 * q + 4 * PASSES, :].bitcast(I32),
+                in_=x_scales[:, 4 * q : 4 * q + 4, :].bitcast(I32),
+            )
+        x_table.append(load_x(1))
+        load_w1(*W1_LOADS[1])
+        pos_t = [load_list("pos1_t", pos1), load_list("pos2_t", pos2), load_list("pos3_t", pos3)]
+        cen_t = load_list("cen_t", cen)
+        load_w1(*W1_LOADS[2])
+        w2_raw = keep.tile([P, PACK, H], F32)
+        nc.sync.dma_start(out=w2_raw[:], in_=w2.rearrange("(p j) c -> p j c", j=PACK))
+        turn_raw = keep.tile([P, PACK], F32)
+        nc.sync.dma_start(out=turn_raw[:], in_=turn.rearrange("(p t) o -> p (t o)", t=PACK))
+
+        ident = keep.tile([P, P], F32)
+        make_identity(nc, ident[:])
+
+        w1_codes, w1_scales, w1_bf = {}, {}, {}
+
+        def round_w1(a, copy):
+            w1_bf[a] = keep.tile([P, PASSES, P, PACK], BF16, tag="w1_bf_%d" % a, name="w1_bf_%d" % a, align_bytes=64)
+            for g in range(PASSES):
+                copy(
+                    out=w1_bf[a][:, g, :, :].rearrange("p (c i) j -> p c j i", i=PACK),
+                    in_=w1_raw[a, g].rearrange("p j (c i) -> p c j i", i=PACK),
+                )
+
+        def quantize_w1(a):
+            w1_codes[a] = keep.tile([P, PASSES * P], U32, name="w1_codes_%d" % a, align_bytes=64)
+            w1_scales[a] = keep.tile([P, PASSES * P], U8, name="w1_scales_%d" % a, align_bytes=64)
+            nc.vector.quantize_mx(
+                out=w1_codes[a][:].bitcast(FP8X4),
+                scales=w1_scales[a][:],
+                in_=w1_bf[a][:].rearrange("p g c j -> p (g c j)"),
+            )
+
+        round_w1(0, nc.vector.tensor_copy)
+        quantize_w1(0)
+
+        gates = []
+        for d in range(D):
+            spread = work.tile([P, PACK, P], F32, tag="work", name="spread_%d" % d)
+            for e in range(PACK):
+                nc.tensor.transpose(spread[:, e, :], gate_cols[:, d, e : e + 1].to_broadcast([P, P]), ident[:])
+            gate_d = keep.tile([P, V], F32, name="gate_%d" % d)
+            nc.scalar.activation(
+                out=gate_d[:].rearrange("m (p e) -> m p e", e=PACK),
+                in_=spread[:].rearrange("m e p -> m p e"),
+                func=COPY,
+                scale=9.0,
+            )
+            gates.append(gate_d)
+
+        picked_scales = keep.tile([P, S], U8, align_bytes=64)
+        nc.vector.tensor_copy(picked_scales[:], scale_table[:].indirect(offs_t[:]))
+        picked = {}
+        whole = keep.tile([P, S], U32, name="picked_0", align_bytes=64)
+        nc.vector.tensor_copy(whole[:], x_table[0][:].bitcast(U32).indirect(offs_t[:]))
+        for half in range(S // BANK):
+            picked[0, half] = whole[:, half * BANK : (half + 1) * BANK]
+            part = keep.tile([P, BANK], U32, name="picked_1_%d" % half, align_bytes=64)
+            entries = offs_t[:, half * BANK // STRIPE : (half + 1) * BANK // STRIPE]
+            nc.vector.tensor_copy(part[:], x_table[1][:].bitcast(U32).indirect(entries))
+            picked[1, half] = part[:]
+
+        h = {}
+
+        def hidden(a):
+            h[a] = keep.tile([P, S], F32, name="h_%d" % a)
+            for half in range(S // BANK):
+                cols = slice(half * BANK, (half + 1) * BANK)
+                acc = work.tile([P, BANK], F32, tag="work", name="h_acc_%d_%d" % (a, half))
+                for g in range(PASSES):
+                    nc.tensor.matmul_mx(
+                        out=acc[:],
+                        lhsT=w1_codes[a][:, g * P : (g + 1) * P].bitcast(FP8X4),
+                        lhsT_scale=w1_scales[a][:, g * P : (g + 1) * P],
+                        rhs=picked[g, half].bitcast(FP8X4),
+                        rhs_scale=picked_scales[4 * g :, cols],
+                        start=(g == 0),
+                        stop=(g == PASSES - 1),
+                    )
+                nc.scalar.activation(out=h[a][:, cols], in_=acc[:], func=GELU)
+
+        z_sum = [sums.tile([P, H], F32, name="z_sum_%d" % c) for c in range(CHUNKS)]
+
+        def mix(a, first, last, behind):
+            width = (last - first) * P
+            cols = slice(first * P, last * P)
+            entries = slice(first * P // STRIPE, last * P // STRIPE)
+            terms = []
+
+            def place(n):
+                if n in behind:
+                    return keep.tile([P, width], F32, tag=behind[n], name="term_%d" % n, align_bytes=64)
+                return ring.tile([P, width], F32, tag="term_%d" % n, name="term_%d" % n)
+
+            for d in range(D):
+                term = place(d)
+                nc.vector.tensor_tensor(term[:], h[a][:].indirect(pos_t[d][:, entries]), gates[d][:, cols], MULT)
+                terms.append(term)
+            own = place(D)
+            nc.vector.tensor_tensor(own[:], h[a][:].indirect(cen_t[:, entries]), terms[0][:], ADD)
+            summands = terms[1:] + [own]
+            for n, summand in enumerate(summands):
+                for c in range(first, last):
+                    nc.tensor.matmul(
+                        out=z_sum[c][:, a * P : (a + 1) * P],
+                        lhsT=summand[:, (c - first) * P : (c - first + 1) * P],
+                        rhs=ident[:],
+                        start=(n == 0),
+                        stop=(n == len(summands) - 1),
+                        is_transpose=True,
+                    )
+
+        hidden(0)
+        round_w1(1, nc.vector.tensor_copy)
+        quantize_w1(1)
+        hidden(1)
+        mix(0, 0, CHUNKS, {0: "w1_bf_1"})
+        for a in (2, 3):
+            round_w1(a, nc.scalar.copy)
+            quantize_w1(a)
+            hidden(a)
+
+        w2_bf = keep.tile([P, PACK, P, PACK], BF16, tag="w2_bf", align_bytes=64)
+        for m0 in range(0, P, P // 2):
+            nc.scalar.copy(
+                out=w2_bf[:, :, m0 : m0 + P // 2, :].rearrange("p t m j -> p m j t"),
+                in_=w2_raw[:, :, PACK * m0 : PACK * (m0 + P // 2)].rearrange("p j (m t) -> p m j t", t=PACK),
+            )
+        w2_codes = keep.tile([P, H], U32, align_bytes=64)
+        w2_scales = keep.tile([P, H], U8, align_bytes=64)
+        nc.vector.quantize_mx(
+            out=w2_codes[:].bitcast(FP8X4), scales=w2_scales[:], in_=w2_bf[:].rearrange("p t m j -> p (t m j)")
+        )
+        mix(1, 0, CHUNKS, {0: "w1_bf_2", 2: "w1_bf_3"})
+        turn_t = keep.tile([P, PACK], F32)
+        nc.scalar.activation(out=turn_t[:], in_=turn_raw[:], func=COPY, scale=0.4)
+
+        out_codes = keep.tile([P, V], U32, align_bytes=64)
+        out_scales = keep.tile([P, V], U8, align_bytes=64)
+        z_bf, z_part, y, out_bf = {}, {}, {}, {}
+
+        def turn_back(c):
+            z_rows = keep.tile([P, PACK, P], F32, tag="z_rows_%d" % c, name="z_rows", align_bytes=64)
+            nc.scalar.copy(out=z_rows[:], in_=z_sum[c][:].rearrange("v (p t) -> v t p", t=PACK))
+            z_back = work.tile([P, PACK, P], F32, tag="work", name="z_back_%d" % c)
+            for t in range(PACK):
+                nc.tensor.transpose(z_back[:, t, :], z_rows[:, t, :], ident[:])
+            z_bf[c] = keep.tile([P, P, PACK], BF16, tag="z_bf_%d" % c, name="z_bf", align_bytes=64)
+            nc.scalar.activation(out=z_bf[c][:], in_=z_back[:].rearrange("p t v -> p v t"), func=COPY, scale=0.1)
+            z_part[c] = keep.tile([P, PACK, P], F32, tag="z_part_%d" % c, name="z_part", align_bytes=64)
+            nc.scalar.activation(out=z_part[c][:], in_=z_back[:], func=COPY, scale=0.06)
+
+        def second_product(c):
+            z_codes = ring.tile([P, P], U32, tag="z_codes", name="z_codes", align_bytes=64)
+            z_scales = ring.tile([P, P], U8, tag="z_scales", name="z_scales", align_bytes=64)
+            nc.vector.quantize_mx(
+                out=z_codes[:].bitcast(FP8X4), scales=z_scales[:], in_=z_bf[c][:].rearrange("p v t -> p (v t)")
+            )
+            y[c] = work.tile([P, PACK, P], F32, tag="work", name="y_%d" % c)
+            for t in range(PACK):
+                nc.tensor.matmul_mx(
+                    out=y[c][:, t, :],
+                    lhsT=w2_codes[:, t * P : (t + 1) * P].bitcast(FP8X4),
+                    lhsT_scale=w2_scales[:, t * P : (t + 1) * P],
+                    rhs=z_codes[:].bitcast(FP8X4),
+                    rhs_scale=z_scales[:],
+                    start=True,
+                    stop=True,
+                )
+
+        def combine(c):
+            cols = slice(c * P, (c + 1) * P)
+            result = ring.tile([P, PACK, P], F32, tag="result", name="result")
+            for t in range(PACK):
+                nc.vector.scalar_tensor_tensor(
+                    out=result[:, t, :],
+                    in0=y[c][:, t, :],
+                    scalar=turn_t[:, t : t + 1],
+                    in1=z_part[c][:, t, :],
+                    op0=MULT,
+                    op1=ADD,
+                )
+            nc.sync.dma_start(out=out_0[:, cols].rearrange("(p t) v -> p t v", t=PACK), in_=result[:])
+            out_bf[c] = keep.tile([P, P, PACK], BF16, tag="out_bf_%d" % c, name="out_bf", align_bytes=64)
+            copy = nc.vector.tensor_copy if c == CHUNKS - 1 else nc.scalar.copy
+            copy(
+                out=out_bf[c][:].rearrange("p (v i) t -> p v t i", i=PACK),
+                in_=result[:].rearrange("p t (v i) -> p v t i", i=PACK),
+            )
+
+        def hand_on(c):
+            cols = slice(c * P, (c + 1) * P)
+            nc.vector.quantize_mx(
+                out=out_codes[:, cols].bitcast(FP8X4),
+                scales=out_scales[:, cols],
+                in_=out_bf[c][:].rearrange("p v t -> p (v t)"),
+            )
+            nc.sync.dma_start(
+                out=out_1[0].rearrange("p n r -> p (n r)").bitcast(I32)[:, cols], in_=out_codes[:, cols].bitcast(I32)
+            )
+
+        for step in range(CHUNKS + 3):
+            if 0 <= step - 2 < CHUNKS:
+                second_product(step - 2)
+            if 0 <= step - 3 < CHUNKS:
+                hand_on(step - 3)
+            if step < CHUNKS:
+                behind = {}
+                if step == 1:
+                    behind[0] = "w2_bf"
+                if step >= 2:
+                    behind[0] = "z_bf_%d" % (step - 2)
+                if step >= 3:
+                    behind[1] = "out_bf_%d" % (step - 3)
+                mix(2, step, step + 1, behind)
+            if 0 <= step - 2 < CHUNKS:
+                combine(step - 2)
+            if step < CHUNKS:
+                behind = {}
+                if step >= 1:
+                    behind[1] = "z_rows_%d" % (step - 1)
+                if step >= 2:
+                    behind[0] = "z_part_%d" % (step - 2)
+                mix(3, step, step + 1, behind)
+                turn_back(step)
+
+        for q in range(4):
+            nc.sync.dma_start(
+                out=out_2[0, 4 * q : 4 * q + 4, :].bitcast(I32), in_=out_scales[32 * q : 32 * q + 4, :].bitcast(I32)
+            )

@@ -26,6 +26,9 @@ BANK = 512
 STRIPE = 16
 ROW_BLOCKS = H // P
 CHUNKS = V // P
+GROUP_CHUNKS = 2
+GROUP = GROUP_CHUNKS * P
+GROUPS = V // GROUP
 W1_LOADS = ((0, 1), (1, 2), (2, 4))
 
 
@@ -35,7 +38,7 @@ def tile_picked_zgcnii_gelu_po_kernel(
     nc = tc.nc
     with ExitStack() as ctx:
         keep = ctx.enter_context(tc.tile_pool(name="keep", bufs=1))
-        ring = ctx.enter_context(tc.tile_pool(name="ring", bufs=2))
+        ring = ctx.enter_context(tc.tile_pool(name="ring", bufs=3))
         sums = ctx.enter_context(tc.psum_pool(name="sums", bufs=1))
         work = ctx.enter_context(tc.psum_pool(name="work", bufs=4))
 
@@ -151,7 +154,7 @@ def tile_picked_zgcnii_gelu_po_kernel(
                     )
                 nc.scalar.activation(out=h[a][:, cols], in_=acc[:], func=GELU)
 
-        z_sum = [sums.tile([P, H], F32, name="z_sum_%d" % c) for c in range(CHUNKS)]
+        z_sum = [sums.tile([P, H], F32, tag="z_sum_%d" % c, name="z_sum_%d" % c) for c in range(CHUNKS)]
 
         def mix(a, first, last, behind):
             width = (last - first) * P
@@ -207,96 +210,124 @@ def tile_picked_zgcnii_gelu_po_kernel(
         turn_t = keep.tile([P, PACK], F32)
         nc.scalar.activation(out=turn_t[:], in_=turn_raw[:], func=COPY, scale=0.4)
 
+        mix(2, 0, CHUNKS, {2: "w2_bf"})
+
         out_codes = keep.tile([P, V], U32, align_bytes=64)
         out_scales = keep.tile([P, V], U8, align_bytes=64)
-        z_bf, z_part, y, out_bf = {}, {}, {}, {}
+        z_rows, z_back, z_bf, z_part, y, result = {}, {}, {}, {}, {}, {}
 
-        def turn_back(c):
-            z_rows = keep.tile([P, PACK, P], F32, tag="z_rows_%d" % c, name="z_rows", align_bytes=64)
-            nc.scalar.copy(out=z_rows[:], in_=z_sum[c][:].rearrange("v (p t) -> v t p", t=PACK))
-            z_back = work.tile([P, PACK, P], F32, tag="work", name="z_back_%d" % c)
-            for t in range(PACK):
-                nc.tensor.transpose(z_back[:, t, :], z_rows[:, t, :], ident[:])
-            z_bf[c] = keep.tile([P, P, PACK], BF16, tag="z_bf_%d" % c, name="z_bf", align_bytes=64)
-            nc.scalar.activation(out=z_bf[c][:], in_=z_back[:].rearrange("p t v -> p v t"), func=COPY, scale=0.1)
-            z_part[c] = keep.tile([P, PACK, P], F32, tag="z_part_%d" % c, name="z_part", align_bytes=64)
-            nc.scalar.activation(out=z_part[c][:], in_=z_back[:], func=COPY, scale=0.06)
+        def copy_rows(c, first, last):
+            ps = slice(first * P // PACK, last * P // PACK)
+            nc.scalar.copy(out=z_rows[c][:, :, ps], in_=z_sum[c][:].rearrange("v (p t) -> v t p", t=PACK)[:, :, ps])
 
-        def second_product(c):
-            z_codes = ring.tile([P, P], U32, tag="z_codes", name="z_codes", align_bytes=64)
-            z_scales = ring.tile([P, P], U8, tag="z_scales", name="z_scales", align_bytes=64)
-            nc.vector.quantize_mx(
-                out=z_codes[:].bitcast(FP8X4), scales=z_scales[:], in_=z_bf[c][:].rearrange("p v t -> p (v t)")
-            )
-            y[c] = work.tile([P, PACK, P], F32, tag="work", name="y_%d" % c)
-            for t in range(PACK):
-                nc.tensor.matmul_mx(
-                    out=y[c][:, t, :],
-                    lhsT=w2_codes[:, t * P : (t + 1) * P].bitcast(FP8X4),
-                    lhsT_scale=w2_scales[:, t * P : (t + 1) * P],
-                    rhs=z_codes[:].bitcast(FP8X4),
-                    rhs_scale=z_scales[:],
-                    start=True,
-                    stop=True,
+        for c in range(CHUNKS):
+            z_rows[c] = keep.tile([P, PACK, P], F32, tag="z_rows_%d" % c, name="z_rows_%d" % c, align_bytes=64)
+            copy_rows(c, 0, ROW_BLOCKS - 1)
+
+        def chunks_of(group):
+            return range(group * GROUP_CHUNKS, (group + 1) * GROUP_CHUNKS)
+
+        def cols_in_group(c):
+            return slice((c % GROUP_CHUNKS) * P, (c % GROUP_CHUNKS + 1) * P)
+
+        def finish_rows(group):
+            for c in chunks_of(group):
+                copy_rows(c, ROW_BLOCKS - 1, ROW_BLOCKS)
+
+        def turn_back(group):
+            for c in chunks_of(group):
+                z_back[c] = work.tile([P, PACK, P], F32, tag="work", name="z_back_%d" % c)
+                for t in range(PACK):
+                    nc.tensor.transpose(z_back[c][:, t, :], z_rows[c][:, t, :], ident[:])
+            z_bf[group] = keep.tile([P, GROUP, PACK], BF16, name="z_bf_%d" % group, align_bytes=64)
+            for c in chunks_of(group):
+                nc.scalar.activation(
+                    out=z_bf[group][:, cols_in_group(c), :],
+                    in_=z_back[c][:].rearrange("p t v -> p v t"),
+                    func=COPY,
+                    scale=0.1,
                 )
 
-        def combine(c):
-            cols = slice(c * P, (c + 1) * P)
-            result = ring.tile([P, PACK, P], F32, tag="result", name="result")
+        def keep_part(group):
+            z_part[group] = keep.tile([P, PACK, GROUP], F32, name="z_part_%d" % group)
+            for c in chunks_of(group):
+                part = z_part[group][:, :, cols_in_group(c)]
+                if c == 1:
+                    nc.vector.tensor_scalar(out=part, in0=z_back[c][:], scalar1=0.06, scalar2=None, op0=MULT)
+                else:
+                    nc.scalar.activation(out=part, in_=z_back[c][:], func=COPY, scale=0.06)
+
+        def second_product(group):
+            z_codes = keep.tile([P, GROUP], U32, name="z_codes_%d" % group, align_bytes=64)
+            z_scales = keep.tile([P, GROUP], U8, name="z_scales_%d" % group, align_bytes=64)
+            nc.vector.quantize_mx(
+                out=z_codes[:].bitcast(FP8X4), scales=z_scales[:], in_=z_bf[group][:].rearrange("p v t -> p (v t)")
+            )
+            for n, c in enumerate(chunks_of(group)):
+                bank = sums.tile([P, BANK // GROUP, GROUP], F32, tag="z_sum_%d" % c, name="y_%d" % c)
+                for slot in range(BANK // GROUP):
+                    t = n * (BANK // GROUP) + slot
+                    y[group, t] = bank[:, slot, :]
+                    nc.tensor.matmul_mx(
+                        out=y[group, t],
+                        lhsT=w2_codes[:, t * P : (t + 1) * P].bitcast(FP8X4),
+                        lhsT_scale=w2_scales[:, t * P : (t + 1) * P],
+                        rhs=z_codes[:].bitcast(FP8X4),
+                        rhs_scale=z_scales[:],
+                        start=True,
+                        stop=True,
+                    )
+
+        def combine(group):
+            cols = slice(group * GROUP, (group + 1) * GROUP)
+            result[group] = keep.tile([P, PACK, GROUP], F32, name="result_%d" % group)
+            rows = out_0[:, cols].rearrange("(p t) v -> p t v", t=PACK)
             for t in range(PACK):
                 nc.vector.scalar_tensor_tensor(
-                    out=result[:, t, :],
-                    in0=y[c][:, t, :],
+                    out=result[group][:, t, :],
+                    in0=y[group, t],
                     scalar=turn_t[:, t : t + 1],
-                    in1=z_part[c][:, t, :],
+                    in1=z_part[group][:, t, :],
                     op0=MULT,
                     op1=ADD,
                 )
-            nc.sync.dma_start(out=out_0[:, cols].rearrange("(p t) v -> p t v", t=PACK), in_=result[:])
-            out_bf[c] = keep.tile([P, P, PACK], BF16, tag="out_bf_%d" % c, name="out_bf", align_bytes=64)
-            copy = nc.vector.tensor_copy if c == CHUNKS - 1 else nc.scalar.copy
-            copy(
-                out=out_bf[c][:].rearrange("p (v i) t -> p v t i", i=PACK),
-                in_=result[:].rearrange("p t (v i) -> p v t i", i=PACK),
-            )
+                if t % 2 == 1:
+                    nc.sync.dma_start(out=rows[:, t - 1 : t + 1, :], in_=result[group][:, t - 1 : t + 1, :])
 
-        def hand_on(c):
-            cols = slice(c * P, (c + 1) * P)
+        def hand_on(group, shares):
+            cols = slice(group * GROUP, (group + 1) * GROUP)
+            out_bf = keep.tile([P, GROUP, PACK], BF16, name="out_bf_%d" % group, align_bytes=64)
+            for copy, share in shares:
+                copy(
+                    out=out_bf[:, share, :].rearrange("p (v i) t -> p v t i", i=PACK),
+                    in_=result[group][:, :, share].rearrange("p t (v i) -> p v t i", i=PACK),
+                )
             nc.vector.quantize_mx(
                 out=out_codes[:, cols].bitcast(FP8X4),
                 scales=out_scales[:, cols],
-                in_=out_bf[c][:].rearrange("p v t -> p (v t)"),
+                in_=out_bf[:].rearrange("p v t -> p (v t)"),
             )
             nc.sync.dma_start(
                 out=out_1[0].rearrange("p n r -> p (n r)").bitcast(I32)[:, cols], in_=out_codes[:, cols].bitcast(I32)
             )
 
-        for step in range(CHUNKS + 3):
-            if 0 <= step - 2 < CHUNKS:
-                second_product(step - 2)
-            if 0 <= step - 3 < CHUNKS:
-                hand_on(step - 3)
-            if step < CHUNKS:
-                behind = {}
-                if step == 1:
-                    behind[0] = "w2_bf"
-                if step >= 2:
-                    behind[0] = "z_bf_%d" % (step - 2)
-                if step >= 3:
-                    behind[1] = "out_bf_%d" % (step - 3)
-                mix(2, step, step + 1, behind)
-            if 0 <= step - 2 < CHUNKS:
-                combine(step - 2)
-            if step < CHUNKS:
-                behind = {}
-                if step >= 1:
-                    behind[1] = "z_rows_%d" % (step - 1)
-                if step >= 2:
-                    behind[0] = "z_part_%d" % (step - 2)
-                mix(3, step, step + 1, behind)
-                turn_back(step)
+        mix(3, 0, 2, {})
+        finish_rows(0)
+        turn_back(0)
+        mix(3, 2, 4, {3: "z_rows_0"})
+        finish_rows(1)
+        second_product(0)
+        keep_part(0)
+        turn_back(1)
+        keep_part(1)
+        combine(0)
+        second_product(1)
+        combine(1)
+        hand_on(0, [(nc.vector.tensor_copy, slice(0, GROUP))])
+        hand_on(1, [(nc.vector.tensor_copy, slice(0, 192)), (nc.scalar.copy, slice(192, GROUP))])
 
         for q in range(4):
-            nc.sync.dma_start(
+            queue = nc.sync if q % 2 == 0 else nc.scalar
+            queue.dma_start(
                 out=out_2[0, 4 * q : 4 * q + 4, :].bitcast(I32), in_=out_scales[32 * q : 32 * q + 4, :].bitcast(I32)
             )

@@ -24,12 +24,10 @@ K_PASS = P * PACK
 PASSES = K // K_PASS
 BANK = 512
 STRIPE = 16
-ROW_BLOCKS = H // P
+QUADRANTS = 4
 CHUNKS = V // P
-GROUP_CHUNKS = 2
-GROUP = GROUP_CHUNKS * P
-GROUPS = V // GROUP
-W1_LOADS = ((0, 1), (1, 2), (2, 4))
+HALF = P // 2
+GROUP = V // 2
 
 
 def tile_picked_zgcnii_gelu_po_kernel(
@@ -49,13 +47,12 @@ def tile_picked_zgcnii_gelu_po_kernel(
 
         w1_raw = {}
 
-        def load_w1(first, last):
+        def load_w1(side):
             for g in range(PASSES):
-                raw = keep.tile([P, PACK, (last - first) * P], F32, name="w1_raw_%d_%d" % (first, g))
-                rows = w1[g * K_PASS : (g + 1) * K_PASS, first * P : last * P]
+                raw = keep.tile([P, PACK, H // 2], F32, name="w1_raw_%d_%d" % (side, g))
+                rows = w1[g * K_PASS : (g + 1) * K_PASS, side * H // 2 : (side + 1) * H // 2]
                 nc.sync.dma_start(out=raw[:], in_=rows.rearrange("(p j) c -> p j c", j=PACK))
-                for a in range(first, last):
-                    w1_raw[a, g] = raw[:, :, (a - first) * P : (a - first + 1) * P]
+                w1_raw[side, g] = raw[:].rearrange("p j (m t) -> p m j t", t=PACK)
 
         def load_x(g):
             tile = keep.tile([P, T], I32, name="x_table_%d" % g, align_bytes=64)
@@ -64,21 +61,20 @@ def tile_picked_zgcnii_gelu_po_kernel(
 
         scale_table = keep.tile([P, T], U8, align_bytes=64)
         nc.vector.memset(scale_table[:].bitcast(I32), 0)
-        load_w1(*W1_LOADS[0])
+        load_w1(0)
         offs_t = load_list("offs_t", offs)
         gate_cols = keep.tile([P, D, PACK], F32)
         nc.sync.dma_start(out=gate_cols[:], in_=gate[:, 0, :].rearrange("d (p e) -> p d e", e=PACK))
         x_table = [load_x(0)]
-        for q in range(4):
+        for q in range(QUADRANTS):
             nc.sync.dma_start(
                 out=scale_table[32 * q : 32 * q + 4 * PASSES, :].bitcast(I32),
                 in_=x_scales[:, 4 * q : 4 * q + 4, :].bitcast(I32),
             )
         x_table.append(load_x(1))
-        load_w1(*W1_LOADS[1])
+        load_w1(1)
         pos_t = [load_list("pos1_t", pos1), load_list("pos2_t", pos2), load_list("pos3_t", pos3)]
         cen_t = load_list("cen_t", cen)
-        load_w1(*W1_LOADS[2])
         w2_raw = keep.tile([P, PACK, H], F32)
         nc.sync.dma_start(out=w2_raw[:], in_=w2.rearrange("(p j) c -> p j c", j=PACK))
         turn_raw = keep.tile([P, PACK], F32)
@@ -87,41 +83,49 @@ def tile_picked_zgcnii_gelu_po_kernel(
         ident = keep.tile([P, P], F32)
         make_identity(nc, ident[:])
 
-        w1_codes, w1_scales, w1_bf = {}, {}, {}
+        def quantize(name, values):
+            width = values.shape[1] // PACK
+            codes = keep.tile([P, width], U32, name=name + "_codes", align_bytes=64)
+            scales = keep.tile([P, width], U8, name=name + "_scales", align_bytes=64)
+            nc.vector.quantize_mx(out=codes[:].bitcast(FP8X4), scales=scales[:], in_=values)
+            return codes, scales
 
-        def round_w1(a, copy):
-            w1_bf[a] = keep.tile([P, PASSES, P, PACK], BF16, tag="w1_bf_%d" % a, name="w1_bf_%d" % a, align_bytes=64)
+        w1_mx = {}
+
+        def quantize_w1_low(side):
+            low = keep.tile([P, PASSES, 2, HALF, PACK], BF16, tag="w1_low_%d" % side, name="low", align_bytes=64)
             for g in range(PASSES):
-                copy(
-                    out=w1_bf[a][:, g, :, :].rearrange("p (c i) j -> p c j i", i=PACK),
-                    in_=w1_raw[a, g].rearrange("p j (c i) -> p c j i", i=PACK),
+                nc.vector.tensor_copy(
+                    out=low[:, g, :, :, :].rearrange("p t m j -> p m j t"), in_=w1_raw[side, g][:, :, :, 0:2]
+                )
+            codes, scales = quantize("w1_low_%d" % side, low[:].rearrange("p g t m j -> p (g t m j)"))
+            w1_mx[side] = (codes, scales, 0)
+
+        high = keep.tile([P, 2, PASSES, P, PACK], BF16, tag="w1_high", align_bytes=64)
+
+        def round_w1_high(side):
+            for g in range(PASSES):
+                nc.scalar.copy(
+                    out=high[:, :, g, side * HALF : (side + 1) * HALF, :].rearrange("p t m j -> p m j t"),
+                    in_=w1_raw[side, g][:, :, :, 2:4],
                 )
 
-        def quantize_w1(a):
-            w1_codes[a] = keep.tile([P, PASSES * P], U32, name="w1_codes_%d" % a, align_bytes=64)
-            w1_scales[a] = keep.tile([P, PASSES * P], U8, name="w1_scales_%d" % a, align_bytes=64)
-            nc.vector.quantize_mx(
-                out=w1_codes[a][:].bitcast(FP8X4),
-                scales=w1_scales[a][:],
-                in_=w1_bf[a][:].rearrange("p g c j -> p (g c j)"),
-            )
+        quantize_w1_low(0)
 
-        round_w1(0, nc.vector.tensor_copy)
-        quantize_w1(0)
-
-        gates = []
+        gates, last_gates = [], {}
         for d in range(D):
             spread = work.tile([P, PACK, P], F32, tag="work", name="spread_%d" % d)
             for e in range(PACK):
                 nc.tensor.transpose(spread[:, e, :], gate_cols[:, d, e : e + 1].to_broadcast([P, P]), ident[:])
-            gate_d = keep.tile([P, V], F32, name="gate_%d" % d)
-            nc.scalar.activation(
-                out=gate_d[:].rearrange("m (p e) -> m p e", e=PACK),
-                in_=spread[:].rearrange("m e p -> m p e"),
-                func=COPY,
-                scale=9.0,
-            )
-            gates.append(gate_d)
+            in_order = spread[:].rearrange("m e p -> m p e")
+            gate_d = keep.tile([P, P, PACK], F32, name="gate_%d" % d)
+            nc.scalar.activation(out=gate_d[:], in_=in_order, func=COPY, scale=9.0)
+            gates.append(gate_d[:].rearrange("m p e -> m (p e)"))
+            if d > 0:
+                last_d = keep.tile([P, P, PACK], F32, name="last_gate_%d" % d)
+                nc.scalar.activation(out=last_d[:], in_=in_order, func=COPY, scale=0.54)
+                last_gates[d] = last_d[:].rearrange("m p e -> m (p e)")
+        round_w1_high(0)
 
         picked_scales = keep.tile([P, S], U8, align_bytes=64)
         nc.vector.tensor_copy(picked_scales[:], scale_table[:].indirect(offs_t[:]))
@@ -137,171 +141,176 @@ def tile_picked_zgcnii_gelu_po_kernel(
 
         h = {}
 
-        def hidden(a):
-            h[a] = keep.tile([P, S], F32, name="h_%d" % a)
+        def hidden(block):
+            codes, scales, first = w1_mx[block]
+            h[block] = keep.tile([P, S], F32, name="h_%d" % block)
             for half in range(S // BANK):
                 cols = slice(half * BANK, (half + 1) * BANK)
-                acc = work.tile([P, BANK], F32, tag="work", name="h_acc_%d_%d" % (a, half))
+                acc = work.tile([P, BANK], F32, tag="work", name="h_acc_%d_%d" % (block, half))
                 for g in range(PASSES):
+                    w_cols = slice(first + g * P, first + (g + 1) * P)
                     nc.tensor.matmul_mx(
                         out=acc[:],
-                        lhsT=w1_codes[a][:, g * P : (g + 1) * P].bitcast(FP8X4),
-                        lhsT_scale=w1_scales[a][:, g * P : (g + 1) * P],
+                        lhsT=codes[:, w_cols].bitcast(FP8X4),
+                        lhsT_scale=scales[:, w_cols],
                         rhs=picked[g, half].bitcast(FP8X4),
                         rhs_scale=picked_scales[4 * g :, cols],
                         start=(g == 0),
                         stop=(g == PASSES - 1),
                     )
-                nc.scalar.activation(out=h[a][:, cols], in_=acc[:], func=GELU)
+                nc.scalar.activation(out=h[block][:, cols], in_=acc[:], func=GELU)
 
-        z_sum = [sums.tile([P, H], F32, tag="z_sum_%d" % c, name="z_sum_%d" % c) for c in range(CHUNKS)]
+        def term_tile(n, width, behind):
+            if n in behind:
+                return keep.tile([P, width], F32, tag=behind[n], name="term_%d" % n, align_bytes=64)
+            return ring.tile([P, width], F32, tag="term_%d" % n, name="term_%d" % n)
 
-        def mix(a, first, last, behind):
-            width = (last - first) * P
-            cols = slice(first * P, last * P)
-            entries = slice(first * P // STRIPE, last * P // STRIPE)
+        z_sum = [sums.tile([P, BANK], F32, tag="z_sum_%d" % c, name="z_sum_%d" % c) for c in range(CHUNKS)]
+
+        def mix(block, behind):
             terms = []
-
-            def place(n):
-                if n in behind:
-                    return keep.tile([P, width], F32, tag=behind[n], name="term_%d" % n, align_bytes=64)
-                return ring.tile([P, width], F32, tag="term_%d" % n, name="term_%d" % n)
-
             for d in range(D):
-                term = place(d)
-                nc.vector.tensor_tensor(term[:], h[a][:].indirect(pos_t[d][:, entries]), gates[d][:, cols], MULT)
+                term = term_tile(d, V, behind)
+                nc.vector.tensor_tensor(term[:], h[block][:].indirect(pos_t[d][:]), gates[d], MULT)
                 terms.append(term)
-            own = place(D)
-            nc.vector.tensor_tensor(own[:], h[a][:].indirect(cen_t[:, entries]), terms[0][:], ADD)
+            own = term_tile(D, V, behind)
+            nc.vector.tensor_tensor(own[:], h[block][:].indirect(cen_t[:]), terms[0][:], ADD)
             summands = terms[1:] + [own]
             for n, summand in enumerate(summands):
-                for c in range(first, last):
+                for c in range(CHUNKS):
                     nc.tensor.matmul(
-                        out=z_sum[c][:, a * P : (a + 1) * P],
-                        lhsT=summand[:, (c - first) * P : (c - first + 1) * P],
+                        out=z_sum[c][:, block * P : (block + 1) * P],
+                        lhsT=summand[:, c * P : (c + 1) * P],
                         rhs=ident[:],
                         start=(n == 0),
                         stop=(n == len(summands) - 1),
                         is_transpose=True,
                     )
 
+        z_part = keep.tile([P, PACK, V], F32)
+
+        def turn_back(t, first, rows):
+            back = work.tile([P, len(rows) * P], F32, tag="work", name="z_back_%d" % t)
+            for n, chunk_rows in enumerate(rows):
+                nc.tensor.transpose(back[:, n * P : (n + 1) * P], chunk_rows, ident[:])
+            nc.scalar.activation(
+                out=z_part[:, t, first * P : (first + len(rows)) * P], in_=back[:], func=COPY, scale=0.06
+            )
+
         hidden(0)
-        round_w1(1, nc.vector.tensor_copy)
-        quantize_w1(1)
+        quantize_w1_low(1)
         hidden(1)
-        mix(0, 0, CHUNKS, {0: "w1_bf_1"})
-        for a in (2, 3):
-            round_w1(a, nc.scalar.copy)
-            quantize_w1(a)
-            hidden(a)
+        mix(0, {0: "w1_low_1"})
+        round_w1_high(1)
+        codes, scales = quantize("w1_high", high[:].rearrange("p t g m j -> p (t g m j)"))
+        for block in (2, 3):
+            w1_mx[block] = (codes, scales, (block - 2) * PASSES * P)
+            hidden(block)
 
         w2_bf = keep.tile([P, PACK, P, PACK], BF16, tag="w2_bf", align_bytes=64)
-        for m0 in range(0, P, P // 2):
+        for m0 in range(0, P, HALF):
             nc.scalar.copy(
-                out=w2_bf[:, :, m0 : m0 + P // 2, :].rearrange("p t m j -> p m j t"),
-                in_=w2_raw[:, :, PACK * m0 : PACK * (m0 + P // 2)].rearrange("p j (m t) -> p m j t", t=PACK),
+                out=w2_bf[:, :, m0 : m0 + HALF, :].rearrange("p t m j -> p m j t"),
+                in_=w2_raw[:, :, PACK * m0 : PACK * (m0 + HALF)].rearrange("p j (m t) -> p m j t", t=PACK),
             )
-        w2_codes = keep.tile([P, H], U32, align_bytes=64)
-        w2_scales = keep.tile([P, H], U8, align_bytes=64)
-        nc.vector.quantize_mx(
-            out=w2_codes[:].bitcast(FP8X4), scales=w2_scales[:], in_=w2_bf[:].rearrange("p t m j -> p (t m j)")
-        )
-        mix(1, 0, CHUNKS, {0: "w1_bf_2", 2: "w1_bf_3"})
+        w2_codes, w2_scales = quantize("w2", w2_bf[:].rearrange("p t m j -> p (t m j)"))
+        mix(1, {0: "w1_high"})
         turn_t = keep.tile([P, PACK], F32)
         nc.scalar.activation(out=turn_t[:], in_=turn_raw[:], func=COPY, scale=0.4)
 
-        mix(2, 0, CHUNKS, {2: "w2_bf"})
+        low_rows = []
+        for c in range(CHUNKS):
+            rows = keep.tile([P, 2, 2, HALF], F32, tag="low_rows_%d" % c, name="low_rows", align_bytes=64)
+            nc.scalar.copy(out=rows[:], in_=z_sum[c][:, 0 : 2 * P].rearrange("v (s t m) -> v t s m", s=2, t=2))
+            low_rows.append(rows)
+        for t in range(2):
+            turn_back(t, 0, [rows[:, t, :, :].rearrange("v s m -> v (s m)") for rows in low_rows])
+
+        mix(2, {2: "w2_bf", D: "low_rows_0"})
+        for first in range(0, CHUNKS, 2):
+            third_rows = []
+            for c in (first, first + 1):
+                rows = keep.tile([P, P], F32, name="third_rows_%d" % c)
+                nc.scalar.copy(out=rows[:], in_=z_sum[c][:, 2 * P : 3 * P])
+                third_rows.append(rows[:])
+            turn_back(2, first, third_rows)
 
         out_codes = keep.tile([P, V], U32, align_bytes=64)
         out_scales = keep.tile([P, V], U8, align_bytes=64)
-        z_rows, z_back, z_bf, z_part, y, result = {}, {}, {}, {}, {}, {}
+        pair, own, z_bf, y, result = {}, {}, {}, {}, {}
 
-        def copy_rows(c, first, last):
-            ps = slice(first * P // PACK, last * P // PACK)
-            nc.scalar.copy(out=z_rows[c][:, :, ps], in_=z_sum[c][:].rearrange("v (p t) -> v t p", t=PACK)[:, :, ps])
+        def cols_of(group):
+            return slice(group * GROUP, (group + 1) * GROUP)
 
-        for c in range(CHUNKS):
-            z_rows[c] = keep.tile([P, PACK, P], F32, tag="z_rows_%d" % c, name="z_rows_%d" % c, align_bytes=64)
-            copy_rows(c, 0, ROW_BLOCKS - 1)
+        def entries_of(group):
+            return slice(group * GROUP // STRIPE, (group + 1) * GROUP // STRIPE)
 
-        def chunks_of(group):
-            return range(group * GROUP_CHUNKS, (group + 1) * GROUP_CHUNKS)
+        def interleave(copy, out, in_):
+            copy(out=out.rearrange("p (v i) t -> p v t i", i=PACK), in_=in_.rearrange("p t (v i) -> p v t i", i=PACK))
 
-        def cols_in_group(c):
-            return slice((c % GROUP_CHUNKS) * P, (c % GROUP_CHUNKS + 1) * P)
+        def last_neighbours(group):
+            terms = {}
+            for d in (1, 2, 0):
+                terms[d] = term_tile(d, GROUP, {})
+                weights = (gates[0] if d == 0 else last_gates[d])[:, cols_of(group)]
+                nc.vector.tensor_tensor(terms[d][:], h[3][:].indirect(pos_t[d][:, entries_of(group)]), weights, MULT)
+            pair[group] = keep.tile([P, GROUP], F32, name="pair_%d" % group)
+            nc.vector.tensor_tensor(pair[group][:], terms[1][:], terms[2][:], ADD)
+            return terms[0]
 
-        def finish_rows(group):
-            for c in chunks_of(group):
-                copy_rows(c, ROW_BLOCKS - 1, ROW_BLOCKS)
+        def last_own(group, first_term, behind):
+            own[group] = term_tile(D, GROUP, behind)
+            nc.vector.tensor_tensor(own[group][:], h[3][:].indirect(cen_t[:, entries_of(group)]), first_term[:], ADD)
 
-        def turn_back(group):
-            for c in chunks_of(group):
-                z_back[c] = work.tile([P, PACK, P], F32, tag="work", name="z_back_%d" % c)
-                for t in range(PACK):
-                    nc.tensor.transpose(z_back[c][:, t, :], z_rows[c][:, t, :], ident[:])
-            z_bf[group] = keep.tile([P, GROUP, PACK], BF16, name="z_bf_%d" % group, align_bytes=64)
-            for c in chunks_of(group):
-                nc.scalar.activation(
-                    out=z_bf[group][:, cols_in_group(c), :],
-                    in_=z_back[c][:].rearrange("p t v -> p v t"),
-                    func=COPY,
-                    scale=0.1,
-                )
+        def scaled_copy(out, in_):
+            nc.scalar.activation(out=out, in_=in_, func=COPY, scale=1.0 / 0.6)
 
-        def keep_part(group):
-            z_part[group] = keep.tile([P, PACK, GROUP], F32, name="z_part_%d" % group)
-            for c in chunks_of(group):
-                part = z_part[group][:, :, cols_in_group(c)]
-                if c == 1:
-                    nc.vector.tensor_scalar(out=part, in0=z_back[c][:], scalar1=0.06, scalar2=None, op0=MULT)
-                else:
-                    nc.scalar.activation(out=part, in_=z_back[c][:], func=COPY, scale=0.06)
+        def close_z(group):
+            nc.vector.scalar_tensor_tensor(
+                out=z_part[:, 3, cols_of(group)], in0=own[group][:], scalar=0.06, in1=pair[group][:], op0=MULT, op1=ADD
+            )
+            z_bf[group] = keep.tile([P, GROUP, PACK], BF16, tag="z_bf_%d" % group, name="z_bf", align_bytes=64)
+            interleave(scaled_copy, z_bf[group][:], z_part[:, :, cols_of(group)])
 
         def second_product(group):
-            z_codes = keep.tile([P, GROUP], U32, name="z_codes_%d" % group, align_bytes=64)
-            z_scales = keep.tile([P, GROUP], U8, name="z_scales_%d" % group, align_bytes=64)
-            nc.vector.quantize_mx(
-                out=z_codes[:].bitcast(FP8X4), scales=z_scales[:], in_=z_bf[group][:].rearrange("p v t -> p (v t)")
-            )
-            for n, c in enumerate(chunks_of(group)):
-                bank = sums.tile([P, BANK // GROUP, GROUP], F32, tag="z_sum_%d" % c, name="y_%d" % c)
-                for slot in range(BANK // GROUP):
-                    t = n * (BANK // GROUP) + slot
-                    y[group, t] = bank[:, slot, :]
-                    nc.tensor.matmul_mx(
-                        out=y[group, t],
-                        lhsT=w2_codes[:, t * P : (t + 1) * P].bitcast(FP8X4),
-                        lhsT_scale=w2_scales[:, t * P : (t + 1) * P],
-                        rhs=z_codes[:].bitcast(FP8X4),
-                        rhs_scale=z_scales[:],
-                        start=True,
-                        stop=True,
-                    )
+            z_codes, z_scales = quantize("z_%d" % group, z_bf[group][:].rearrange("p v t -> p (v t)"))
+            for t in range(PACK):
+                if t % 2 == 0:
+                    bank = sums.tile([P, 2, GROUP], F32, tag="z_sum_%d" % (2 * group + t // 2), name="y_bank")
+                y[group, t] = bank[:, t % 2, :]
+                nc.tensor.matmul_mx(
+                    out=y[group, t],
+                    lhsT=w2_codes[:, t * P : (t + 1) * P].bitcast(FP8X4),
+                    lhsT_scale=w2_scales[:, t * P : (t + 1) * P],
+                    rhs=z_codes[:].bitcast(FP8X4),
+                    rhs_scale=z_scales[:],
+                    start=True,
+                    stop=True,
+                )
 
         def combine(group):
-            cols = slice(group * GROUP, (group + 1) * GROUP)
             result[group] = keep.tile([P, PACK, GROUP], F32, name="result_%d" % group)
-            rows = out_0[:, cols].rearrange("(p t) v -> p t v", t=PACK)
+            rows = out_0[:, cols_of(group)].rearrange("(p t) v -> p t v", t=PACK)
             for t in range(PACK):
                 nc.vector.scalar_tensor_tensor(
                     out=result[group][:, t, :],
                     in0=y[group, t],
                     scalar=turn_t[:, t : t + 1],
-                    in1=z_part[group][:, t, :],
+                    in1=z_part[:, t, cols_of(group)],
                     op0=MULT,
                     op1=ADD,
                 )
                 if t % 2 == 1:
                     nc.sync.dma_start(out=rows[:, t - 1 : t + 1, :], in_=result[group][:, t - 1 : t + 1, :])
 
-        def hand_on(group, shares):
-            cols = slice(group * GROUP, (group + 1) * GROUP)
+        def hand_on(group, scalar_share):
+            cols = cols_of(group)
             out_bf = keep.tile([P, GROUP, PACK], BF16, name="out_bf_%d" % group, align_bytes=64)
-            for copy, share in shares:
-                copy(
-                    out=out_bf[:, share, :].rearrange("p (v i) t -> p v t i", i=PACK),
-                    in_=result[group][:, :, share].rearrange("p t (v i) -> p v t i", i=PACK),
-                )
+            for copy, share in (
+                (nc.scalar.copy, slice(0, scalar_share)),
+                (nc.vector.tensor_copy, slice(scalar_share, GROUP)),
+            ):
+                interleave(copy, out_bf[:, share, :], result[group][:, :, share])
             nc.vector.quantize_mx(
                 out=out_codes[:, cols].bitcast(FP8X4),
                 scales=out_scales[:, cols],
@@ -311,22 +320,19 @@ def tile_picked_zgcnii_gelu_po_kernel(
                 out=out_1[0].rearrange("p n r -> p (n r)").bitcast(I32)[:, cols], in_=out_codes[:, cols].bitcast(I32)
             )
 
-        mix(3, 0, 2, {})
-        finish_rows(0)
-        turn_back(0)
-        mix(3, 2, 4, {3: "z_rows_0"})
-        finish_rows(1)
+        last_own(0, last_neighbours(0), {})
+        close_z(0)
+        first_term = last_neighbours(1)
         second_product(0)
-        keep_part(0)
-        turn_back(1)
-        keep_part(1)
+        last_own(1, first_term, {D: "z_bf_0"})
+        close_z(1)
         combine(0)
         second_product(1)
+        hand_on(0, GROUP // 2)
         combine(1)
-        hand_on(0, [(nc.vector.tensor_copy, slice(0, GROUP))])
-        hand_on(1, [(nc.vector.tensor_copy, slice(0, 192)), (nc.scalar.copy, slice(192, GROUP))])
+        hand_on(1, GROUP // 4)
 
-        for q in range(4):
+        for q in range(QUADRANTS):
             queue = nc.sync if q % 2 == 0 else nc.scalar
             queue.dma_start(
                 out=out_2[0, 4 * q : 4 * q + 4, :].bitcast(I32), in_=out_scales[32 * q : 32 * q + 4, :].bitcast(I32)

@@ -22,12 +22,21 @@ P = 128
 PACK = 4
 K_PASS = P * PACK
 PASSES = K // K_PASS
+MX_BLOCK = 32
 BANK = 512
 STRIPE = 16
-QUADRANTS = 4
+QUADRANT = 32
+SCALE_ROWS = 4
 CHUNKS = V // P
 HALF = P // 2
+PAIR = 2
 GROUP = V // 2
+OWN = D
+
+GATE_SCALE = 0.9 / 0.1
+Z_SHARE = 0.6
+SUM_TO_PART = Z_SHARE * 0.1
+Y_SHARE = 0.4
 
 
 def tile_picked_zgcnii_gelu_po_kernel(
@@ -54,27 +63,32 @@ def tile_picked_zgcnii_gelu_po_kernel(
                 nc.sync.dma_start(out=raw[:], in_=rows.rearrange("(p j) c -> p j c", j=PACK))
                 w1_raw[side, g] = raw[:].rearrange("p j (m t) -> p m j t", t=PACK)
 
-        def load_x(g):
-            tile = keep.tile([P, T], I32, name="x_table_%d" % g, align_bytes=64)
+        def load_words(g):
+            tile = keep.tile([P, T], I32, name="word_table_%d" % g, align_bytes=64)
             nc.sync.dma_start(out=tile[:], in_=x_words[g].rearrange("p n r -> p (n r)").bitcast(I32))
             return tile
 
         scale_table = keep.tile([P, T], U8, align_bytes=64)
         nc.vector.memset(scale_table[:].bitcast(I32), 0)
+
+        def load_scales(g):
+            for r in range(SCALE_ROWS):
+                nc.sync.dma_start(
+                    out=scale_table[SCALE_ROWS * g + r : P : QUADRANT, :].bitcast(I32),
+                    in_=x_scales[g, r : K_PASS // MX_BLOCK : SCALE_ROWS, :].bitcast(I32),
+                )
+
+        offs_list = load_list("offs_list", offs)
+        load_scales(0)
         load_w1(0)
-        offs_t = load_list("offs_t", offs)
+        word_table = [load_words(0)]
+        load_scales(1)
         gate_cols = keep.tile([P, D, PACK], F32)
         nc.sync.dma_start(out=gate_cols[:], in_=gate[:, 0, :].rearrange("d (p e) -> p d e", e=PACK))
-        x_table = [load_x(0)]
-        for q in range(QUADRANTS):
-            nc.sync.dma_start(
-                out=scale_table[32 * q : 32 * q + 4 * PASSES, :].bitcast(I32),
-                in_=x_scales[:, 4 * q : 4 * q + 4, :].bitcast(I32),
-            )
-        x_table.append(load_x(1))
+        word_table.append(load_words(1))
         load_w1(1)
-        pos_t = [load_list("pos1_t", pos1), load_list("pos2_t", pos2), load_list("pos3_t", pos3)]
-        cen_t = load_list("cen_t", cen)
+        pos_lists = [load_list("pos1_list", pos1), load_list("pos2_list", pos2), load_list("pos3_list", pos3)]
+        cen_list = load_list("cen_list", cen)
         w2_raw = keep.tile([P, PACK, H], F32)
         nc.sync.dma_start(out=w2_raw[:], in_=w2.rearrange("(p j) c -> p j c", j=PACK))
         turn_raw = keep.tile([P, PACK], F32)
@@ -85,7 +99,7 @@ def tile_picked_zgcnii_gelu_po_kernel(
 
         def quantize(name, values):
             width = values.shape[1] // PACK
-            codes = keep.tile([P, width], U32, name=name + "_codes", align_bytes=64)
+            codes = keep.tile([P, width], U32, tag=name + "_codes", name=name + "_codes", align_bytes=64)
             scales = keep.tile([P, width], U8, name=name + "_scales", align_bytes=64)
             nc.vector.quantize_mx(out=codes[:].bitcast(FP8X4), scales=scales[:], in_=values)
             return codes, scales
@@ -93,88 +107,78 @@ def tile_picked_zgcnii_gelu_po_kernel(
         w1_mx = {}
 
         def quantize_w1_low(side):
-            low = keep.tile([P, PASSES, 2, HALF, PACK], BF16, tag="w1_low_%d" % side, name="low", align_bytes=64)
+            low = keep.tile([P, PASSES, PAIR, HALF, PACK], BF16, tag="w1_low_%d" % side, name="low", align_bytes=64)
             for g in range(PASSES):
                 nc.vector.tensor_copy(
-                    out=low[:, g, :, :, :].rearrange("p t m j -> p m j t"), in_=w1_raw[side, g][:, :, :, 0:2]
+                    out=low[:, g, :, :, :].rearrange("p t m j -> p m j t"), in_=w1_raw[side, g][:, :, :, 0:PAIR]
                 )
             codes, scales = quantize("w1_low_%d" % side, low[:].rearrange("p g t m j -> p (g t m j)"))
             w1_mx[side] = (codes, scales, 0)
 
-        high = keep.tile([P, 2, PASSES, P, PACK], BF16, tag="w1_high", align_bytes=64)
-
-        def round_w1_high(side):
-            for g in range(PASSES):
-                nc.scalar.copy(
-                    out=high[:, :, g, side * HALF : (side + 1) * HALF, :].rearrange("p t m j -> p m j t"),
-                    in_=w1_raw[side, g][:, :, :, 2:4],
-                )
-
         quantize_w1_low(0)
 
-        gates, last_gates = [], {}
+        sum_gates, part_gates = [], {}
         for d in range(D):
             spread = work.tile([P, PACK, P], F32, tag="work", name="spread_%d" % d)
             for e in range(PACK):
                 nc.tensor.transpose(spread[:, e, :], gate_cols[:, d, e : e + 1].to_broadcast([P, P]), ident[:])
             in_order = spread[:].rearrange("m e p -> m p e")
-            gate_d = keep.tile([P, P, PACK], F32, name="gate_%d" % d)
-            nc.scalar.activation(out=gate_d[:], in_=in_order, func=COPY, scale=9.0)
-            gates.append(gate_d[:].rearrange("m p e -> m (p e)"))
+            sum_gate = keep.tile([P, P, PACK], F32, name="sum_gate_%d" % d)
+            nc.scalar.activation(out=sum_gate[:], in_=in_order, func=COPY, scale=GATE_SCALE)
+            sum_gates.append(sum_gate[:].rearrange("m p e -> m (p e)"))
             if d > 0:
-                last_d = keep.tile([P, P, PACK], F32, name="last_gate_%d" % d)
-                nc.scalar.activation(out=last_d[:], in_=in_order, func=COPY, scale=0.54)
-                last_gates[d] = last_d[:].rearrange("m p e -> m (p e)")
-        round_w1_high(0)
+                part_gate = keep.tile([P, P, PACK], F32, name="part_gate_%d" % d)
+                nc.scalar.activation(out=part_gate[:], in_=in_order, func=COPY, scale=GATE_SCALE * SUM_TO_PART)
+                part_gates[d] = part_gate[:].rearrange("m p e -> m (p e)")
 
         picked_scales = keep.tile([P, S], U8, align_bytes=64)
-        nc.vector.tensor_copy(picked_scales[:], scale_table[:].indirect(offs_t[:]))
-        picked = {}
-        whole = keep.tile([P, S], U32, name="picked_0", align_bytes=64)
-        nc.vector.tensor_copy(whole[:], x_table[0][:].bitcast(U32).indirect(offs_t[:]))
+        nc.vector.tensor_copy(picked_scales[:], scale_table[:].indirect(offs_list[:]))
+        picked_words = {}
+        first_pass = keep.tile([P, S], U32, align_bytes=64)
+        nc.vector.tensor_copy(first_pass[:], word_table[0][:].bitcast(U32).indirect(offs_list[:]))
         for half in range(S // BANK):
-            picked[0, half] = whole[:, half * BANK : (half + 1) * BANK]
-            part = keep.tile([P, BANK], U32, name="picked_1_%d" % half, align_bytes=64)
-            entries = offs_t[:, half * BANK // STRIPE : (half + 1) * BANK // STRIPE]
-            nc.vector.tensor_copy(part[:], x_table[1][:].bitcast(U32).indirect(entries))
-            picked[1, half] = part[:]
+            picked_words[0, half] = first_pass[:, half * BANK : (half + 1) * BANK]
+            last_pass = keep.tile([P, BANK], U32, name="last_pass_%d" % half, align_bytes=64)
+            entries = offs_list[:, half * BANK // STRIPE : (half + 1) * BANK // STRIPE]
+            nc.vector.tensor_copy(last_pass[:], word_table[1][:].bitcast(U32).indirect(entries))
+            picked_words[1, half] = last_pass[:]
 
         h = {}
 
-        def hidden(block):
-            codes, scales, first = w1_mx[block]
+        def make_h(block):
+            codes, scales, first_col = w1_mx[block]
             h[block] = keep.tile([P, S], F32, name="h_%d" % block)
             for half in range(S // BANK):
                 cols = slice(half * BANK, (half + 1) * BANK)
                 acc = work.tile([P, BANK], F32, tag="work", name="h_acc_%d_%d" % (block, half))
                 for g in range(PASSES):
-                    w_cols = slice(first + g * P, first + (g + 1) * P)
+                    w_cols = slice(first_col + g * P, first_col + (g + 1) * P)
                     nc.tensor.matmul_mx(
                         out=acc[:],
                         lhsT=codes[:, w_cols].bitcast(FP8X4),
                         lhsT_scale=scales[:, w_cols],
-                        rhs=picked[g, half].bitcast(FP8X4),
-                        rhs_scale=picked_scales[4 * g :, cols],
+                        rhs=picked_words[g, half].bitcast(FP8X4),
+                        rhs_scale=picked_scales[SCALE_ROWS * g :, cols],
                         start=(g == 0),
                         stop=(g == PASSES - 1),
                     )
                 nc.scalar.activation(out=h[block][:, cols], in_=acc[:], func=GELU)
 
-        def term_tile(n, width, behind):
-            if n in behind:
-                return keep.tile([P, width], F32, tag=behind[n], name="term_%d" % n, align_bytes=64)
+        def term_tile(n, width, slots):
+            if n in slots:
+                return keep.tile([P, width], F32, tag=slots[n], name="term_%d" % n, align_bytes=64)
             return ring.tile([P, width], F32, tag="term_%d" % n, name="term_%d" % n)
 
         z_sum = [sums.tile([P, BANK], F32, tag="z_sum_%d" % c, name="z_sum_%d" % c) for c in range(CHUNKS)]
 
-        def mix(block, behind):
+        def mix_by_transposes(block, slots):
             terms = []
             for d in range(D):
-                term = term_tile(d, V, behind)
-                nc.vector.tensor_tensor(term[:], h[block][:].indirect(pos_t[d][:]), gates[d], MULT)
+                term = term_tile(d, V, slots)
+                nc.vector.tensor_tensor(term[:], h[block][:].indirect(pos_lists[d][:]), sum_gates[d], MULT)
                 terms.append(term)
-            own = term_tile(D, V, behind)
-            nc.vector.tensor_tensor(own[:], h[block][:].indirect(cen_t[:]), terms[0][:], ADD)
+            own = term_tile(OWN, V, slots)
+            nc.vector.tensor_tensor(own[:], h[block][:].indirect(cen_list[:]), terms[0][:], ADD)
             summands = terms[1:] + [own]
             for n, summand in enumerate(summands):
                 for c in range(CHUNKS):
@@ -189,23 +193,22 @@ def tile_picked_zgcnii_gelu_po_kernel(
 
         z_part = keep.tile([P, PACK, V], F32)
 
-        def turn_back(t, first, rows):
-            back = work.tile([P, len(rows) * P], F32, tag="work", name="z_back_%d" % t)
-            for n, chunk_rows in enumerate(rows):
-                nc.tensor.transpose(back[:, n * P : (n + 1) * P], chunk_rows, ident[:])
-            nc.scalar.activation(
-                out=z_part[:, t, first * P : (first + len(rows)) * P], in_=back[:], func=COPY, scale=0.06
-            )
-
-        hidden(0)
+        make_h(0)
         quantize_w1_low(1)
-        hidden(1)
-        mix(0, {0: "w1_low_1"})
-        round_w1_high(1)
-        codes, scales = quantize("w1_high", high[:].rearrange("p t g m j -> p (t g m j)"))
-        for block in (2, 3):
-            w1_mx[block] = (codes, scales, (block - 2) * PASSES * P)
-            hidden(block)
+        make_h(1)
+        mix_by_transposes(0, {0: "w1_low_1"})
+
+        high = keep.tile([P, PAIR, PASSES, P, PACK], BF16, tag="w1_low_0_codes", align_bytes=64)
+        for side in range(2):
+            for g in range(PASSES):
+                nc.scalar.copy(
+                    out=high[:, :, g, side * HALF : (side + 1) * HALF, :].rearrange("p t m j -> p m j t"),
+                    in_=w1_raw[side, g][:, :, :, PAIR:PACK],
+                )
+        high_codes, high_scales = quantize("w1_high", high[:].rearrange("p t g m j -> p (t g m j)"))
+        for block in range(PAIR, PACK):
+            w1_mx[block] = (high_codes, high_scales, (block - PAIR) * PASSES * P)
+            make_h(block)
 
         w2_bf = keep.tile([P, PACK, P, PACK], BF16, tag="w2_bf", align_bytes=64)
         for m0 in range(0, P, HALF):
@@ -214,63 +217,64 @@ def tile_picked_zgcnii_gelu_po_kernel(
                 in_=w2_raw[:, :, PACK * m0 : PACK * (m0 + HALF)].rearrange("p j (m t) -> p m j t", t=PACK),
             )
         w2_codes, w2_scales = quantize("w2", w2_bf[:].rearrange("p t m j -> p (t m j)"))
-        mix(1, {0: "w1_high"})
-        turn_t = keep.tile([P, PACK], F32)
-        nc.scalar.activation(out=turn_t[:], in_=turn_raw[:], func=COPY, scale=0.4)
+        mix_by_transposes(1, {2: "w1_low_0_codes"})
+        turn_share = keep.tile([P, PACK], F32)
+        nc.scalar.activation(out=turn_share[:], in_=turn_raw[:], func=COPY, scale=Y_SHARE)
 
         low_rows = []
         for c in range(CHUNKS):
-            rows = keep.tile([P, 2, 2, HALF], F32, tag="low_rows_%d" % c, name="low_rows", align_bytes=64)
-            nc.scalar.copy(out=rows[:], in_=z_sum[c][:, 0 : 2 * P].rearrange("v (s t m) -> v t s m", s=2, t=2))
+            rows = keep.tile([P, PAIR, 2, HALF], F32, name="low_rows_%d" % c, align_bytes=64)
+            nc.scalar.copy(out=rows[:], in_=z_sum[c][:, 0 : 2 * P].rearrange("v (s t m) -> v t s m", s=2, t=PAIR))
             low_rows.append(rows)
-        for t in range(2):
-            turn_back(t, 0, [rows[:, t, :, :].rearrange("v s m -> v (s m)") for rows in low_rows])
+        for t in range(PAIR):
+            back = work.tile([P, V], F32, tag="work", name="z_back_%d" % t)
+            for c in range(CHUNKS):
+                plane_rows = low_rows[c][:, t, :, :].rearrange("v s m -> v (s m)")
+                nc.tensor.transpose(back[:, c * P : (c + 1) * P], plane_rows, ident[:])
+            nc.scalar.activation(out=z_part[:, t, :], in_=back[:], func=COPY, scale=SUM_TO_PART)
 
-        mix(2, {2: "w2_bf", D: "low_rows_0"})
-        for first in range(0, CHUNKS, 2):
-            third_rows = []
-            for c in (first, first + 1):
-                rows = keep.tile([P, P], F32, name="third_rows_%d" % c)
-                nc.scalar.copy(out=rows[:], in_=z_sum[c][:, 2 * P : 3 * P])
-                third_rows.append(rows[:])
-            turn_back(2, first, third_rows)
+        def entries_of(index_list, cols):
+            return index_list[:, cols.start // STRIPE : cols.stop // STRIPE]
+
+        def neighbour(t, d, cols, slots):
+            term = term_tile(d, cols.stop - cols.start, slots)
+            weights = (sum_gates[0] if d == 0 else part_gates[d])[:, cols]
+            nc.vector.tensor_tensor(term[:], h[t][:].indirect(entries_of(pos_lists[d], cols)), weights, MULT)
+            return term
+
+        def other_neighbours(t, cols, second, slots):
+            third = neighbour(t, 2, cols, slots)
+            first = neighbour(t, 0, cols, slots)
+            later = ring.tile([P, cols.stop - cols.start], F32, tag="later", name="later")
+            nc.vector.tensor_tensor(later[:], second[:], third[:], ADD)
+            return first, later
+
+        def own_features(t, cols, first, slots):
+            own = term_tile(OWN, cols.stop - cols.start, slots)
+            nc.vector.tensor_tensor(own[:], h[t][:].indirect(entries_of(cen_list, cols)), first[:], ADD)
+            return own
+
+        def close_plane(t, cols, own, later):
+            nc.vector.scalar_tensor_tensor(
+                out=z_part[:, t, cols], in0=own[:], scalar=SUM_TO_PART, in1=later[:], op0=MULT, op1=ADD
+            )
 
         out_codes = keep.tile([P, V], U32, align_bytes=64)
         out_scales = keep.tile([P, V], U8, align_bytes=64)
-        pair, own, z_bf, y, result = {}, {}, {}, {}, {}
+        z_bf, y, result = {}, {}, {}
 
         def cols_of(group):
             return slice(group * GROUP, (group + 1) * GROUP)
 
-        def entries_of(group):
-            return slice(group * GROUP // STRIPE, (group + 1) * GROUP // STRIPE)
-
         def interleave(copy, out, in_):
             copy(out=out.rearrange("p (v i) t -> p v t i", i=PACK), in_=in_.rearrange("p t (v i) -> p v t i", i=PACK))
 
-        def last_neighbours(group):
-            terms = {}
-            for d in (1, 2, 0):
-                terms[d] = term_tile(d, GROUP, {})
-                weights = (gates[0] if d == 0 else last_gates[d])[:, cols_of(group)]
-                nc.vector.tensor_tensor(terms[d][:], h[3][:].indirect(pos_t[d][:, entries_of(group)]), weights, MULT)
-            pair[group] = keep.tile([P, GROUP], F32, name="pair_%d" % group)
-            nc.vector.tensor_tensor(pair[group][:], terms[1][:], terms[2][:], ADD)
-            return terms[0]
+        def part_to_z(out, in_):
+            nc.scalar.activation(out=out, in_=in_, func=COPY, scale=1.0 / Z_SHARE)
 
-        def last_own(group, first_term, behind):
-            own[group] = term_tile(D, GROUP, behind)
-            nc.vector.tensor_tensor(own[group][:], h[3][:].indirect(cen_t[:, entries_of(group)]), first_term[:], ADD)
-
-        def scaled_copy(out, in_):
-            nc.scalar.activation(out=out, in_=in_, func=COPY, scale=1.0 / 0.6)
-
-        def close_z(group):
-            nc.vector.scalar_tensor_tensor(
-                out=z_part[:, 3, cols_of(group)], in0=own[group][:], scalar=0.06, in1=pair[group][:], op0=MULT, op1=ADD
-            )
+        def round_z(group):
             z_bf[group] = keep.tile([P, GROUP, PACK], BF16, tag="z_bf_%d" % group, name="z_bf", align_bytes=64)
-            interleave(scaled_copy, z_bf[group][:], z_part[:, :, cols_of(group)])
+            interleave(part_to_z, z_bf[group][:], z_part[:, :, cols_of(group)])
 
         def second_product(group):
             z_codes, z_scales = quantize("z_%d" % group, z_bf[group][:].rearrange("p v t -> p (v t)"))
@@ -295,7 +299,7 @@ def tile_picked_zgcnii_gelu_po_kernel(
                 nc.vector.scalar_tensor_tensor(
                     out=result[group][:, t, :],
                     in0=y[group, t],
-                    scalar=turn_t[:, t : t + 1],
+                    scalar=turn_share[:, t : t + 1],
                     in1=z_part[:, t, cols_of(group)],
                     op0=MULT,
                     op1=ADD,
@@ -320,20 +324,30 @@ def tile_picked_zgcnii_gelu_po_kernel(
                 out=out_1[0].rearrange("p n r -> p (n r)").bitcast(I32)[:, cols], in_=out_codes[:, cols].bitcast(I32)
             )
 
-        last_own(0, last_neighbours(0), {})
-        close_z(0)
-        first_term = last_neighbours(1)
+        every = slice(0, V)
+        first, later = other_neighbours(2, every, neighbour(2, 1, every, {}), {0: "w2_bf"})
+        own = own_features(2, every, first, {})
+        second = neighbour(3, 1, cols_of(0), {})
+        close_plane(2, every, own, later)
+        first, later = other_neighbours(3, cols_of(0), second, {})
+        own = own_features(3, cols_of(0), first, {})
+        second = neighbour(3, 1, cols_of(1), {})
+        close_plane(3, cols_of(0), own, later)
+        round_z(0)
+        first, later = other_neighbours(3, cols_of(1), second, {})
         second_product(0)
-        last_own(1, first_term, {D: "z_bf_0"})
-        close_z(1)
+        own = own_features(3, cols_of(1), first, {OWN: "z_bf_0"})
+        close_plane(3, cols_of(1), own, later)
+        round_z(1)
         combine(0)
         second_product(1)
         hand_on(0, GROUP // 2)
         combine(1)
         hand_on(1, GROUP // 4)
 
-        for q in range(QUADRANTS):
+        for q in range(P // QUADRANT):
             queue = nc.sync if q % 2 == 0 else nc.scalar
             queue.dma_start(
-                out=out_2[0, 4 * q : 4 * q + 4, :].bitcast(I32), in_=out_scales[32 * q : 32 * q + 4, :].bitcast(I32)
+                out=out_2[0, SCALE_ROWS * q : SCALE_ROWS * (q + 1), :].bitcast(I32),
+                in_=out_scales[QUADRANT * q : QUADRANT * q + SCALE_ROWS, :].bitcast(I32),
             )

@@ -71,20 +71,22 @@ def tile_picked_zgcnii_gelu_po_kernel(
         scale_table = keep.tile([P, T], U8, align_bytes=64)
         nc.vector.memset(scale_table[:].bitcast(I32), 0)
 
-        def load_scales(g):
-            for r in range(SCALE_ROWS):
-                nc.sync.dma_start(
-                    out=scale_table[SCALE_ROWS * g + r : P : QUADRANT, :].bitcast(I32),
-                    in_=x_scales[g, r : K_PASS // MX_BLOCK : SCALE_ROWS, :].bitcast(I32),
-                )
+        def load_scales(rows):
+            for r in rows:
+                for g in range(PASSES):
+                    nc.sync.dma_start(
+                        out=scale_table[SCALE_ROWS * g + r : P : QUADRANT, :].bitcast(I32),
+                        in_=x_scales[g, r : K_PASS // MX_BLOCK : SCALE_ROWS, :].bitcast(I32),
+                    )
 
-        offs_list = load_list("offs_list", offs)
-        load_scales(0)
         load_w1(0)
+        load_scales(range(SCALE_ROWS - 1))
         word_table = [load_words(0)]
-        load_scales(1)
-        gate_cols = keep.tile([P, D, PACK], F32)
-        nc.sync.dma_start(out=gate_cols[:], in_=gate[:, 0, :].rearrange("d (p e) -> p d e", e=PACK))
+        load_scales([SCALE_ROWS - 1])
+        offs_list = load_list("offs_list", offs)
+        gate_rows = keep.tile([P, P], F32)
+        nc.gpsimd.memset(gate_rows[:], 0.0)
+        nc.sync.dma_start(out=gate_rows[0 : D * CHUNKS, :], in_=gate[:, 0, :].rearrange("d (c v) -> d c v", v=P))
         word_table.append(load_words(1))
         load_w1(1)
         pos_lists = [load_list("pos1_list", pos1), load_list("pos2_list", pos2), load_list("pos3_list", pos3)]
@@ -117,19 +119,23 @@ def tile_picked_zgcnii_gelu_po_kernel(
 
         quantize_w1_low(0)
 
+        gate_turned = work.tile([P, P], F32, tag="work", name="gate_turned")
+        nc.tensor.transpose(gate_turned[:], gate_rows[:], ident[:])
+        gate_cols = keep.tile([P, D * CHUNKS], F32)
+        nc.scalar.copy(out=gate_cols[:], in_=gate_turned[:, 0 : D * CHUNKS])
         sum_gates, part_gates = [], {}
         for d in range(D):
-            spread = work.tile([P, PACK, P], F32, tag="work", name="spread_%d" % d)
-            for e in range(PACK):
-                nc.tensor.transpose(spread[:, e, :], gate_cols[:, d, e : e + 1].to_broadcast([P, P]), ident[:])
-            in_order = spread[:].rearrange("m e p -> m p e")
-            sum_gate = keep.tile([P, P, PACK], F32, name="sum_gate_%d" % d)
-            nc.scalar.activation(out=sum_gate[:], in_=in_order, func=COPY, scale=GATE_SCALE)
-            sum_gates.append(sum_gate[:].rearrange("m p e -> m (p e)"))
+            spread = work.tile([P, V], F32, tag="work", name="spread_%d" % d)
+            for c in range(CHUNKS):
+                column = gate_cols[:, CHUNKS * d + c : CHUNKS * d + c + 1]
+                nc.tensor.transpose(spread[:, c * P : (c + 1) * P], column.to_broadcast([P, P]), ident[:])
+            sum_gate = keep.tile([P, V], F32, name="sum_gate_%d" % d)
+            nc.scalar.activation(out=sum_gate[:], in_=spread[:], func=COPY, scale=GATE_SCALE)
+            sum_gates.append(sum_gate[:])
             if d > 0:
-                part_gate = keep.tile([P, P, PACK], F32, name="part_gate_%d" % d)
-                nc.scalar.activation(out=part_gate[:], in_=in_order, func=COPY, scale=GATE_SCALE * SUM_TO_PART)
-                part_gates[d] = part_gate[:].rearrange("m p e -> m (p e)")
+                part_gate = keep.tile([P, V], F32, name="part_gate_%d" % d)
+                nc.scalar.activation(out=part_gate[:], in_=spread[:], func=COPY, scale=GATE_SCALE * SUM_TO_PART)
+                part_gates[d] = part_gate[:]
 
         picked_scales = keep.tile([P, S], U8, align_bytes=64)
         nc.vector.tensor_copy(picked_scales[:], scale_table[:].indirect(offs_list[:]))

@@ -151,19 +151,20 @@ def tile_picked_zgcnii_gelu_po_kernel(
 
         h = {}
 
-        def make_h(block):
+        def make_h(block, pieces=(slice(0, BANK), slice(BANK, S))):
             codes, scales, first_col = w1_mx[block]
             h[block] = keep.tile([P, S], F32, name="h_%d" % block)
-            for half in range(S // BANK):
-                cols = slice(half * BANK, (half + 1) * BANK)
-                acc = work.tile([P, BANK], F32, tag="work", name="h_acc_%d_%d" % (block, half))
+            for cols in pieces:
+                half = cols.start // BANK
+                in_half = slice(cols.start - half * BANK, cols.stop - half * BANK)
+                acc = work.tile([P, cols.stop - cols.start], F32, tag="work", name="h_acc")
                 for g in range(PASSES):
                     w_cols = slice(first_col + g * P, first_col + (g + 1) * P)
                     nc.tensor.matmul_mx(
                         out=acc[:],
                         lhsT=codes[:, w_cols].bitcast(FP8X4),
                         lhsT_scale=scales[:, w_cols],
-                        rhs=picked_words[g, half].bitcast(FP8X4),
+                        rhs=picked_words[g, half][:, in_half].bitcast(FP8X4),
                         rhs_scale=picked_scales[SCALE_ROWS * g :, cols],
                         start=(g == 0),
                         stop=(g == PASSES - 1),
@@ -199,7 +200,7 @@ def tile_picked_zgcnii_gelu_po_kernel(
 
         z_part = keep.tile([P, PACK, V], F32)
 
-        make_h(0)
+        make_h(0, (slice(0, BANK), slice(BANK, BANK + GROUP), slice(BANK + GROUP, S)))
         quantize_w1_low(1)
         make_h(1)
         mix_by_transposes(0, {0: "w1_low_1"})
@@ -268,9 +269,10 @@ def tile_picked_zgcnii_gelu_po_kernel(
         out_codes = keep.tile([P, V], U32, align_bytes=64)
         out_scales = keep.tile([P, V], U8, align_bytes=64)
         z_bf, y, result = {}, {}, {}
+        groups = [slice(0, 2 * P), slice(2 * P, 3 * P), slice(3 * P, V)]
 
-        def cols_of(group):
-            return slice(group * GROUP, (group + 1) * GROUP)
+        def width_of(group):
+            return groups[group].stop - groups[group].start
 
         def interleave(copy, out, in_):
             copy(out=out.rearrange("p (v i) t -> p v t i", i=PACK), in_=in_.rearrange("p t (v i) -> p v t i", i=PACK))
@@ -279,15 +281,21 @@ def tile_picked_zgcnii_gelu_po_kernel(
             nc.scalar.activation(out=out, in_=in_, func=COPY, scale=1.0 / Z_SHARE)
 
         def round_z(group):
-            z_bf[group] = keep.tile([P, GROUP, PACK], BF16, tag="z_bf_%d" % group, name="z_bf", align_bytes=64)
-            interleave(part_to_z, z_bf[group][:], z_part[:, :, cols_of(group)])
+            z_bf[group] = keep.tile(
+                [P, width_of(group), PACK], BF16, tag="z_bf_%d" % group, name="z_bf", align_bytes=64
+            )
+            interleave(part_to_z, z_bf[group][:], z_part[:, :, groups[group]])
 
         def second_product(group):
             z_codes, z_scales = quantize("z_%d" % group, z_bf[group][:].rearrange("p v t -> p (v t)"))
             for t in range(PACK):
                 if t % 2 == 0:
-                    bank = sums.tile([P, 2, GROUP], F32, tag="z_sum_%d" % (2 * group + t // 2), name="y_bank")
-                y[group, t] = bank[:, t % 2, :]
+                    bank_number = 2 * group + t // 2
+                    if bank_number < CHUNKS:
+                        bank = sums.tile([P, BANK], F32, tag="z_sum_%d" % bank_number, name="y_bank")
+                    else:
+                        bank = work.tile([P, BANK], F32, tag="work", name="y_bank")
+                y[group, t] = bank[:, (t % 2) * width_of(group) : (t % 2 + 1) * width_of(group)]
                 nc.tensor.matmul_mx(
                     out=y[group, t],
                     lhsT=w2_codes[:, t * P : (t + 1) * P].bitcast(FP8X4),
@@ -298,29 +306,28 @@ def tile_picked_zgcnii_gelu_po_kernel(
                     stop=True,
                 )
 
-        def combine(group):
-            result[group] = keep.tile([P, PACK, GROUP], F32, name="result_%d" % group)
-            rows = out_0[:, cols_of(group)].rearrange("(p t) v -> p t v", t=PACK)
+        def combine(group, planes_a_store):
+            result[group] = keep.tile([P, PACK, width_of(group)], F32, name="result_%d" % group)
+            rows = out_0[:, groups[group]].rearrange("(p t) v -> p t v", t=PACK)
             for t in range(PACK):
                 nc.vector.scalar_tensor_tensor(
                     out=result[group][:, t, :],
                     in0=y[group, t],
                     scalar=turn_share[:, t : t + 1],
-                    in1=z_part[:, t, cols_of(group)],
+                    in1=z_part[:, t, groups[group]],
                     op0=MULT,
                     op1=ADD,
                 )
-                if t % 2 == 1:
-                    nc.sync.dma_start(out=rows[:, t - 1 : t + 1, :], in_=result[group][:, t - 1 : t + 1, :])
+                if (t + 1) % planes_a_store == 0:
+                    planes = slice(t + 1 - planes_a_store, t + 1)
+                    nc.sync.dma_start(out=rows[:, planes, :], in_=result[group][:, planes, :])
 
-        def hand_on(group, scalar_share):
-            cols = cols_of(group)
-            out_bf = keep.tile([P, GROUP, PACK], BF16, name="out_bf_%d" % group, align_bytes=64)
-            for copy, share in (
-                (nc.scalar.copy, slice(0, scalar_share)),
-                (nc.vector.tensor_copy, slice(scalar_share, GROUP)),
-            ):
-                interleave(copy, out_bf[:, share, :], result[group][:, :, share])
+        def hand_on(name, shares):
+            cols = slice(groups[shares[0][0]].start, groups[shares[-1][0]].stop)
+            out_bf = keep.tile([P, cols.stop - cols.start, PACK], BF16, name=name, align_bytes=64)
+            for group, copy in shares:
+                own_cols = slice(groups[group].start - cols.start, groups[group].stop - cols.start)
+                interleave(copy, out_bf[:, own_cols, :], result[group][:])
             nc.vector.quantize_mx(
                 out=out_codes[:, cols].bitcast(FP8X4),
                 scales=out_scales[:, cols],
@@ -333,23 +340,30 @@ def tile_picked_zgcnii_gelu_po_kernel(
         every = slice(0, V)
         first, later = other_neighbours(2, every, neighbour(2, 1, every, {}), {0: "w2_bf"})
         own = own_features(2, every, first, {})
-        second = neighbour(3, 1, cols_of(0), {})
+        second = neighbour(3, 1, groups[0], {})
         close_plane(2, every, own, later)
-        first, later = other_neighbours(3, cols_of(0), second, {})
-        own = own_features(3, cols_of(0), first, {})
-        second = neighbour(3, 1, cols_of(1), {})
-        close_plane(3, cols_of(0), own, later)
+        first, later = other_neighbours(3, groups[0], second, {})
+        own = own_features(3, groups[0], first, {})
+        second = neighbour(3, 1, groups[1], {})
+        close_plane(3, groups[0], own, later)
         round_z(0)
-        first, later = other_neighbours(3, cols_of(1), second, {})
+        first, later = other_neighbours(3, groups[1], second, {})
+        own = own_features(3, groups[1], first, {})
+        second = neighbour(3, 1, groups[2], {})
         second_product(0)
-        own = own_features(3, cols_of(1), first, {OWN: "z_bf_0"})
-        close_plane(3, cols_of(1), own, later)
+        close_plane(3, groups[1], own, later)
         round_z(1)
-        combine(0)
+        first, later = other_neighbours(3, groups[2], second, {0: "z_bf_0"})
+        own = own_features(3, groups[2], first, {})
         second_product(1)
-        hand_on(0, GROUP // 2)
-        combine(1)
-        hand_on(1, GROUP // 4)
+        close_plane(3, groups[2], own, later)
+        round_z(2)
+        combine(0, PAIR)
+        second_product(2)
+        combine(1, PACK)
+        combine(2, PACK)
+        hand_on("out_bf_first", [(0, nc.scalar.copy)])
+        hand_on("out_bf_last", [(1, nc.scalar.copy), (2, nc.vector.tensor_copy)])
 
         for q in range(P // QUADRANT):
             queue = nc.sync if q % 2 == 0 else nc.scalar

@@ -280,11 +280,14 @@ def tile_picked_zgcnii_gelu_po_kernel(
         def part_to_z(out, in_):
             nc.scalar.activation(out=out, in_=in_, func=COPY, scale=1.0 / Z_SHARE)
 
-        def round_z(group):
+        for group, cols in enumerate(groups):
             z_bf[group] = keep.tile(
                 [P, width_of(group), PACK], BF16, tag="z_bf_%d" % group, name="z_bf", align_bytes=64
             )
-            interleave(part_to_z, z_bf[group][:], z_part[:, :, groups[group]])
+            interleave(part_to_z, z_bf[group][:, :, 0:PAIR], z_part[:, 0:PAIR, cols])
+
+        def round_z(group):
+            interleave(part_to_z, z_bf[group][:, :, PAIR:PACK], z_part[:, PAIR:PACK, groups[group]])
 
         def second_product(group):
             z_codes, z_scales = quantize("z_%d" % group, z_bf[group][:].rearrange("p v t -> p (v t)"))
@@ -344,26 +347,25 @@ def tile_picked_zgcnii_gelu_po_kernel(
         close_plane(2, every, own, later)
         first, later = other_neighbours(3, groups[0], second, {})
         own = own_features(3, groups[0], first, {})
-        second = neighbour(3, 1, groups[1], {})
+        late = slice(groups[1].start, V)
+        second = neighbour(3, 1, late, {})
         close_plane(3, groups[0], own, later)
         round_z(0)
-        first, later = other_neighbours(3, groups[1], second, {})
-        own = own_features(3, groups[1], first, {})
-        second = neighbour(3, 1, groups[2], {})
+        first, later = other_neighbours(3, late, second, {})
         second_product(0)
-        close_plane(3, groups[1], own, later)
+        own = own_features(3, groups[1], first[:, 0:P], {OWN: "z_bf_0"})
+        last_own = own_features(3, groups[2], first[:, P:GROUP], {})
+        close_plane(3, groups[1], own, later[:, 0:P])
         round_z(1)
-        first, later = other_neighbours(3, groups[2], second, {0: "z_bf_0"})
-        own = own_features(3, groups[2], first, {})
+        close_plane(3, groups[2], last_own, later[:, P:GROUP])
         second_product(1)
-        close_plane(3, groups[2], own, later)
         round_z(2)
         combine(0, PAIR)
         second_product(2)
         combine(1, PACK)
         combine(2, PACK)
         hand_on("out_bf_first", [(0, nc.scalar.copy)])
-        hand_on("out_bf_last", [(1, nc.scalar.copy), (2, nc.vector.tensor_copy)])
+        hand_on("out_bf_last", [(1, nc.vector.tensor_copy), (2, nc.vector.tensor_copy)])
 
         for q in range(P // QUADRANT):
             queue = nc.sync if q % 2 == 0 else nc.scalar

@@ -31,6 +31,7 @@ CHUNKS = V // P
 HALF = P // 2
 PAIR = 2
 GROUP = V // 2
+SCALES_AHEAD = 5
 OWN = D
 
 GATE_SCALE = 0.9 / 0.1
@@ -64,26 +65,26 @@ def tile_picked_zgcnii_gelu_po_kernel(
                 w1_raw[side, g] = raw[:].rearrange("p j (m t) -> p m j t", t=PACK)
 
         def load_words(g):
-            tile = keep.tile([P, T], I32, name="word_table_%d" % g, align_bytes=64)
+            tile = keep.tile([P, T], I32, tag="word_table_%d" % g, name="word_table", align_bytes=64)
             nc.sync.dma_start(out=tile[:], in_=x_words[g].rearrange("p n r -> p (n r)").bitcast(I32))
             return tile
 
         scale_table = keep.tile([P, T], U8, align_bytes=64)
         nc.vector.memset(scale_table[:].bitcast(I32), 0)
 
-        def load_scales(rows):
-            for r in rows:
-                for g in range(PASSES):
-                    nc.sync.dma_start(
-                        out=scale_table[SCALE_ROWS * g + r : P : QUADRANT, :].bitcast(I32),
-                        in_=x_scales[g, r : K_PASS // MX_BLOCK : SCALE_ROWS, :].bitcast(I32),
-                    )
+        def load_scales(pieces):
+            for piece in pieces:
+                r, g = divmod(piece, PASSES)
+                nc.sync.dma_start(
+                    out=scale_table[SCALE_ROWS * g + r : P : QUADRANT, :].bitcast(I32),
+                    in_=x_scales[g, r : K_PASS // MX_BLOCK : SCALE_ROWS, :].bitcast(I32),
+                )
 
-        load_w1(0)
-        load_scales(range(SCALE_ROWS - 1))
-        word_table = [load_words(0)]
-        load_scales([SCALE_ROWS - 1])
         offs_list = load_list("offs_list", offs)
+        load_w1(0)
+        load_scales(range(SCALES_AHEAD))
+        word_table = [load_words(0)]
+        load_scales(range(SCALES_AHEAD, PASSES * SCALE_ROWS))
         gate_rows = keep.tile([P, P], F32)
         nc.gpsimd.memset(gate_rows[:], 0.0)
         nc.sync.dma_start(out=gate_rows[0 : D * CHUNKS, :], in_=gate[:, 0, :].rearrange("d (c v) -> d c v", v=P))
@@ -137,11 +138,11 @@ def tile_picked_zgcnii_gelu_po_kernel(
                 nc.scalar.activation(out=part_gate[:], in_=spread[:], func=COPY, scale=GATE_SCALE * SUM_TO_PART)
                 part_gates[d] = part_gate[:]
 
-        picked_scales = keep.tile([P, S], U8, align_bytes=64)
-        nc.vector.tensor_copy(picked_scales[:], scale_table[:].indirect(offs_list[:]))
         picked_words = {}
         first_pass = keep.tile([P, S], U32, align_bytes=64)
         nc.vector.tensor_copy(first_pass[:], word_table[0][:].bitcast(U32).indirect(offs_list[:]))
+        picked_scales = keep.tile([P, S], U8, tag="word_table_0", align_bytes=64)
+        nc.vector.tensor_copy(picked_scales[:], scale_table[:].indirect(offs_list[:]))
         for half in range(S // BANK):
             picked_words[0, half] = first_pass[:, half * BANK : (half + 1) * BANK]
             last_pass = keep.tile([P, BANK], U32, name="last_pass_%d" % half, align_bytes=64)

@@ -31,7 +31,7 @@ CHUNKS = V // P
 HALF = P // 2
 PAIR = 2
 GROUP = V // 2
-SCALES_AHEAD = 5
+SCALES_AHEAD = 6
 OWN = D
 
 GATE_SCALE = 0.9 / 0.1
@@ -57,8 +57,8 @@ def tile_picked_zgcnii_gelu_po_kernel(
 
         w1_raw = {}
 
-        def load_w1(side):
-            for g in range(PASSES):
+        def load_w1(side, passes):
+            for g in passes:
                 raw = keep.tile([P, PACK, H // 2], F32, name="w1_raw_%d_%d" % (side, g))
                 rows = w1[g * K_PASS : (g + 1) * K_PASS, side * H // 2 : (side + 1) * H // 2]
                 nc.sync.dma_start(out=raw[:], in_=rows.rearrange("(p j) c -> p j c", j=PACK))
@@ -69,7 +69,7 @@ def tile_picked_zgcnii_gelu_po_kernel(
             nc.sync.dma_start(out=tile[:], in_=x_words[g].rearrange("p n r -> p (n r)").bitcast(I32))
             return tile
 
-        scale_table = keep.tile([P, T], U8, align_bytes=64)
+        scale_table = keep.tile([P, T], U8, tag="w1_low_0_codes", align_bytes=64)
         nc.vector.memset(scale_table[:].bitcast(I32), 0)
 
         def load_scales(pieces):
@@ -81,15 +81,16 @@ def tile_picked_zgcnii_gelu_po_kernel(
                 )
 
         offs_list = load_list("offs_list", offs)
-        load_w1(0)
+        load_w1(0, [0])
         load_scales(range(SCALES_AHEAD))
         word_table = [load_words(0)]
         load_scales(range(SCALES_AHEAD, PASSES * SCALE_ROWS))
         gate_rows = keep.tile([P, P], F32)
         nc.gpsimd.memset(gate_rows[:], 0.0)
         nc.sync.dma_start(out=gate_rows[0 : D * CHUNKS, :], in_=gate[:, 0, :].rearrange("d (c v) -> d c v", v=P))
+        load_w1(0, [1])
         word_table.append(load_words(1))
-        load_w1(1)
+        load_w1(1, range(PASSES))
         pos_lists = [load_list("pos1_list", pos1), load_list("pos2_list", pos2), load_list("pos3_list", pos3)]
         cen_list = load_list("cen_list", cen)
         w2_raw = keep.tile([P, PACK, H], F32)
@@ -109,16 +110,12 @@ def tile_picked_zgcnii_gelu_po_kernel(
 
         w1_mx = {}
 
-        def quantize_w1_low(side):
+        def quantize_w1_low(side, copy):
             low = keep.tile([P, PASSES, PAIR, HALF, PACK], BF16, tag="w1_low_%d" % side, name="low", align_bytes=64)
             for g in range(PASSES):
-                nc.vector.tensor_copy(
-                    out=low[:, g, :, :, :].rearrange("p t m j -> p m j t"), in_=w1_raw[side, g][:, :, :, 0:PAIR]
-                )
+                copy(out=low[:, g, :, :, :].rearrange("p t m j -> p m j t"), in_=w1_raw[side, g][:, :, :, 0:PAIR])
             codes, scales = quantize("w1_low_%d" % side, low[:].rearrange("p g t m j -> p (g t m j)"))
             w1_mx[side] = (codes, scales, 0)
-
-        quantize_w1_low(0)
 
         gate_turned = work.tile([P, P], F32, tag="work", name="gate_turned")
         nc.tensor.transpose(gate_turned[:], gate_rows[:], ident[:])
@@ -143,6 +140,7 @@ def tile_picked_zgcnii_gelu_po_kernel(
         nc.vector.tensor_copy(first_pass[:], word_table[0][:].bitcast(U32).indirect(offs_list[:]))
         picked_scales = keep.tile([P, S], U8, tag="word_table_0", align_bytes=64)
         nc.vector.tensor_copy(picked_scales[:], scale_table[:].indirect(offs_list[:]))
+        quantize_w1_low(0, nc.scalar.copy)
         for half in range(S // BANK):
             picked_words[0, half] = first_pass[:, half * BANK : (half + 1) * BANK]
             last_pass = keep.tile([P, BANK], U32, name="last_pass_%d" % half, align_bytes=64)
@@ -202,7 +200,7 @@ def tile_picked_zgcnii_gelu_po_kernel(
         z_part = keep.tile([P, PACK, V], F32)
 
         make_h(0, (slice(0, BANK), slice(BANK, BANK + GROUP), slice(BANK + GROUP, S)))
-        quantize_w1_low(1)
+        quantize_w1_low(1, nc.vector.tensor_copy)
         make_h(1)
         mix_by_transposes(0, {0: "w1_low_1"})
 

@@ -57,9 +57,10 @@ def tile_picked_zgcnii_gelu_po_kernel(
 
         w1_raw = {}
 
-        def load_w1(side, passes):
+        def load_w1(side, passes, slots=None):
             for g in passes:
-                raw = keep.tile([P, PACK, H // 2], F32, name="w1_raw_%d_%d" % (side, g))
+                name = "w1_raw_%d_%d" % (side, g)
+                raw = keep.tile([P, PACK, H // 2], F32, tag=slots[g] if slots else name, name=name, align_bytes=64)
                 rows = w1[g * K_PASS : (g + 1) * K_PASS, side * H // 2 : (side + 1) * H // 2]
                 nc.sync.dma_start(out=raw[:], in_=rows.rearrange("(p j) c -> p j c", j=PACK))
                 w1_raw[side, g] = raw[:].rearrange("p j (m t) -> p m j t", t=PACK)
@@ -69,27 +70,21 @@ def tile_picked_zgcnii_gelu_po_kernel(
             nc.sync.dma_start(out=tile[:], in_=x_words[g].rearrange("p n r -> p (n r)").bitcast(I32))
             return tile
 
-        scale_table = keep.tile([P, T], U8, tag="w1_low_0_codes", align_bytes=64)
-        nc.vector.memset(scale_table[:].bitcast(I32), 0)
-
-        def load_scales(pieces):
-            for piece in pieces:
-                r, g = divmod(piece, PASSES)
-                nc.sync.dma_start(
-                    out=scale_table[SCALE_ROWS * g + r : P : QUADRANT, :].bitcast(I32),
-                    in_=x_scales[g, r : K_PASS // MX_BLOCK : SCALE_ROWS, :].bitcast(I32),
-                )
+        scale_table = keep.tile([P, T], U8, tag="scale_table", align_bytes=64)
+        nc.vector.memset(scale_table[QUADRANT : 2 * QUADRANT, :].bitcast(I32), 0)
+        nc.vector.memset(scale_table[2 * QUADRANT : P, :].bitcast(I32), 0)
+        picked_scales = keep.tile([P, PASSES, S], U8, align_bytes=64)
+        nc.vector.memset(picked_scales[:].rearrange("p g s -> p (g s)").bitcast(I32), 0)
 
         offs_list = load_list("offs_list", offs)
-        load_w1(0, [0])
-        load_scales(range(SCALES_AHEAD))
+        for g in range(PASSES):
+            nc.sync.dma_start(out=scale_table[g:QUADRANT:PASSES, :].bitcast(I32), in_=x_scales[g].bitcast(I32))
         word_table = [load_words(0)]
-        load_scales(range(SCALES_AHEAD, PASSES * SCALE_ROWS))
         gate_rows = keep.tile([P, P], F32)
         nc.gpsimd.memset(gate_rows[:], 0.0)
         nc.sync.dma_start(out=gate_rows[0 : D * CHUNKS, :], in_=gate[:, 0, :].rearrange("d (c v) -> d c v", v=P))
-        load_w1(0, [1])
         word_table.append(load_words(1))
+        load_w1(0, range(PASSES))
         load_w1(1, range(PASSES))
         pos_lists = [load_list("pos1_list", pos1), load_list("pos2_list", pos2), load_list("pos3_list", pos3)]
         cen_list = load_list("cen_list", cen)
@@ -100,6 +95,8 @@ def tile_picked_zgcnii_gelu_po_kernel(
 
         ident = keep.tile([P, P], F32)
         make_identity(nc, ident[:])
+        table_warm_up = keep.tile([P, 1], F32)
+        nc.scalar.activation(out=table_warm_up[:], in_=ident[:, 0:1], func=GELU)
 
         def quantize(name, values):
             width = values.shape[1] // PACK
@@ -109,13 +106,6 @@ def tile_picked_zgcnii_gelu_po_kernel(
             return codes, scales
 
         w1_mx = {}
-
-        def quantize_w1_low(side, copy):
-            low = keep.tile([P, PASSES, PAIR, HALF, PACK], BF16, tag="w1_low_%d" % side, name="low", align_bytes=64)
-            for g in range(PASSES):
-                copy(out=low[:, g, :, :, :].rearrange("p t m j -> p m j t"), in_=w1_raw[side, g][:, :, :, 0:PAIR])
-            codes, scales = quantize("w1_low_%d" % side, low[:].rearrange("p g t m j -> p (g t m j)"))
-            w1_mx[side] = (codes, scales, 0)
 
         gate_turned = work.tile([P, P], F32, tag="work", name="gate_turned")
         nc.tensor.transpose(gate_turned[:], gate_rows[:], ident[:])
@@ -136,35 +126,56 @@ def tile_picked_zgcnii_gelu_po_kernel(
                 part_gates[d] = part_gate[:]
 
         picked_words = {}
+        loose_scales = keep.tile([P, S], U8, tag="loose_scales", align_bytes=64)
+        nc.vector.tensor_copy(loose_scales[:], scale_table[:].indirect(offs_list[:]))
+        for q in range(P // QUADRANT):
+            nc.scalar.dma_start(
+                out=picked_scales[QUADRANT * q : QUADRANT * q + SCALE_ROWS, :, :].rearrange("p g s -> p (g s)").bitcast(I32),
+                in_=loose_scales[PASSES * SCALE_ROWS * q : PASSES * SCALE_ROWS * (q + 1), :].bitcast(I32),
+            )
         first_pass = keep.tile([P, S], U32, align_bytes=64)
         nc.vector.tensor_copy(first_pass[:], word_table[0][:].bitcast(U32).indirect(offs_list[:]))
-        picked_scales = keep.tile([P, S], U8, tag="word_table_0", align_bytes=64)
-        nc.vector.tensor_copy(picked_scales[:], scale_table[:].indirect(offs_list[:]))
-        quantize_w1_low(0, nc.scalar.copy)
-        for half in range(S // BANK):
+
+        def gather_last_pass(half, slot):
             picked_words[0, half] = first_pass[:, half * BANK : (half + 1) * BANK]
-            last_pass = keep.tile([P, BANK], U32, name="last_pass_%d" % half, align_bytes=64)
+            last_pass = keep.tile([P, BANK], U32, tag=slot, name="last_pass", align_bytes=64)
             entries = offs_list[:, half * BANK // STRIPE : (half + 1) * BANK // STRIPE]
             nc.vector.tensor_copy(last_pass[:], word_table[1][:].bitcast(U32).indirect(entries))
             picked_words[1, half] = last_pass[:]
 
+        gather_last_pass(0, "last_pass")
+        later_w1 = keep.tile([P, (PACK - 1) * PASSES, P, PACK], BF16, tag="later_w1", align_bytes=64)
+        later_flat = later_w1[:].rearrange("p r m j -> p (r m j)")
+        row_of = {(block, g): (PACK - 1) * g + n for g in range(PASSES) for n, block in enumerate((2, 3, 1))}
+        borrowed = row_of[1, 0] * K_PASS - 3 * K_PASS // 4
+        first_block = []
+        first_low = keep.tile([P, K_PASS], BF16, tag="first_low", align_bytes=64)
+        for g, low in enumerate((first_low[:], later_flat[:, borrowed : borrowed + K_PASS])):
+            rounded = low.rearrange("p (t m j) -> p m j t", t=PAIR, j=PACK)
+            copies = (nc.scalar.copy, nc.vector.tensor_copy) if g == 0 else (nc.scalar.copy,)
+            for n, copy in enumerate(copies):
+                share = slice(n * HALF // len(copies), (n + 1) * HALF // len(copies))
+                copy(out=rounded[:, share, :, :], in_=w1_raw[0, g][:, share, :, 0:PAIR])
+            first_block.append(quantize("w1_first_%d" % g, low))
+            if g == 0:
+                gather_last_pass(1, "first_low")
+
         h = {}
 
         def make_h(block, pieces=(slice(0, BANK), slice(BANK, S))):
-            codes, scales, first_col = w1_mx[block]
             h[block] = keep.tile([P, S], F32, name="h_%d" % block)
             for cols in pieces:
                 half = cols.start // BANK
                 in_half = slice(cols.start - half * BANK, cols.stop - half * BANK)
                 acc = work.tile([P, cols.stop - cols.start], F32, tag="work", name="h_acc")
                 for g in range(PASSES):
-                    w_cols = slice(first_col + g * P, first_col + (g + 1) * P)
+                    codes, scales = w1_mx[block, g]
                     nc.tensor.matmul_mx(
                         out=acc[:],
-                        lhsT=codes[:, w_cols].bitcast(FP8X4),
-                        lhsT_scale=scales[:, w_cols],
+                        lhsT=codes.bitcast(FP8X4),
+                        lhsT_scale=scales,
                         rhs=picked_words[g, half][:, in_half].bitcast(FP8X4),
-                        rhs_scale=picked_scales[SCALE_ROWS * g :, cols],
+                        rhs_scale=picked_scales[:, g, cols],
                         start=(g == 0),
                         stop=(g == PASSES - 1),
                     )
@@ -199,31 +210,56 @@ def tile_picked_zgcnii_gelu_po_kernel(
 
         z_part = keep.tile([P, PACK, V], F32)
 
-        make_h(0, (slice(0, BANK), slice(BANK, BANK + GROUP), slice(BANK + GROUP, S)))
-        quantize_w1_low(1, nc.vector.tensor_copy)
-        make_h(1)
-        mix_by_transposes(0, {0: "w1_low_1"})
+        h[0] = keep.tile([P, S], F32, name="h_0")
+        pieces = [slice(c, c + GROUP) for c in range(0, S, GROUP)]
+        accs = [work.tile([P, cols.stop - cols.start], F32, tag="work", name="first_acc") for cols in pieces]
+        for g in range(PASSES):
+            codes, scales = first_block[g]
+            for cols, acc in zip(pieces, accs):
+                nc.tensor.matmul_mx(
+                    out=acc[:],
+                    lhsT=codes[:].bitcast(FP8X4),
+                    lhsT_scale=scales[:],
+                    rhs=picked_words[g, cols.start // BANK][:, cols.start % BANK : cols.start % BANK + GROUP].bitcast(FP8X4),
+                    rhs_scale=picked_scales[:, g, cols],
+                    start=(g == 0),
+                    stop=(g == PASSES - 1),
+                )
+                if g == PASSES - 1:
+                    nc.scalar.activation(out=h[0][:, cols], in_=acc[:], func=GELU)
 
-        high = keep.tile([P, PAIR, PASSES, P, PACK], BF16, tag="w1_low_0_codes", align_bytes=64)
-        for side in range(2):
-            for g in range(PASSES):
-                nc.scalar.copy(
-                    out=high[:, :, g, side * HALF : (side + 1) * HALF, :].rearrange("p t m j -> p m j t"),
+        for g in range(PASSES):
+            (nc.scalar.copy if g else nc.vector.tensor_copy)(
+                out=later_w1[:, row_of[1, g], :, :].rearrange("p (t m) j -> p m j t", t=PAIR),
+                in_=w1_raw[1, g][:, :, :, 0:PAIR],
+            )
+            for side in range(2):
+                copy = nc.scalar.copy if g == PASSES - 1 else nc.vector.tensor_copy
+                copy(
+                    out=later_w1[:, row_of[2, g] : row_of[3, g] + 1, side * HALF : (side + 1) * HALF, :].rearrange(
+                        "p t m j -> p m j t"
+                    ),
                     in_=w1_raw[side, g][:, :, :, PAIR:PACK],
                 )
-        high_codes, high_scales = quantize("w1_high", high[:].rearrange("p t g m j -> p (t g m j)"))
+            low_row, high_row = row_of[1, g] * K_PASS, row_of[2, g] * K_PASS
+            codes, scales = quantize("w1_low_%d" % g, later_flat[:, low_row : low_row + K_PASS])
+            w1_mx[1, g] = (codes[:], scales[:])
+            codes, scales = quantize("w1_high_%d" % g, later_flat[:, high_row : high_row + PAIR * K_PASS])
+            for t in range(PAIR):
+                w1_mx[PAIR + t, g] = (codes[:, t * P : (t + 1) * P], scales[:, t * P : (t + 1) * P])
+        make_h(1)
+        mix_by_transposes(0, {})
         for block in range(PAIR, PACK):
-            w1_mx[block] = (high_codes, high_scales, (block - PAIR) * PASSES * P)
             make_h(block)
 
-        w2_bf = keep.tile([P, PACK, P, PACK], BF16, tag="w2_bf", align_bytes=64)
+        w2_bf = keep.tile([P, PACK, P, PACK], BF16, tag="later_w1", align_bytes=64)
         for m0 in range(0, P, HALF):
             nc.scalar.copy(
                 out=w2_bf[:, :, m0 : m0 + HALF, :].rearrange("p t m j -> p m j t"),
                 in_=w2_raw[:, :, PACK * m0 : PACK * (m0 + HALF)].rearrange("p j (m t) -> p m j t", t=PACK),
             )
         w2_codes, w2_scales = quantize("w2", w2_bf[:].rearrange("p t m j -> p (t m j)"))
-        mix_by_transposes(1, {2: "w1_low_0_codes"})
+        mix_by_transposes(1, {})
         turn_share = keep.tile([P, PACK], F32)
         nc.scalar.activation(out=turn_share[:], in_=turn_raw[:], func=COPY, scale=Y_SHARE)
 
@@ -251,7 +287,7 @@ def tile_picked_zgcnii_gelu_po_kernel(
         def other_neighbours(t, cols, second, slots):
             third = neighbour(t, 2, cols, slots)
             first = neighbour(t, 0, cols, slots)
-            later = ring.tile([P, cols.stop - cols.start], F32, tag="later", name="later")
+            later = keep.tile([P, cols.stop - cols.start], F32, tag=slots["later"], name="later", align_bytes=64)
             nc.vector.tensor_tensor(later[:], second[:], third[:], ADD)
             return first, later
 
@@ -262,7 +298,7 @@ def tile_picked_zgcnii_gelu_po_kernel(
 
         def close_plane(t, cols, own, later):
             nc.vector.scalar_tensor_tensor(
-                out=z_part[:, t, cols], in0=own[:], scalar=SUM_TO_PART, in1=later[:], op0=MULT, op1=ADD
+                out=z_part[:, t, cols], in0=own, scalar=SUM_TO_PART, in1=later, op0=MULT, op1=ADD
             )
 
         out_codes = keep.tile([P, V], U32, align_bytes=64)
@@ -340,31 +376,37 @@ def tile_picked_zgcnii_gelu_po_kernel(
             )
 
         every = slice(0, V)
-        first, later = other_neighbours(2, every, neighbour(2, 1, every, {}), {0: "w2_bf"})
-        own = own_features(2, every, first, {})
-        second = neighbour(3, 1, groups[0], {})
-        close_plane(2, every, own, later)
-        first, later = other_neighbours(3, groups[0], second, {})
-        own = own_features(3, groups[0], first, {})
+        second = neighbour(2, 1, every, {1: "second"})
+        first, later = other_neighbours(2, every, second, {2: "third", 0: "first", "later": "later"})
+        own = own_features(2, every, first, {OWN: "own"})
+        second = neighbour(3, 1, groups[0], {1: "second"})
+        close_plane(2, every, own[:], later[:])
+        first, later = other_neighbours(3, groups[0], second, {2: "third", 0: "first", "later": "later_3"})
+        own = own_features(3, groups[0], first, {OWN: "own"})
         late = slice(groups[1].start, V)
-        second = neighbour(3, 1, late, {})
-        close_plane(3, groups[0], own, later)
+        second = neighbour(3, 1, late, {1: "second"})
+        close_plane(3, groups[0], own[:], later[:])
         round_z(0)
-        first, later = other_neighbours(3, late, second, {})
+        first = neighbour(3, 0, late, {0: "first"})
+        third = neighbour(3, 2, late, {2: "own"})
         second_product(0)
-        own = own_features(3, groups[1], first[:, 0:P], {OWN: "z_bf_0"})
-        last_own = own_features(3, groups[2], first[:, P:GROUP], {})
+        closing = keep.tile([P, 2 * GROUP], F32, tag="z_bf_0", align_bytes=64)
+        later, own, last_own = closing[:, 0:GROUP], closing[:, GROUP : GROUP + P], closing[:, GROUP + P :]
+        nc.vector.tensor_tensor(later, second[:], third[:], ADD)
+        for n, features in enumerate((own, last_own)):
+            entries = entries_of(cen_list, groups[1 + n])
+            nc.vector.tensor_tensor(features, h[3][:].indirect(entries), first[:, n * P : (n + 1) * P], ADD)
         close_plane(3, groups[1], own, later[:, 0:P])
         round_z(1)
         close_plane(3, groups[2], last_own, later[:, P:GROUP])
         second_product(1)
         round_z(2)
-        combine(0, PAIR)
         second_product(2)
+        combine(0, PAIR)
         combine(1, PACK)
         combine(2, PACK)
         hand_on("out_bf_first", [(0, nc.scalar.copy)])
-        hand_on("out_bf_last", [(1, nc.vector.tensor_copy), (2, nc.vector.tensor_copy)])
+        hand_on("out_bf_last", [(1, nc.scalar.copy), (2, nc.vector.tensor_copy)])
 
         for q in range(P // QUADRANT):
             queue = nc.sync if q % 2 == 0 else nc.scalar

@@ -275,6 +275,18 @@ def tile_picked_zgcnii_gelu_po_kernel(
                 nc.tensor.transpose(back[:, c * P : (c + 1) * P], plane_rows, ident[:])
             nc.scalar.activation(out=z_part[:, t, :], in_=back[:], func=COPY, scale=SUM_TO_PART)
 
+        mix_by_transposes(2, {})
+        for half in range(2):
+            back = work.tile([P, GROUP], F32, tag="work", name="z_back_2")
+            for n in range(CHUNKS // 2):
+                c = half * CHUNKS // 2 + n
+                rows = keep.tile([P, P], F32, name="plane_rows_%d" % c, align_bytes=64)
+                nc.scalar.copy(out=rows[:], in_=z_sum[c][:, 2 * P : 3 * P])
+                nc.tensor.transpose(back[:, n * P : (n + 1) * P], rows[:], ident[:])
+            nc.scalar.activation(
+                out=z_part[:, 2, half * GROUP : (half + 1) * GROUP], in_=back[:], func=COPY, scale=SUM_TO_PART
+            )
+
         def entries_of(index_list, cols):
             return index_list[:, cols.start // STRIPE : cols.stop // STRIPE]
 
@@ -375,12 +387,7 @@ def tile_picked_zgcnii_gelu_po_kernel(
                 out=out_1[0].rearrange("p n r -> p (n r)").bitcast(I32)[:, cols], in_=out_codes[:, cols].bitcast(I32)
             )
 
-        every = slice(0, V)
-        second = neighbour(2, 1, every, {1: "second"})
-        first, later = other_neighbours(2, every, second, {2: "third", 0: "first", "later": "later"})
-        own = own_features(2, every, first, {OWN: "own"})
         second = neighbour(3, 1, groups[0], {1: "second"})
-        close_plane(2, every, own[:], later[:])
         first, later = other_neighbours(3, groups[0], second, {2: "third", 0: "first", "later": "later_3"})
         own = own_features(3, groups[0], first, {OWN: "own"})
         late = slice(groups[1].start, V)

@@ -188,19 +188,24 @@ def tile_picked_zgcnii_gelu_po_kernel(
 
         z_sum = [sums.tile([P, BANK], F32, tag="z_sum_%d" % c, name="z_sum_%d" % c) for c in range(CHUNKS)]
 
-        def mix_by_transposes(block, slots):
+        def entries_of(index_list, cols):
+            return index_list[:, cols.start // STRIPE : cols.stop // STRIPE]
+
+        def mix_by_transposes(block, cols=slice(0, V)):
+            width = cols.stop - cols.start
             terms = []
             for d in range(D):
-                term = term_tile(d, V, slots)
-                nc.vector.tensor_tensor(term[:], h[block][:].indirect(pos_lists[d][:]), sum_gates[d], MULT)
+                term = term_tile(d, width, {})
+                looked_up = h[block][:].indirect(entries_of(pos_lists[d], cols))
+                nc.vector.tensor_tensor(term[:], looked_up, sum_gates[d][:, cols], MULT)
                 terms.append(term)
-            own = term_tile(OWN, V, slots)
-            nc.vector.tensor_tensor(own[:], h[block][:].indirect(cen_list[:]), terms[0][:], ADD)
+            own = term_tile(OWN, width, {})
+            nc.vector.tensor_tensor(own[:], h[block][:].indirect(entries_of(cen_list, cols)), terms[0][:], ADD)
             summands = terms[1:] + [own]
             for n, summand in enumerate(summands):
-                for c in range(CHUNKS):
+                for c in range(width // P):
                     nc.tensor.matmul(
-                        out=z_sum[c][:, block * P : (block + 1) * P],
+                        out=z_sum[cols.start // P + c][:, block * P : (block + 1) * P],
                         lhsT=summand[:, c * P : (c + 1) * P],
                         rhs=ident[:],
                         start=(n == 0),
@@ -248,7 +253,7 @@ def tile_picked_zgcnii_gelu_po_kernel(
             for t in range(PAIR):
                 w1_mx[PAIR + t, g] = (codes[:, t * P : (t + 1) * P], scales[:, t * P : (t + 1) * P])
         make_h(1)
-        mix_by_transposes(0, {})
+        mix_by_transposes(0)
         for block in range(PAIR, PACK):
             make_h(block)
 
@@ -259,7 +264,7 @@ def tile_picked_zgcnii_gelu_po_kernel(
                 in_=w2_raw[:, :, PACK * m0 : PACK * (m0 + HALF)].rearrange("p j (m t) -> p m j t", t=PACK),
             )
         w2_codes, w2_scales = quantize("w2", w2_bf[:].rearrange("p t m j -> p (t m j)"))
-        mix_by_transposes(1, {})
+        mix_by_transposes(1)
         turn_share = keep.tile([P, PACK], F32)
         nc.scalar.activation(out=turn_share[:], in_=turn_raw[:], func=COPY, scale=Y_SHARE)
 
@@ -275,38 +280,25 @@ def tile_picked_zgcnii_gelu_po_kernel(
                 nc.tensor.transpose(back[:, c * P : (c + 1) * P], plane_rows, ident[:])
             nc.scalar.activation(out=z_part[:, t, :], in_=back[:], func=COPY, scale=SUM_TO_PART)
 
-        mix_by_transposes(2, {})
-        for half in range(2):
-            back = work.tile([P, GROUP], F32, tag="work", name="z_back_2")
-            for n in range(CHUNKS // 2):
-                c = half * CHUNKS // 2 + n
-                rows = keep.tile([P, P], F32, name="plane_rows_%d" % c, align_bytes=64)
-                nc.scalar.copy(out=rows[:], in_=z_sum[c][:, 2 * P : 3 * P])
+        def turn_back(plane, cols):
+            back = work.tile([P, GROUP], F32, tag="work", name="z_back_high")
+            for n in range(GROUP // P):
+                c = cols.start // P + n
+                rows = keep.tile([P, P], F32, name="plane_rows_%d_%d" % (plane, c), align_bytes=64)
+                nc.scalar.copy(out=rows[:], in_=z_sum[c][:, plane * P : (plane + 1) * P])
                 nc.tensor.transpose(back[:, n * P : (n + 1) * P], rows[:], ident[:])
-            nc.scalar.activation(
-                out=z_part[:, 2, half * GROUP : (half + 1) * GROUP], in_=back[:], func=COPY, scale=SUM_TO_PART
-            )
+            nc.scalar.activation(out=z_part[:, plane, cols], in_=back[:], func=COPY, scale=SUM_TO_PART)
 
-        def entries_of(index_list, cols):
-            return index_list[:, cols.start // STRIPE : cols.stop // STRIPE]
+        early, late = slice(0, GROUP), slice(GROUP, V)
+        for plane, cols in ((2, early), (3, early), (2, late)):
+            mix_by_transposes(plane, cols)
+            turn_back(plane, cols)
 
         def neighbour(t, d, cols, slots):
             term = term_tile(d, cols.stop - cols.start, slots)
             weights = (sum_gates[0] if d == 0 else part_gates[d])[:, cols]
             nc.vector.tensor_tensor(term[:], h[t][:].indirect(entries_of(pos_lists[d], cols)), weights, MULT)
             return term
-
-        def other_neighbours(t, cols, second, slots):
-            third = neighbour(t, 2, cols, slots)
-            first = neighbour(t, 0, cols, slots)
-            later = keep.tile([P, cols.stop - cols.start], F32, tag=slots["later"], name="later", align_bytes=64)
-            nc.vector.tensor_tensor(later[:], second[:], third[:], ADD)
-            return first, later
-
-        def own_features(t, cols, first, slots):
-            own = term_tile(OWN, cols.stop - cols.start, slots)
-            nc.vector.tensor_tensor(own[:], h[t][:].indirect(entries_of(cen_list, cols)), first[:], ADD)
-            return own
 
         def close_plane(t, cols, own, later):
             nc.vector.scalar_tensor_tensor(
@@ -387,15 +379,10 @@ def tile_picked_zgcnii_gelu_po_kernel(
                 out=out_1[0].rearrange("p n r -> p (n r)").bitcast(I32)[:, cols], in_=out_codes[:, cols].bitcast(I32)
             )
 
-        second = neighbour(3, 1, groups[0], {1: "second"})
-        first, later = other_neighbours(3, groups[0], second, {2: "third", 0: "first", "later": "later_3"})
-        own = own_features(3, groups[0], first, {OWN: "own"})
-        late = slice(groups[1].start, V)
-        second = neighbour(3, 1, late, {1: "second"})
-        close_plane(3, groups[0], own[:], later[:])
         round_z(0)
-        first = neighbour(3, 0, late, {0: "first"})
-        third = neighbour(3, 2, late, {2: "own"})
+        second = neighbour(3, 1, late, {})
+        third = neighbour(3, 2, late, {})
+        first = neighbour(3, 0, late, {})
         second_product(0)
         closing = keep.tile([P, 2 * GROUP], F32, tag="z_bf_0", align_bytes=64)
         later, own, last_own = closing[:, 0:GROUP], closing[:, GROUP : GROUP + P], closing[:, GROUP + P :]

@@ -22,7 +22,6 @@ P = 128
 PACK = 4
 K_PASS = P * PACK
 PASSES = K // K_PASS
-MX_BLOCK = 32
 BANK = 512
 STRIPE = 16
 QUADRANT = 32
@@ -31,7 +30,7 @@ CHUNKS = V // P
 HALF = P // 2
 PAIR = 2
 GROUP = V // 2
-SCALES_AHEAD = 6
+PIECE = 256
 OWN = D
 
 GATE_SCALE = 0.9 / 0.1
@@ -57,20 +56,19 @@ def tile_picked_zgcnii_gelu_po_kernel(
 
         w1_raw = {}
 
-        def load_w1(side, passes, slots=None):
-            for g in passes:
-                name = "w1_raw_%d_%d" % (side, g)
-                raw = keep.tile([P, PACK, H // 2], F32, tag=slots[g] if slots else name, name=name, align_bytes=64)
+        def load_w1(side):
+            for g in range(PASSES):
+                raw = keep.tile([P, PACK, H // 2], F32, name="w1_raw_%d_%d" % (side, g), align_bytes=64)
                 rows = w1[g * K_PASS : (g + 1) * K_PASS, side * H // 2 : (side + 1) * H // 2]
                 nc.sync.dma_start(out=raw[:], in_=rows.rearrange("(p j) c -> p j c", j=PACK))
                 w1_raw[side, g] = raw[:].rearrange("p j (m t) -> p m j t", t=PACK)
 
         def load_words(g):
-            tile = keep.tile([P, T], I32, tag="word_table_%d" % g, name="word_table", align_bytes=64)
+            tile = keep.tile([P, T], I32, name="word_table_%d" % g, align_bytes=64)
             nc.sync.dma_start(out=tile[:], in_=x_words[g].rearrange("p n r -> p (n r)").bitcast(I32))
             return tile
 
-        scale_table = keep.tile([P, T], U8, tag="scale_table", align_bytes=64)
+        scale_table = keep.tile([P, T], U8, align_bytes=64)
         nc.vector.memset(scale_table[QUADRANT : 2 * QUADRANT, :].bitcast(I32), 0)
         nc.vector.memset(scale_table[2 * QUADRANT : P, :].bitcast(I32), 0)
         picked_scales = keep.tile([P, PASSES, S], U8, align_bytes=64)
@@ -84,8 +82,8 @@ def tile_picked_zgcnii_gelu_po_kernel(
         nc.gpsimd.memset(gate_rows[:], 0.0)
         nc.sync.dma_start(out=gate_rows[0 : D * CHUNKS, :], in_=gate[:, 0, :].rearrange("d (c v) -> d c v", v=P))
         word_table.append(load_words(1))
-        load_w1(0, range(PASSES))
-        load_w1(1, range(PASSES))
+        load_w1(0)
+        load_w1(1)
         pos_lists = [load_list("pos1_list", pos1), load_list("pos2_list", pos2), load_list("pos3_list", pos3)]
         cen_list = load_list("cen_list", cen)
         w2_raw = keep.tile([P, PACK, H], F32)
@@ -100,13 +98,12 @@ def tile_picked_zgcnii_gelu_po_kernel(
 
         def quantize(name, values):
             width = values.shape[1] // PACK
-            codes = keep.tile([P, width], U32, tag=name + "_codes", name=name + "_codes", align_bytes=64)
+            codes = keep.tile([P, width], U32, name=name + "_codes", align_bytes=64)
             scales = keep.tile([P, width], U8, name=name + "_scales", align_bytes=64)
             nc.vector.quantize_mx(out=codes[:].bitcast(FP8X4), scales=scales[:], in_=values)
             return codes, scales
 
-        w1_mx = {}
-
+        early, late = slice(0, GROUP), slice(GROUP, V)
         gate_turned = work.tile([P, P], F32, tag="work", name="gate_turned")
         nc.tensor.transpose(gate_turned[:], gate_rows[:], ident[:])
         gate_cols = keep.tile([P, D * CHUNKS], F32)
@@ -121,91 +118,93 @@ def tile_picked_zgcnii_gelu_po_kernel(
             nc.scalar.activation(out=sum_gate[:], in_=spread[:], func=COPY, scale=GATE_SCALE)
             sum_gates.append(sum_gate[:])
             if d > 0:
-                part_gate = keep.tile([P, V], F32, name="part_gate_%d" % d)
-                nc.scalar.activation(out=part_gate[:], in_=spread[:], func=COPY, scale=GATE_SCALE * SUM_TO_PART)
+                part_gate = keep.tile([P, GROUP], F32, name="part_gate_%d" % d)
+                nc.scalar.activation(out=part_gate[:], in_=spread[:, late], func=COPY, scale=GATE_SCALE * SUM_TO_PART)
                 part_gates[d] = part_gate[:]
 
-        picked_words = {}
-        loose_scales = keep.tile([P, S], U8, tag="loose_scales", align_bytes=64)
+        loose_scales = keep.tile([P, S], U8, align_bytes=64)
         nc.vector.tensor_copy(loose_scales[:], scale_table[:].indirect(offs_list[:]))
         for q in range(P // QUADRANT):
+            placed = picked_scales[QUADRANT * q : QUADRANT * q + SCALE_ROWS, :, :]
             nc.scalar.dma_start(
-                out=picked_scales[QUADRANT * q : QUADRANT * q + SCALE_ROWS, :, :].rearrange("p g s -> p (g s)").bitcast(I32),
+                out=placed.rearrange("p g s -> p (g s)").bitcast(I32),
                 in_=loose_scales[PASSES * SCALE_ROWS * q : PASSES * SCALE_ROWS * (q + 1), :].bitcast(I32),
             )
-        first_pass = keep.tile([P, S], U32, align_bytes=64)
-        nc.vector.tensor_copy(first_pass[:], word_table[0][:].bitcast(U32).indirect(offs_list[:]))
-
-        def gather_last_pass(half, slot):
-            picked_words[0, half] = first_pass[:, half * BANK : (half + 1) * BANK]
-            last_pass = keep.tile([P, BANK], U32, tag=slot, name="last_pass", align_bytes=64)
-            entries = offs_list[:, half * BANK // STRIPE : (half + 1) * BANK // STRIPE]
-            nc.vector.tensor_copy(last_pass[:], word_table[1][:].bitcast(U32).indirect(entries))
-            picked_words[1, half] = last_pass[:]
-
-        gather_last_pass(0, "last_pass")
-        later_w1 = keep.tile([P, (PACK - 1) * PASSES, P, PACK], BF16, tag="later_w1", align_bytes=64)
-        later_flat = later_w1[:].rearrange("p r m j -> p (r m j)")
-        row_of = {(block, g): (PACK - 1) * g + n for g in range(PASSES) for n, block in enumerate((2, 3, 1))}
-        borrowed = row_of[1, 0] * K_PASS - 3 * K_PASS // 4
-        first_block = []
-        first_low = keep.tile([P, K_PASS], BF16, tag="first_low", align_bytes=64)
-        for g, low in enumerate((first_low[:], later_flat[:, borrowed : borrowed + K_PASS])):
-            rounded = low.rearrange("p (t m j) -> p m j t", t=PAIR, j=PACK)
-            copies = (nc.scalar.copy, nc.vector.tensor_copy) if g == 0 else (nc.scalar.copy,)
-            for n, copy in enumerate(copies):
-                share = slice(n * HALF // len(copies), (n + 1) * HALF // len(copies))
-                copy(out=rounded[:, share, :, :], in_=w1_raw[0, g][:, share, :, 0:PAIR])
-            first_block.append(quantize("w1_first_%d" % g, low))
-            if g == 0:
-                gather_last_pass(1, "first_low")
-
-        h = {}
-
-        def make_h(block, pieces=(slice(0, BANK), slice(BANK, S))):
-            h[block] = keep.tile([P, S], F32, name="h_%d" % block)
-            for cols in pieces:
-                half = cols.start // BANK
-                in_half = slice(cols.start - half * BANK, cols.stop - half * BANK)
-                acc = work.tile([P, cols.stop - cols.start], F32, tag="work", name="h_acc")
-                for g in range(PASSES):
-                    codes, scales = w1_mx[block, g]
-                    nc.tensor.matmul_mx(
-                        out=acc[:],
-                        lhsT=codes.bitcast(FP8X4),
-                        lhsT_scale=scales,
-                        rhs=picked_words[g, half][:, in_half].bitcast(FP8X4),
-                        rhs_scale=picked_scales[:, g, cols],
-                        start=(g == 0),
-                        stop=(g == PASSES - 1),
-                    )
-                nc.scalar.activation(out=h[block][:, cols], in_=acc[:], func=GELU)
-
-        def term_tile(n, width, slots):
-            if n in slots:
-                return keep.tile([P, width], F32, tag=slots[n], name="term_%d" % n, align_bytes=64)
-            return ring.tile([P, width], F32, tag="term_%d" % n, name="term_%d" % n)
-
-        z_sum = [sums.tile([P, BANK], F32, tag="z_sum_%d" % c, name="z_sum_%d" % c) for c in range(CHUNKS)]
 
         def entries_of(index_list, cols):
             return index_list[:, cols.start // STRIPE : cols.stop // STRIPE]
 
-        def mix_by_transposes(block, cols=slice(0, V)):
-            width = cols.stop - cols.start
-            terms = []
-            for d in range(D):
-                term = term_tile(d, width, {})
-                looked_up = h[block][:].indirect(entries_of(pos_lists[d], cols))
-                nc.vector.tensor_tensor(term[:], looked_up, sum_gates[d][:, cols], MULT)
-                terms.append(term)
-            own = term_tile(OWN, width, {})
-            nc.vector.tensor_tensor(own[:], h[block][:].indirect(entries_of(cen_list, cols)), terms[0][:], ADD)
+        halves = [slice(0, BANK), slice(BANK, S)]
+        first_pass = keep.tile([P, S], U32, align_bytes=64)
+        nc.vector.tensor_copy(first_pass[:], word_table[0][:].bitcast(U32).indirect(offs_list[:]))
+        picked_words = {(0, half): first_pass[:, cols] for half, cols in enumerate(halves)}
+
+        def gather_last_pass(half, slot):
+            last_pass = keep.tile([P, BANK], U32, tag=slot, name="last_pass", align_bytes=64)
+            entries = entries_of(offs_list, halves[half])
+            nc.vector.tensor_copy(last_pass[:], word_table[1][:].bitcast(U32).indirect(entries))
+            picked_words[1, half] = last_pass[:]
+
+        gather_last_pass(0, "last_pass")
+
+        w1_mx = {}
+        later_w1 = keep.tile([P, (PACK - 1) * PASSES, P, PACK], BF16, tag="later_w1", align_bytes=64)
+        later_flat = later_w1[:].rearrange("p r m j -> p (r m j)")
+        row_of = {(block, g): (PACK - 1) * g + n for g in range(PASSES) for n, block in enumerate((2, 3, 1))}
+
+        def quantize_first_block(g, rounded, copies):
+            by_row = rounded.rearrange("p (t m j) -> p m j t", t=PAIR, j=PACK)
+            for n, copy in enumerate(copies):
+                share = slice(n * HALF // len(copies), (n + 1) * HALF // len(copies))
+                copy(out=by_row[:, share, :, :], in_=w1_raw[0, g][:, share, :, 0:PAIR])
+            codes, scales = quantize("w1_first_%d" % g, rounded)
+            w1_mx[0, g] = (codes[:], scales[:])
+
+        first_rounded = keep.tile([P, K_PASS], BF16, tag="first_rounded", align_bytes=64)
+        quantize_first_block(0, first_rounded[:], (nc.scalar.copy, nc.vector.tensor_copy))
+        gather_last_pass(1, "first_rounded")
+        borrowed = row_of[1, 0] * K_PASS - 3 * K_PASS // 4
+        quantize_first_block(1, later_flat[:, borrowed : borrowed + K_PASS], (nc.scalar.copy,))
+
+        h = {}
+
+        def multiply_w1(block, g, cols, acc):
+            codes, scales = w1_mx[block, g]
+            half, start = divmod(cols.start, BANK)
+            nc.tensor.matmul_mx(
+                out=acc[:],
+                lhsT=codes.bitcast(FP8X4),
+                lhsT_scale=scales,
+                rhs=picked_words[g, half][:, start : start + cols.stop - cols.start].bitcast(FP8X4),
+                rhs_scale=picked_scales[:, g, cols],
+                start=(g == 0),
+                stop=(g == PASSES - 1),
+            )
+
+        def make_h(block):
+            h[block] = keep.tile([P, S], F32, name="h_%d" % block)
+            for cols in halves:
+                acc = work.tile([P, BANK], F32, tag="work", name="h_acc")
+                for g in range(PASSES):
+                    multiply_w1(block, g, cols, acc)
+                nc.scalar.activation(out=h[block][:, cols], in_=acc[:], func=GELU)
+
+        def look_up(block, n, cols, other, op):
+            term = ring.tile([P, cols.stop - cols.start], F32, tag="term_%d" % n, name="term_%d" % n)
+            entries = entries_of(cen_list if n == OWN else pos_lists[n], cols)
+            nc.vector.tensor_tensor(term[:], h[block][:].indirect(entries), other, op)
+            return term
+
+        z_sum = [sums.tile([P, BANK], F32, tag="z_sum_%d" % c, name="z_sum_%d" % c) for c in range(CHUNKS)]
+
+        def mix_by_transposes(block, cols):
+            terms = [look_up(block, d, cols, sum_gates[d][:, cols], MULT) for d in range(D)]
+            own = look_up(block, OWN, cols, terms[0][:], ADD)
             summands = terms[1:] + [own]
             for n, summand in enumerate(summands):
-                for c in range(width // P):
+                for c in range((cols.stop - cols.start) // P):
                     nc.tensor.matmul(
-                        out=z_sum[cols.start // P + c][:, block * P : (block + 1) * P],
+                        out=z_sum[c][:, block * P : (block + 1) * P],
                         lhsT=summand[:, c * P : (c + 1) * P],
                         rhs=ident[:],
                         start=(n == 0),
@@ -216,44 +215,31 @@ def tile_picked_zgcnii_gelu_po_kernel(
         z_part = keep.tile([P, PACK, V], F32)
 
         h[0] = keep.tile([P, S], F32, name="h_0")
-        pieces = [slice(c, c + GROUP) for c in range(0, S, GROUP)]
-        accs = [work.tile([P, cols.stop - cols.start], F32, tag="work", name="first_acc") for cols in pieces]
+        pieces = [slice(start, start + PIECE) for start in range(0, S, PIECE)]
+        accs = [work.tile([P, PIECE], F32, tag="work", name="first_acc") for cols in pieces]
         for g in range(PASSES):
-            codes, scales = first_block[g]
             for cols, acc in zip(pieces, accs):
-                nc.tensor.matmul_mx(
-                    out=acc[:],
-                    lhsT=codes[:].bitcast(FP8X4),
-                    lhsT_scale=scales[:],
-                    rhs=picked_words[g, cols.start // BANK][:, cols.start % BANK : cols.start % BANK + GROUP].bitcast(FP8X4),
-                    rhs_scale=picked_scales[:, g, cols],
-                    start=(g == 0),
-                    stop=(g == PASSES - 1),
-                )
+                multiply_w1(0, g, cols, acc)
                 if g == PASSES - 1:
                     nc.scalar.activation(out=h[0][:, cols], in_=acc[:], func=GELU)
 
-        for g in range(PASSES):
-            (nc.scalar.copy if g else nc.vector.tensor_copy)(
+        for g, copy in enumerate((nc.vector.tensor_copy, nc.scalar.copy)):
+            copy(
                 out=later_w1[:, row_of[1, g], :, :].rearrange("p (t m) j -> p m j t", t=PAIR),
                 in_=w1_raw[1, g][:, :, :, 0:PAIR],
             )
             for side in range(2):
-                copy = nc.scalar.copy if g == PASSES - 1 else nc.vector.tensor_copy
-                copy(
-                    out=later_w1[:, row_of[2, g] : row_of[3, g] + 1, side * HALF : (side + 1) * HALF, :].rearrange(
-                        "p t m j -> p m j t"
-                    ),
-                    in_=w1_raw[side, g][:, :, :, PAIR:PACK],
-                )
+                upper = later_w1[:, row_of[2, g] : row_of[3, g] + 1, side * HALF : (side + 1) * HALF, :]
+                copy(out=upper.rearrange("p t m j -> p m j t"), in_=w1_raw[side, g][:, :, :, PAIR:PACK])
             low_row, high_row = row_of[1, g] * K_PASS, row_of[2, g] * K_PASS
             codes, scales = quantize("w1_low_%d" % g, later_flat[:, low_row : low_row + K_PASS])
             w1_mx[1, g] = (codes[:], scales[:])
             codes, scales = quantize("w1_high_%d" % g, later_flat[:, high_row : high_row + PAIR * K_PASS])
             for t in range(PAIR):
                 w1_mx[PAIR + t, g] = (codes[:, t * P : (t + 1) * P], scales[:, t * P : (t + 1) * P])
+        every = slice(0, V)
         make_h(1)
-        mix_by_transposes(0)
+        mix_by_transposes(0, every)
         for block in range(PAIR, PACK):
             make_h(block)
 
@@ -264,7 +250,7 @@ def tile_picked_zgcnii_gelu_po_kernel(
                 in_=w2_raw[:, :, PACK * m0 : PACK * (m0 + HALF)].rearrange("p j (m t) -> p m j t", t=PACK),
             )
         w2_codes, w2_scales = quantize("w2", w2_bf[:].rearrange("p t m j -> p (t m j)"))
-        mix_by_transposes(1)
+        mix_by_transposes(1, every)
         turn_share = keep.tile([P, PACK], F32)
         nc.scalar.activation(out=turn_share[:], in_=turn_raw[:], func=COPY, scale=Y_SHARE)
 
@@ -280,35 +266,19 @@ def tile_picked_zgcnii_gelu_po_kernel(
                 nc.tensor.transpose(back[:, c * P : (c + 1) * P], plane_rows, ident[:])
             nc.scalar.activation(out=z_part[:, t, :], in_=back[:], func=COPY, scale=SUM_TO_PART)
 
-        def turn_back(plane, cols):
-            back = work.tile([P, GROUP], F32, tag="work", name="z_back_high")
-            for n in range(GROUP // P):
-                c = cols.start // P + n
-                rows = keep.tile([P, P], F32, name="plane_rows_%d_%d" % (plane, c), align_bytes=64)
-                nc.scalar.copy(out=rows[:], in_=z_sum[c][:, plane * P : (plane + 1) * P])
-                nc.tensor.transpose(back[:, n * P : (n + 1) * P], rows[:], ident[:])
-            nc.scalar.activation(out=z_part[:, plane, cols], in_=back[:], func=COPY, scale=SUM_TO_PART)
-
-        early, late = slice(0, GROUP), slice(GROUP, V)
         for plane, cols in ((2, early), (3, early), (2, late)):
             mix_by_transposes(plane, cols)
-            turn_back(plane, cols)
-
-        def neighbour(t, d, cols, slots):
-            term = term_tile(d, cols.stop - cols.start, slots)
-            weights = (sum_gates[0] if d == 0 else part_gates[d])[:, cols]
-            nc.vector.tensor_tensor(term[:], h[t][:].indirect(entries_of(pos_lists[d], cols)), weights, MULT)
-            return term
-
-        def close_plane(t, cols, own, later):
-            nc.vector.scalar_tensor_tensor(
-                out=z_part[:, t, cols], in0=own, scalar=SUM_TO_PART, in1=later, op0=MULT, op1=ADD
-            )
+            back = work.tile([P, GROUP], F32, tag="work", name="z_back_high")
+            for c in range(GROUP // P):
+                rows = keep.tile([P, P], F32, name="rows_%d_%d_%d" % (plane, cols.start, c), align_bytes=64)
+                nc.scalar.copy(out=rows[:], in_=z_sum[c][:, plane * P : (plane + 1) * P])
+                nc.tensor.transpose(back[:, c * P : (c + 1) * P], rows[:], ident[:])
+            nc.scalar.activation(out=z_part[:, plane, cols], in_=back[:], func=COPY, scale=SUM_TO_PART)
 
         out_codes = keep.tile([P, V], U32, align_bytes=64)
         out_scales = keep.tile([P, V], U8, align_bytes=64)
         z_bf, y, result = {}, {}, {}
-        groups = [slice(0, 2 * P), slice(2 * P, 3 * P), slice(3 * P, V)]
+        groups = [early, slice(GROUP, GROUP + P), slice(GROUP + P, V)]
 
         def width_of(group):
             return groups[group].stop - groups[group].start
@@ -334,7 +304,7 @@ def tile_picked_zgcnii_gelu_po_kernel(
                 if t % 2 == 0:
                     bank_number = 2 * group + t // 2
                     if bank_number < CHUNKS:
-                        bank = sums.tile([P, BANK], F32, tag="z_sum_%d" % bank_number, name="y_bank")
+                        bank = sums.tile([P, BANK], F32, tag="z_sum_%d" % ((bank_number + 2) % CHUNKS), name="y_bank")
                     else:
                         bank = work.tile([P, BANK], F32, tag="work", name="y_bank")
                 y[group, t] = bank[:, (t % 2) * width_of(group) : (t % 2 + 1) * width_of(group)]
@@ -380,21 +350,28 @@ def tile_picked_zgcnii_gelu_po_kernel(
             )
 
         round_z(0)
-        second = neighbour(3, 1, late, {})
-        third = neighbour(3, 2, late, {})
-        first = neighbour(3, 0, late, {})
+        second = look_up(3, 1, late, part_gates[1], MULT)
+        third = look_up(3, 2, late, part_gates[2], MULT)
+        first = look_up(3, 0, late, sum_gates[0][:, late], MULT)
         second_product(0)
         closing = keep.tile([P, 2 * GROUP], F32, tag="z_bf_0", align_bytes=64)
-        later, own, last_own = closing[:, 0:GROUP], closing[:, GROUP : GROUP + P], closing[:, GROUP + P :]
-        nc.vector.tensor_tensor(later, second[:], third[:], ADD)
-        for n, features in enumerate((own, last_own)):
-            entries = entries_of(cen_list, groups[1 + n])
-            nc.vector.tensor_tensor(features, h[3][:].indirect(entries), first[:, n * P : (n + 1) * P], ADD)
-        close_plane(3, groups[1], own, later[:, 0:P])
-        round_z(1)
-        close_plane(3, groups[2], last_own, later[:, P:GROUP])
+        neighbours, own = closing[:, 0:GROUP], closing[:, GROUP:]
+        nc.vector.tensor_tensor(neighbours, second[:], third[:], ADD)
+        quarters = [(1, slice(0, P)), (2, slice(P, GROUP))]
+        for group, cols in quarters:
+            entries = entries_of(cen_list, groups[group])
+            nc.vector.tensor_tensor(own[:, cols], h[3][:].indirect(entries), first[:, cols], ADD)
+        for group, cols in quarters:
+            nc.vector.scalar_tensor_tensor(
+                out=z_part[:, 3, groups[group]],
+                in0=own[:, cols],
+                scalar=SUM_TO_PART,
+                in1=neighbours[:, cols],
+                op0=MULT,
+                op1=ADD,
+            )
+            round_z(group)
         second_product(1)
-        round_z(2)
         second_product(2)
         combine(0, PAIR)
         combine(1, PACK)

@@ -45,9 +45,10 @@ def tile_picked_zgcnii_gelu_po_kernel(
     nc = tc.nc
     with ExitStack() as ctx:
         keep = ctx.enter_context(tc.tile_pool(name="keep", bufs=1))
-        ring = ctx.enter_context(tc.tile_pool(name="ring", bufs=3))
-        sums = ctx.enter_context(tc.psum_pool(name="sums", bufs=1))
-        work = ctx.enter_context(tc.psum_pool(name="work", bufs=4))
+        banks = ctx.enter_context(tc.psum_pool(name="banks", bufs=1))
+
+        def bank_tile(number, shape, name):
+            return banks.tile(shape, F32, tag="bank_%d" % number, name=name)
 
         def load_list(name, dram):
             tile = keep.tile(list(dram.shape), U16, name=name)
@@ -58,7 +59,7 @@ def tile_picked_zgcnii_gelu_po_kernel(
 
         def load_w1(side):
             for g in range(PASSES):
-                raw = keep.tile([P, PACK, H // 2], F32, name="w1_raw_%d_%d" % (side, g), align_bytes=64)
+                raw = keep.tile([P, PACK, H // 2], F32, tag="w1_raw_%d_%d" % (side, g), name="w1_raw", align_bytes=64)
                 rows = w1[g * K_PASS : (g + 1) * K_PASS, side * H // 2 : (side + 1) * H // 2]
                 nc.sync.dma_start(out=raw[:], in_=rows.rearrange("(p j) c -> p j c", j=PACK))
                 w1_raw[side, g] = raw[:].rearrange("p j (m t) -> p m j t", t=PACK)
@@ -104,20 +105,20 @@ def tile_picked_zgcnii_gelu_po_kernel(
             return codes, scales
 
         early, late = slice(0, GROUP), slice(GROUP, V)
-        gate_turned = work.tile([P, P], F32, tag="work", name="gate_turned")
+        gate_turned = bank_tile(4, [P, P], "gate_turned")
         nc.tensor.transpose(gate_turned[:], gate_rows[:], ident[:])
         gate_cols = keep.tile([P, D * CHUNKS], F32)
         nc.scalar.copy(out=gate_cols[:], in_=gate_turned[:, 0 : D * CHUNKS])
         sum_gates, part_gates = [], {}
         for d in range(D):
-            spread = work.tile([P, V], F32, tag="work", name="spread_%d" % d)
+            spread = bank_tile(5 + d, [P, V], "spread")
             for c in range(CHUNKS):
                 column = gate_cols[:, CHUNKS * d + c : CHUNKS * d + c + 1]
                 nc.tensor.transpose(spread[:, c * P : (c + 1) * P], column.to_broadcast([P, P]), ident[:])
             sum_gate = keep.tile([P, V], F32, name="sum_gate_%d" % d)
             nc.scalar.activation(out=sum_gate[:], in_=spread[:], func=COPY, scale=GATE_SCALE)
             sum_gates.append(sum_gate[:])
-            if d > 0:
+            if d == D - 1:
                 part_gate = keep.tile([P, GROUP], F32, name="part_gate_%d" % d)
                 nc.scalar.activation(out=part_gate[:], in_=spread[:, late], func=COPY, scale=GATE_SCALE * SUM_TO_PART)
                 part_gates[d] = part_gate[:]
@@ -183,28 +184,34 @@ def tile_picked_zgcnii_gelu_po_kernel(
 
         def make_h(block):
             h[block] = keep.tile([P, S], F32, name="h_%d" % block)
-            for cols in halves:
-                acc = work.tile([P, BANK], F32, tag="work", name="h_acc")
+            for half, cols in enumerate(halves):
+                acc = bank_tile(4 + (2 * (block - 1) + half) % 4, [P, BANK], "h_acc")
                 for g in range(PASSES):
                     multiply_w1(block, g, cols, acc)
                 nc.scalar.activation(out=h[block][:, cols], in_=acc[:], func=GELU)
 
-        def look_up(block, n, cols, other, op):
-            term = ring.tile([P, cols.stop - cols.start], F32, tag="term_%d" % n, name="term_%d" % n)
+        def look_up(block, n, cols, other, op, slot=None):
+            slot = slot or "term_%d_%d_%d" % (block, n, cols.start)
+            term = keep.tile([P, cols.stop - cols.start], F32, tag=slot, name="term", align_bytes=64)
             entries = entries_of(cen_list if n == OWN else pos_lists[n], cols)
             nc.vector.tensor_tensor(term[:], h[block][:].indirect(entries), other, op)
             return term
 
-        z_sum = [sums.tile([P, BANK], F32, tag="z_sum_%d" % c, name="z_sum_%d" % c) for c in range(CHUNKS)]
+        z_sum = [bank_tile(c, [P, PAIR * P], "z_sum") for c in range(CHUNKS)]
 
-        def mix_by_transposes(block, cols):
-            terms = [look_up(block, d, cols, sum_gates[d][:, cols], MULT) for d in range(D)]
-            own = look_up(block, OWN, cols, terms[0][:], ADD)
-            summands = terms[1:] + [own]
+        owns = {}
+
+        def own_features(block, cols, slot=None):
+            slot = slot or "own_%d_%d" % (block, cols.start)
+            own = keep.tile([P, cols.stop - cols.start], F32, tag=slot, name="own", align_bytes=64)
+            nc.scalar.activation(out=own[:], in_=h[block][:].indirect(entries_of(cen_list, cols)), func=COPY)
+            owns[block, cols.start] = own
+
+        def sum_by_transposes(summands, sums):
             for n, summand in enumerate(summands):
-                for c in range((cols.stop - cols.start) // P):
+                for c, total in enumerate(sums):
                     nc.tensor.matmul(
-                        out=z_sum[c][:, block * P : (block + 1) * P],
+                        out=total,
                         lhsT=summand[:, c * P : (c + 1) * P],
                         rhs=ident[:],
                         start=(n == 0),
@@ -212,23 +219,32 @@ def tile_picked_zgcnii_gelu_po_kernel(
                         is_transpose=True,
                     )
 
+        def mix_by_transposes(block, cols, sums, neighbours=D, last_slot=None):
+            terms = [
+                look_up(block, d, cols, sum_gates[d][:, cols], MULT, last_slot if d == D - 1 else None)
+                for d in range(neighbours)
+            ]
+            sum_by_transposes(terms[:1] + [owns[block, cols.start]] + terms[1:], sums)
+
         z_part = keep.tile([P, PACK, V], F32)
 
         h[0] = keep.tile([P, S], F32, name="h_0")
         pieces = [slice(start, start + PIECE) for start in range(0, S, PIECE)]
-        accs = [work.tile([P, PIECE], F32, tag="work", name="first_acc") for cols in pieces]
+        accs = [bank_tile(4 + n, [P, PIECE], "first_acc") for n in range(len(pieces))]
         for g in range(PASSES):
             for cols, acc in zip(pieces, accs):
                 multiply_w1(0, g, cols, acc)
                 if g == PASSES - 1:
                     nc.scalar.activation(out=h[0][:, cols], in_=acc[:], func=GELU)
 
+        every = slice(0, V)
+        own_features(0, every)
         for g, copy in enumerate((nc.vector.tensor_copy, nc.scalar.copy)):
             copy(
                 out=later_w1[:, row_of[1, g], :, :].rearrange("p (t m) j -> p m j t", t=PAIR),
                 in_=w1_raw[1, g][:, :, :, 0:PAIR],
             )
-            for side in range(2):
+            for side in (1, 0):
                 upper = later_w1[:, row_of[2, g] : row_of[3, g] + 1, side * HALF : (side + 1) * HALF, :]
                 copy(out=upper.rearrange("p t m j -> p m j t"), in_=w1_raw[side, g][:, :, :, PAIR:PACK])
             low_row, high_row = row_of[1, g] * K_PASS, row_of[2, g] * K_PASS
@@ -237,43 +253,75 @@ def tile_picked_zgcnii_gelu_po_kernel(
             codes, scales = quantize("w1_high_%d" % g, later_flat[:, high_row : high_row + PAIR * K_PASS])
             for t in range(PAIR):
                 w1_mx[PAIR + t, g] = (codes[:, t * P : (t + 1) * P], scales[:, t * P : (t + 1) * P])
-        every = slice(0, V)
         make_h(1)
-        mix_by_transposes(0, every)
-        for block in range(PAIR, PACK):
-            make_h(block)
-
-        w2_bf = keep.tile([P, PACK, P, PACK], BF16, tag="later_w1", align_bytes=64)
-        for m0 in range(0, P, HALF):
-            nc.scalar.copy(
-                out=w2_bf[:, :, m0 : m0 + HALF, :].rearrange("p t m j -> p m j t"),
-                in_=w2_raw[:, :, PACK * m0 : PACK * (m0 + HALF)].rearrange("p j (m t) -> p m j t", t=PACK),
-            )
-        w2_codes, w2_scales = quantize("w2", w2_bf[:].rearrange("p t m j -> p (t m j)"))
-        mix_by_transposes(1, every)
+        mix_by_transposes(0, every, [total[:, 0:P] for total in z_sum], last_slot="w1_raw_1_1")
+        make_h(2)
+        make_h(3)
+        own_features(1, every)
+        mix_by_transposes(1, every, [total[:, P:] for total in z_sum])
+        own_features(2, early)
+        own_features(3, early)
         turn_share = keep.tile([P, PACK], F32)
         nc.scalar.activation(out=turn_share[:], in_=turn_raw[:], func=COPY, scale=Y_SHARE)
 
         low_rows = []
         for c in range(CHUNKS):
-            rows = keep.tile([P, PAIR, 2, HALF], F32, name="low_rows_%d" % c, align_bytes=64)
-            nc.scalar.copy(out=rows[:], in_=z_sum[c][:, 0 : 2 * P].rearrange("v (s t m) -> v t s m", s=2, t=PAIR))
+            rows = keep.tile([P, PAIR, 2, HALF], F32, tag="low_rows_%d" % c, name="low_rows", align_bytes=64)
+            nc.scalar.copy(out=rows[:], in_=z_sum[c][:].rearrange("v (s t m) -> v t s m", s=2, t=PAIR))
             low_rows.append(rows)
-        for t in range(PAIR):
-            back = work.tile([P, V], F32, tag="work", name="z_back_%d" % t)
-            for c in range(CHUNKS):
-                plane_rows = low_rows[c][:, t, :, :].rearrange("v s m -> v (s m)")
-                nc.tensor.transpose(back[:, c * P : (c + 1) * P], plane_rows, ident[:])
-            nc.scalar.activation(out=z_part[:, t, :], in_=back[:], func=COPY, scale=SUM_TO_PART)
+        own_features(2, late, "term_1_2_0")
 
-        for plane, cols in ((2, early), (3, early), (2, late)):
-            mix_by_transposes(plane, cols)
-            back = work.tile([P, GROUP], F32, tag="work", name="z_back_high")
-            for c in range(GROUP // P):
-                rows = keep.tile([P, P], F32, name="rows_%d_%d_%d" % (plane, cols.start, c), align_bytes=64)
-                nc.scalar.copy(out=rows[:], in_=z_sum[c][:, plane * P : (plane + 1) * P])
-                nc.tensor.transpose(back[:, c * P : (c + 1) * P], rows[:], ident[:])
-            nc.scalar.activation(out=z_part[:, plane, cols], in_=back[:], func=COPY, scale=SUM_TO_PART)
+        def turn_back(name, sums, back):
+            for c, total in enumerate(sums):
+                rows = keep.tile(list(total.shape), F32, tag="%s_%d" % (name, c), name="rows", align_bytes=64)
+                nc.scalar.copy(out=rows[:], in_=total[:])
+                for t in range(total.shape[1] // P):
+                    nc.tensor.transpose(back[:, t, c * P : (c + 1) * P], rows[:, t * P : (t + 1) * P], ident[:])
+
+        early_sums = [bank_tile(6 + c, [P, P], "early_sum") for c in range(2)]
+        mix_by_transposes(2, early, [total[:] for total in early_sums])
+        low_backs = [bank_tile(4 + t, [P, V], "low_back") for t in range(PAIR)]
+        for c in range(CHUNKS):
+            for t in range(PAIR):
+                plane_rows = low_rows[c][:, t, :, :].rearrange("v s m -> v (s m)")
+                nc.tensor.transpose(low_backs[t][:, c * P : (c + 1) * P], plane_rows, ident[:])
+        early_back = bank_tile(0, [P, PAIR, GROUP], "early_back")
+        turn_back("early_rows_2", early_sums, early_back[:, 0:1, :])
+        for t in range(PAIR):
+            nc.scalar.activation(out=z_part[:, t, :], in_=low_backs[t][:], func=COPY, scale=SUM_TO_PART)
+        own_features(3, late, "low_rows_3")
+        early_sums = [bank_tile(2 + c, [P, P], "early_sum") for c in range(2)]
+        mix_by_transposes(3, early, [total[:] for total in early_sums])
+        turn_back("early_rows_3", early_sums, early_back[:, 1:2, :])
+
+        w2_codes = keep.tile([P, H], U32, align_bytes=64)
+        w2_scales = keep.tile([P, H], U8, align_bytes=64)
+
+        def quantize_w2(t0, slot, copy):
+            rounded = keep.tile([P, PAIR, P, PACK], BF16, tag=slot, name="w2_bf", align_bytes=64)
+            copy(
+                out=rounded[:].rearrange("p t m j -> p m j t"),
+                in_=w2_raw[:].rearrange("p j (m t) -> p m j t", t=PACK)[:, :, :, t0 : t0 + PAIR],
+            )
+            cols = slice(t0 * P, (t0 + PAIR) * P)
+            nc.vector.quantize_mx(
+                out=w2_codes[:, cols].bitcast(FP8X4),
+                scales=w2_scales[:, cols],
+                in_=rounded[:].rearrange("p t m j -> p (t m j)"),
+            )
+
+        late_sums = [bank_tile(6 + c, [P, PAIR * P], "late_sum") for c in range(2)]
+        for t in range(PAIR):
+            mix_by_transposes(PAIR + t, late, [total[:, t * P : (t + 1) * P] for total in late_sums], neighbours=D - 1)
+        quantize_w2(0, "term_3_2_0", nc.scalar.copy)
+        nc.scalar.activation(out=z_part[:, PAIR:PACK, early], in_=early_back[:], func=COPY, scale=SUM_TO_PART)
+        late_back = bank_tile(1, [P, PAIR, GROUP], "late_back")
+        turn_back("late_rows", late_sums, late_back)
+        quantize_w2(PAIR, "term_2_1_0", nc.vector.tensor_copy)
+        last_terms = keep.tile([P, PAIR, GROUP], F32, tag="term_2_2_0", align_bytes=64)
+        for t in range(PAIR):
+            entries = entries_of(pos_lists[D - 1], late)
+            nc.vector.tensor_tensor(last_terms[:, t, :], h[PAIR + t][:].indirect(entries), part_gates[D - 1], MULT)
 
         out_codes = keep.tile([P, V], U32, align_bytes=64)
         out_scales = keep.tile([P, V], U8, align_bytes=64)
@@ -289,11 +337,14 @@ def tile_picked_zgcnii_gelu_po_kernel(
         def part_to_z(out, in_):
             nc.scalar.activation(out=out, in_=in_, func=COPY, scale=1.0 / Z_SHARE)
 
+        z_slots = ("z_bf_0", "early_rows_3_0", "early_rows_3_1")
         for group, cols in enumerate(groups):
             z_bf[group] = keep.tile(
-                [P, width_of(group), PACK], BF16, tag="z_bf_%d" % group, name="z_bf", align_bytes=64
+                [P, width_of(group), PACK], BF16, tag=z_slots[group], name="z_bf", align_bytes=64
             )
-            interleave(part_to_z, z_bf[group][:, :, 0:PAIR], z_part[:, 0:PAIR, cols])
+        interleave(part_to_z, z_bf[0][:], z_part[:, :, early])
+        for group in (1, 2):
+            interleave(part_to_z, z_bf[group][:, :, 0:PAIR], z_part[:, 0:PAIR, groups[group]])
 
         def round_z(group):
             interleave(part_to_z, z_bf[group][:, :, PAIR:PACK], z_part[:, PAIR:PACK, groups[group]])
@@ -302,11 +353,7 @@ def tile_picked_zgcnii_gelu_po_kernel(
             z_codes, z_scales = quantize("z_%d" % group, z_bf[group][:].rearrange("p v t -> p (v t)"))
             for t in range(PACK):
                 if t % 2 == 0:
-                    bank_number = 2 * group + t // 2
-                    if bank_number < CHUNKS:
-                        bank = sums.tile([P, BANK], F32, tag="z_sum_%d" % ((bank_number + 2) % CHUNKS), name="y_bank")
-                    else:
-                        bank = work.tile([P, BANK], F32, tag="work", name="y_bank")
+                    bank = bank_tile((4, 2, 6)[group] + t // 2, [P, BANK], "y_bank")
                 y[group, t] = bank[:, (t % 2) * width_of(group) : (t % 2 + 1) * width_of(group)]
                 nc.tensor.matmul_mx(
                     out=y[group, t],
@@ -349,24 +396,13 @@ def tile_picked_zgcnii_gelu_po_kernel(
                 out=out_1[0].rearrange("p n r -> p (n r)").bitcast(I32)[:, cols], in_=out_codes[:, cols].bitcast(I32)
             )
 
-        round_z(0)
-        second = look_up(3, 1, late, part_gates[1], MULT)
-        third = look_up(3, 2, late, part_gates[2], MULT)
-        first = look_up(3, 0, late, sum_gates[0][:, late], MULT)
         second_product(0)
-        closing = keep.tile([P, 2 * GROUP], F32, tag="z_bf_0", align_bytes=64)
-        neighbours, own = closing[:, 0:GROUP], closing[:, GROUP:]
-        nc.vector.tensor_tensor(neighbours, second[:], third[:], ADD)
-        quarters = [(1, slice(0, P)), (2, slice(P, GROUP))]
-        for group, cols in quarters:
-            entries = entries_of(cen_list, groups[group])
-            nc.vector.tensor_tensor(own[:, cols], h[3][:].indirect(entries), first[:, cols], ADD)
-        for group, cols in quarters:
+        for group, cols in ((1, slice(0, P)), (2, slice(P, GROUP))):
             nc.vector.scalar_tensor_tensor(
-                out=z_part[:, 3, groups[group]],
-                in0=own[:, cols],
+                out=z_part[:, PAIR:PACK, groups[group]],
+                in0=late_back[:, :, cols],
                 scalar=SUM_TO_PART,
-                in1=neighbours[:, cols],
+                in1=last_terms[:, :, cols],
                 op0=MULT,
                 op1=ADD,
             )

@@ -31,6 +31,7 @@ HALF = P // 2
 PAIR = 2
 GROUP = V // 2
 PIECE = 256
+W2_SPLIT = 48
 OWN = D
 
 GATE_SCALE = 0.9 / 0.1
@@ -205,7 +206,7 @@ def tile_picked_zgcnii_gelu_po_kernel(
             slot = slot or "own_%d_%d" % (block, cols.start)
             own = keep.tile([P, cols.stop - cols.start], F32, tag=slot, name="own", align_bytes=64)
             nc.scalar.activation(out=own[:], in_=h[block][:].indirect(entries_of(cen_list, cols)), func=COPY)
-            owns[block, cols.start] = own
+            owns[block] = own
 
         def sum_by_transposes(summands, sums):
             for n, summand in enumerate(summands):
@@ -219,12 +220,15 @@ def tile_picked_zgcnii_gelu_po_kernel(
                         is_transpose=True,
                     )
 
-        def mix_by_transposes(block, cols, sums, neighbours=D, last_slot=None):
+        def look_up_terms(block, cols, neighbours=D, last_slot=None):
             terms = [
                 look_up(block, d, cols, sum_gates[d][:, cols], MULT, last_slot if d == D - 1 else None)
                 for d in range(neighbours)
             ]
-            sum_by_transposes(terms[:1] + [owns[block, cols.start]] + terms[1:], sums)
+            return terms[:1] + [owns[block][:, cols]] + terms[1:]
+
+        def mix_by_transposes(block, cols, sums, neighbours=D):
+            sum_by_transposes(look_up_terms(block, cols, neighbours), sums)
 
         z_part = keep.tile([P, PACK, V], F32)
 
@@ -254,13 +258,13 @@ def tile_picked_zgcnii_gelu_po_kernel(
             for t in range(PAIR):
                 w1_mx[PAIR + t, g] = (codes[:, t * P : (t + 1) * P], scales[:, t * P : (t + 1) * P])
         make_h(1)
-        mix_by_transposes(0, every, [total[:, 0:P] for total in z_sum], last_slot="w1_raw_1_1")
-        make_h(2)
-        make_h(3)
+        first_terms = look_up_terms(0, every, last_slot="w1_raw_1_1")
         own_features(1, every)
+        make_h(2)
+        own_features(2, every)
+        make_h(3)
+        sum_by_transposes(first_terms, [total[:, 0:P] for total in z_sum])
         mix_by_transposes(1, every, [total[:, P:] for total in z_sum])
-        own_features(2, early)
-        own_features(3, early)
         turn_share = keep.tile([P, PACK], F32)
         nc.scalar.activation(out=turn_share[:], in_=turn_raw[:], func=COPY, scale=Y_SHARE)
 
@@ -269,7 +273,7 @@ def tile_picked_zgcnii_gelu_po_kernel(
             rows = keep.tile([P, PAIR, 2, HALF], F32, tag="low_rows_%d" % c, name="low_rows", align_bytes=64)
             nc.scalar.copy(out=rows[:], in_=z_sum[c][:].rearrange("v (s t m) -> v t s m", s=2, t=PAIR))
             low_rows.append(rows)
-        own_features(2, late, "term_1_2_0")
+        own_features(3, every, "term_1_2_0")
 
         def turn_back(name, sums, back):
             for c, total in enumerate(sums):
@@ -289,35 +293,27 @@ def tile_picked_zgcnii_gelu_po_kernel(
         turn_back("early_rows_2", early_sums, early_back[:, 0:1, :])
         for t in range(PAIR):
             nc.scalar.activation(out=z_part[:, t, :], in_=low_backs[t][:], func=COPY, scale=SUM_TO_PART)
-        own_features(3, late, "low_rows_3")
         early_sums = [bank_tile(2 + c, [P, P], "early_sum") for c in range(2)]
         mix_by_transposes(3, early, [total[:] for total in early_sums])
         turn_back("early_rows_3", early_sums, early_back[:, 1:2, :])
 
-        w2_codes = keep.tile([P, H], U32, align_bytes=64)
-        w2_scales = keep.tile([P, H], U8, align_bytes=64)
+        w2_bf = keep.tile([P, PACK, P, PACK], BF16, tag="term_3_2_0", align_bytes=64)
 
-        def quantize_w2(t0, slot, copy):
-            rounded = keep.tile([P, PAIR, P, PACK], BF16, tag=slot, name="w2_bf", align_bytes=64)
+        def round_w2(share, copy):
             copy(
-                out=rounded[:].rearrange("p t m j -> p m j t"),
-                in_=w2_raw[:].rearrange("p j (m t) -> p m j t", t=PACK)[:, :, :, t0 : t0 + PAIR],
-            )
-            cols = slice(t0 * P, (t0 + PAIR) * P)
-            nc.vector.quantize_mx(
-                out=w2_codes[:, cols].bitcast(FP8X4),
-                scales=w2_scales[:, cols],
-                in_=rounded[:].rearrange("p t m j -> p (t m j)"),
+                out=w2_bf[:, :, share, :].rearrange("p t m j -> p m j t"),
+                in_=w2_raw[:].rearrange("p j (m t) -> p m j t", t=PACK)[:, share, :, :],
             )
 
         late_sums = [bank_tile(6 + c, [P, PAIR * P], "late_sum") for c in range(2)]
         for t in range(PAIR):
             mix_by_transposes(PAIR + t, late, [total[:, t * P : (t + 1) * P] for total in late_sums], neighbours=D - 1)
-        quantize_w2(0, "term_3_2_0", nc.scalar.copy)
+        round_w2(slice(0, W2_SPLIT), nc.scalar.copy)
         nc.scalar.activation(out=z_part[:, PAIR:PACK, early], in_=early_back[:], func=COPY, scale=SUM_TO_PART)
         late_back = bank_tile(1, [P, PAIR, GROUP], "late_back")
         turn_back("late_rows", late_sums, late_back)
-        quantize_w2(PAIR, "term_2_1_0", nc.vector.tensor_copy)
+        round_w2(slice(W2_SPLIT, P), nc.vector.tensor_copy)
+        w2_codes, w2_scales = quantize("w2", w2_bf[:].rearrange("p t m j -> p (t m j)"))
         last_terms = keep.tile([P, PAIR, GROUP], F32, tag="term_2_2_0", align_bytes=64)
         for t in range(PAIR):
             entries = entries_of(pos_lists[D - 1], late)
@@ -337,17 +333,15 @@ def tile_picked_zgcnii_gelu_po_kernel(
         def part_to_z(out, in_):
             nc.scalar.activation(out=out, in_=in_, func=COPY, scale=1.0 / Z_SHARE)
 
-        z_slots = ("z_bf_0", "early_rows_3_0", "early_rows_3_1")
+        z_slots = ("z_bf_0", "z_bf_1", "z_bf_2")
         for group, cols in enumerate(groups):
             z_bf[group] = keep.tile(
                 [P, width_of(group), PACK], BF16, tag=z_slots[group], name="z_bf", align_bytes=64
             )
         interleave(part_to_z, z_bf[0][:], z_part[:, :, early])
-        for group in (1, 2):
-            interleave(part_to_z, z_bf[group][:, :, 0:PAIR], z_part[:, 0:PAIR, groups[group]])
 
         def round_z(group):
-            interleave(part_to_z, z_bf[group][:, :, PAIR:PACK], z_part[:, PAIR:PACK, groups[group]])
+            interleave(part_to_z, z_bf[group][:], z_part[:, :, groups[group]])
 
         def second_product(group):
             z_codes, z_scales = quantize("z_%d" % group, z_bf[group][:].rearrange("p v t -> p (v t)"))

@@ -31,7 +31,6 @@ HALF = P // 2
 PAIR = 2
 GROUP = V // 2
 PIECE = 256
-W2_SPLIT = 48
 OWN = D
 
 GATE_SCALE = 0.9 / 0.1
@@ -56,13 +55,14 @@ def tile_picked_zgcnii_gelu_po_kernel(
             nc.sync.dma_start(tile[:], dram)
             return tile
 
-        w1_raw = {}
+        w1_raw, w1_bytes = {}, {}
 
         def load_w1(side):
             for g in range(PASSES):
                 raw = keep.tile([P, PACK, H // 2], F32, tag="w1_raw_%d_%d" % (side, g), name="w1_raw", align_bytes=64)
                 rows = w1[g * K_PASS : (g + 1) * K_PASS, side * H // 2 : (side + 1) * H // 2]
                 nc.sync.dma_start(out=raw[:], in_=rows.rearrange("(p j) c -> p j c", j=PACK))
+                w1_bytes[side, g] = raw[:].rearrange("p j c -> p (j c)")
                 w1_raw[side, g] = raw[:].rearrange("p j (m t) -> p m j t", t=PACK)
 
         def load_words(g):
@@ -86,8 +86,9 @@ def tile_picked_zgcnii_gelu_po_kernel(
         word_table.append(load_words(1))
         load_w1(0)
         load_w1(1)
-        pos_lists = [load_list("pos1_list", pos1), load_list("pos2_list", pos2), load_list("pos3_list", pos3)]
+        pos_lists = [load_list("pos1_list", pos1), load_list("pos2_list", pos2)]
         cen_list = load_list("cen_list", cen)
+        pos_lists.append(load_list("pos3_list", pos3))
         w2_raw = keep.tile([P, PACK, H], F32)
         nc.sync.dma_start(out=w2_raw[:], in_=w2.rearrange("(p j) c -> p j c", j=PACK))
         turn_raw = keep.tile([P, PACK], F32)
@@ -191,21 +192,21 @@ def tile_picked_zgcnii_gelu_po_kernel(
                     multiply_w1(block, g, cols, acc)
                 nc.scalar.activation(out=h[block][:, cols], in_=acc[:], func=GELU)
 
-        def look_up(block, n, cols, other, op, slot=None):
-            slot = slot or "term_%d_%d_%d" % (block, n, cols.start)
-            term = keep.tile([P, cols.stop - cols.start], F32, tag=slot, name="term", align_bytes=64)
-            entries = entries_of(cen_list if n == OWN else pos_lists[n], cols)
-            nc.vector.tensor_tensor(term[:], h[block][:].indirect(entries), other, op)
+        def look_up(block, d, cols, term=None):
+            if term is None:
+                slot = "term_%d_%d_%d" % (block, d, cols.start)
+                term = keep.tile([P, cols.stop - cols.start], F32, tag=slot, name="term", align_bytes=64)[:]
+            nc.vector.tensor_tensor(term, h[block][:].indirect(entries_of(pos_lists[d], cols)), sum_gates[d][:, cols], MULT)
             return term
 
         z_sum = [bank_tile(c, [P, PAIR * P], "z_sum") for c in range(CHUNKS)]
 
         owns = {}
 
-        def own_features(block, cols, slot=None):
-            slot = slot or "own_%d_%d" % (block, cols.start)
-            own = keep.tile([P, cols.stop - cols.start], F32, tag=slot, name="own", align_bytes=64)
-            nc.scalar.activation(out=own[:], in_=h[block][:].indirect(entries_of(cen_list, cols)), func=COPY)
+        def own_features(block, slot=None, own=None):
+            if own is None:
+                own = keep.tile([P, V], F32, tag=slot or "own_%d" % block, name="own", align_bytes=64)[:]
+            nc.scalar.activation(out=own, in_=h[block][:].indirect(cen_list[:]), func=COPY)
             owns[block] = own
 
         def sum_by_transposes(summands, sums):
@@ -220,11 +221,8 @@ def tile_picked_zgcnii_gelu_po_kernel(
                         is_transpose=True,
                     )
 
-        def look_up_terms(block, cols, neighbours=D, last_slot=None):
-            terms = [
-                look_up(block, d, cols, sum_gates[d][:, cols], MULT, last_slot if d == D - 1 else None)
-                for d in range(neighbours)
-            ]
+        def look_up_terms(block, cols, neighbours=D, last_term=None):
+            terms = [look_up(block, d, cols, last_term if d == D - 1 else None) for d in range(neighbours)]
             return terms[:1] + [owns[block][:, cols]] + terms[1:]
 
         def mix_by_transposes(block, cols, sums, neighbours=D):
@@ -242,7 +240,6 @@ def tile_picked_zgcnii_gelu_po_kernel(
                     nc.scalar.activation(out=h[0][:, cols], in_=acc[:], func=GELU)
 
         every = slice(0, V)
-        own_features(0, every)
         for g, copy in enumerate((nc.vector.tensor_copy, nc.scalar.copy)):
             copy(
                 out=later_w1[:, row_of[1, g], :, :].rearrange("p (t m) j -> p m j t", t=PAIR),
@@ -257,11 +254,12 @@ def tile_picked_zgcnii_gelu_po_kernel(
             codes, scales = quantize("w1_high_%d" % g, later_flat[:, high_row : high_row + PAIR * K_PASS])
             for t in range(PAIR):
                 w1_mx[PAIR + t, g] = (codes[:, t * P : (t + 1) * P], scales[:, t * P : (t + 1) * P])
+        own_features(0, own=w1_bytes[1, 1][:, 0:V])
         make_h(1)
-        first_terms = look_up_terms(0, every, last_slot="w1_raw_1_1")
-        own_features(1, every)
+        first_terms = look_up_terms(0, every, last_term=w1_bytes[1, 1][:, V:])
+        own_features(1)
         make_h(2)
-        own_features(2, every)
+        own_features(2)
         make_h(3)
         sum_by_transposes(first_terms, [total[:, 0:P] for total in z_sum])
         mix_by_transposes(1, every, [total[:, P:] for total in z_sum])
@@ -273,7 +271,7 @@ def tile_picked_zgcnii_gelu_po_kernel(
             rows = keep.tile([P, PAIR, 2, HALF], F32, tag="low_rows_%d" % c, name="low_rows", align_bytes=64)
             nc.scalar.copy(out=rows[:], in_=z_sum[c][:].rearrange("v (s t m) -> v t s m", s=2, t=PAIR))
             low_rows.append(rows)
-        own_features(3, every, "term_1_2_0")
+        own_features(3, "term_1_2_0")
 
         def turn_back(name, sums, back):
             for c, total in enumerate(sums):
@@ -308,11 +306,11 @@ def tile_picked_zgcnii_gelu_po_kernel(
         late_sums = [bank_tile(6 + c, [P, PAIR * P], "late_sum") for c in range(2)]
         for t in range(PAIR):
             mix_by_transposes(PAIR + t, late, [total[:, t * P : (t + 1) * P] for total in late_sums], neighbours=D - 1)
-        round_w2(slice(0, W2_SPLIT), nc.scalar.copy)
+        round_w2(slice(0, HALF), nc.scalar.copy)
         nc.scalar.activation(out=z_part[:, PAIR:PACK, early], in_=early_back[:], func=COPY, scale=SUM_TO_PART)
         late_back = bank_tile(1, [P, PAIR, GROUP], "late_back")
         turn_back("late_rows", late_sums, late_back)
-        round_w2(slice(W2_SPLIT, P), nc.vector.tensor_copy)
+        round_w2(slice(HALF, P), nc.vector.tensor_copy)
         w2_codes, w2_scales = quantize("w2", w2_bf[:].rearrange("p t m j -> p (t m j)"))
         last_terms = keep.tile([P, PAIR, GROUP], F32, tag="term_2_2_0", align_bytes=64)
         for t in range(PAIR):
@@ -375,12 +373,15 @@ def tile_picked_zgcnii_gelu_po_kernel(
                     planes = slice(t + 1 - planes_a_store, t + 1)
                     nc.sync.dma_start(out=rows[:, planes, :], in_=result[group][:, planes, :])
 
-        def hand_on(name, shares):
+        def round_results(name, shares):
             cols = slice(groups[shares[0][0]].start, groups[shares[-1][0]].stop)
             out_bf = keep.tile([P, cols.stop - cols.start, PACK], BF16, name=name, align_bytes=64)
             for group, copy in shares:
                 own_cols = slice(groups[group].start - cols.start, groups[group].stop - cols.start)
                 interleave(copy, out_bf[:, own_cols, :], result[group][:])
+            return cols, out_bf
+
+        def hand_on(cols, out_bf):
             nc.vector.quantize_mx(
                 out=out_codes[:, cols].bitcast(FP8X4),
                 scales=out_scales[:, cols],
@@ -406,8 +407,10 @@ def tile_picked_zgcnii_gelu_po_kernel(
         combine(0, PAIR)
         combine(1, PACK)
         combine(2, PACK)
-        hand_on("out_bf_first", [(0, nc.scalar.copy)])
-        hand_on("out_bf_last", [(1, nc.scalar.copy), (2, nc.vector.tensor_copy)])
+        first_rounded_out = round_results("out_bf_first", [(0, nc.scalar.copy)])
+        last_rounded_out = round_results("out_bf_last", [(1, nc.scalar.copy), (2, nc.vector.tensor_copy)])
+        hand_on(*first_rounded_out)
+        hand_on(*last_rounded_out)
 
         for q in range(P // QUADRANT):
             queue = nc.sync if q % 2 == 0 else nc.scalar

@@ -121,8 +121,8 @@ def tile_picked_zgcnii_gelu_po_kernel(
             nc.scalar.activation(out=sum_gate[:], in_=spread[:], func=COPY, scale=GATE_SCALE)
             sum_gates.append(sum_gate[:])
             if d == D - 1:
-                part_gate = keep.tile([P, GROUP], F32, name="part_gate_%d" % d)
-                nc.scalar.activation(out=part_gate[:], in_=spread[:, late], func=COPY, scale=GATE_SCALE * SUM_TO_PART)
+                part_gate = keep.tile([P, V], F32, name="part_gate_%d" % d)
+                nc.scalar.activation(out=part_gate[:], in_=spread[:], func=COPY, scale=GATE_SCALE * SUM_TO_PART)
                 part_gates[d] = part_gate[:]
 
         loose_scales = keep.tile([P, S], U8, align_bytes=64)
@@ -273,49 +273,45 @@ def tile_picked_zgcnii_gelu_po_kernel(
             low_rows.append(rows)
         own_features(3, "term_1_2_0")
 
-        def turn_back(name, sums, back):
-            for c, total in enumerate(sums):
-                rows = keep.tile(list(total.shape), F32, tag="%s_%d" % (name, c), name="rows", align_bytes=64)
-                nc.scalar.copy(out=rows[:], in_=total[:])
-                for t in range(total.shape[1] // P):
-                    nc.tensor.transpose(back[:, t, c * P : (c + 1) * P], rows[:, t * P : (t + 1) * P], ident[:])
-
-        early_sums = [bank_tile(6 + c, [P, P], "early_sum") for c in range(2)]
-        mix_by_transposes(2, early, [total[:] for total in early_sums])
         low_backs = [bank_tile(4 + t, [P, V], "low_back") for t in range(PAIR)]
         for c in range(CHUNKS):
             for t in range(PAIR):
                 plane_rows = low_rows[c][:, t, :, :].rearrange("v s m -> v (s m)")
                 nc.tensor.transpose(low_backs[t][:, c * P : (c + 1) * P], plane_rows, ident[:])
-        early_back = bank_tile(0, [P, PAIR, GROUP], "early_back")
-        turn_back("early_rows_2", early_sums, early_back[:, 0:1, :])
         for t in range(PAIR):
             nc.scalar.activation(out=z_part[:, t, :], in_=low_backs[t][:], func=COPY, scale=SUM_TO_PART)
-        early_sums = [bank_tile(2 + c, [P, P], "early_sum") for c in range(2)]
-        mix_by_transposes(3, early, [total[:] for total in early_sums])
-        turn_back("early_rows_3", early_sums, early_back[:, 1:2, :])
+        high_sums = [bank_tile(c, [P, PAIR * P], "high_sum") for c in range(CHUNKS)]
+        for t in range(PAIR):
+            mix_by_transposes(PAIR + t, every, [total[:, t * P : (t + 1) * P] for total in high_sums], neighbours=D - 1)
 
-        w2_bf = keep.tile([P, PACK, P, PACK], BF16, tag="term_3_2_0", align_bytes=64)
+        w2_codes = keep.tile([P, H], U32, align_bytes=64)
+        w2_scales = keep.tile([P, H], U8, align_bytes=64)
 
-        def round_w2(share, copy):
+        def quantize_w2(t0, slot, copy):
+            rounded = keep.tile([P, PAIR, P, PACK], BF16, tag=slot, name="w2_bf", align_bytes=64)
             copy(
-                out=w2_bf[:, :, share, :].rearrange("p t m j -> p m j t"),
-                in_=w2_raw[:].rearrange("p j (m t) -> p m j t", t=PACK)[:, share, :, :],
+                out=rounded[:].rearrange("p t m j -> p m j t"),
+                in_=w2_raw[:].rearrange("p j (m t) -> p m j t", t=PACK)[:, :, :, t0 : t0 + PAIR],
+            )
+            cols = slice(t0 * P, (t0 + PAIR) * P)
+            nc.vector.quantize_mx(
+                out=w2_codes[:, cols].bitcast(FP8X4),
+                scales=w2_scales[:, cols],
+                in_=rounded[:].rearrange("p t m j -> p (t m j)"),
             )
 
-        late_sums = [bank_tile(6 + c, [P, PAIR * P], "late_sum") for c in range(2)]
+        quantize_w2(0, "low_rows_3", nc.scalar.copy)
+        high_backs = [bank_tile(6 + half, [P, PAIR, GROUP], "high_back") for half in range(2)]
+        for c, total in enumerate(high_sums):
+            rows = keep.tile([P, PAIR * P], F32, tag="high_rows_%d" % c, name="high_rows", align_bytes=64)
+            nc.scalar.copy(out=rows[:], in_=total[:])
+            for t in range(PAIR):
+                back = high_backs[c // 2][:, t, (c % 2) * P : (c % 2 + 1) * P]
+                nc.tensor.transpose(back, rows[:, t * P : (t + 1) * P], ident[:])
+        quantize_w2(PAIR, "high_rows_1", nc.scalar.copy)
+        last_terms = keep.tile([P, PAIR, V], F32, tag="term_2_0_0", align_bytes=64)
         for t in range(PAIR):
-            mix_by_transposes(PAIR + t, late, [total[:, t * P : (t + 1) * P] for total in late_sums], neighbours=D - 1)
-        round_w2(slice(0, HALF), nc.scalar.copy)
-        nc.scalar.activation(out=z_part[:, PAIR:PACK, early], in_=early_back[:], func=COPY, scale=SUM_TO_PART)
-        late_back = bank_tile(1, [P, PAIR, GROUP], "late_back")
-        turn_back("late_rows", late_sums, late_back)
-        round_w2(slice(HALF, P), nc.vector.tensor_copy)
-        w2_codes, w2_scales = quantize("w2", w2_bf[:].rearrange("p t m j -> p (t m j)"))
-        last_terms = keep.tile([P, PAIR, GROUP], F32, tag="term_2_2_0", align_bytes=64)
-        for t in range(PAIR):
-            entries = entries_of(pos_lists[D - 1], late)
-            nc.vector.tensor_tensor(last_terms[:, t, :], h[PAIR + t][:].indirect(entries), part_gates[D - 1], MULT)
+            nc.vector.tensor_tensor(last_terms[:, t, :], h[PAIR + t][:].indirect(pos_lists[D - 1][:]), part_gates[D - 1], MULT)
 
         out_codes = keep.tile([P, V], U32, align_bytes=64)
         out_scales = keep.tile([P, V], U8, align_bytes=64)
@@ -336,16 +332,20 @@ def tile_picked_zgcnii_gelu_po_kernel(
             z_bf[group] = keep.tile(
                 [P, width_of(group), PACK], BF16, tag=z_slots[group], name="z_bf", align_bytes=64
             )
-        interleave(part_to_z, z_bf[0][:], z_part[:, :, early])
+
+        def part_to_z_on_vector(out, in_):
+            nc.vector.tensor_scalar(out=out, in0=in_, scalar1=1.0 / Z_SHARE, scalar2=None, op0=MULT)
 
         def round_z(group):
-            interleave(part_to_z, z_bf[group][:], z_part[:, :, groups[group]])
+            start = groups[group].start
+            for n, copy in enumerate((part_to_z, part_to_z_on_vector)[: width_of(group) // P]):
+                interleave(copy, z_bf[group][:, n * P : (n + 1) * P, :], z_part[:, :, start + n * P : start + (n + 1) * P])
 
         def second_product(group):
             z_codes, z_scales = quantize("z_%d" % group, z_bf[group][:].rearrange("p v t -> p (v t)"))
             for t in range(PACK):
                 if t % 2 == 0:
-                    bank = bank_tile((4, 2, 6)[group] + t // 2, [P, BANK], "y_bank")
+                    bank = bank_tile((4, 0, 2)[group] + t // 2, [P, BANK], "y_bank")
                 y[group, t] = bank[:, (t % 2) * width_of(group) : (t % 2 + 1) * width_of(group)]
                 nc.tensor.matmul_mx(
                     out=y[group, t],
@@ -391,17 +391,17 @@ def tile_picked_zgcnii_gelu_po_kernel(
                 out=out_1[0].rearrange("p n r -> p (n r)").bitcast(I32)[:, cols], in_=out_codes[:, cols].bitcast(I32)
             )
 
-        second_product(0)
-        for group, cols in ((1, slice(0, P)), (2, slice(P, GROUP))):
+        for group, half, cols in ((0, 0, early), (1, 1, slice(0, P)), (2, 1, slice(P, GROUP))):
             nc.vector.scalar_tensor_tensor(
                 out=z_part[:, PAIR:PACK, groups[group]],
-                in0=late_back[:, :, cols],
+                in0=high_backs[half][:, :, cols],
                 scalar=SUM_TO_PART,
-                in1=last_terms[:, :, cols],
+                in1=last_terms[:, :, groups[group]],
                 op0=MULT,
                 op1=ADD,
             )
             round_z(group)
+        second_product(0)
         second_product(1)
         second_product(2)
         combine(0, PAIR)

from contextlib import ExitStack

import concourse.mybir as mybir
from concourse.masks import make_identity

K, T, S, D, V, H = 1024, 4096, 1024, 3, 512, 512
FLOPS = 2 * K * H * S + 2 * H * H * V

F32 = mybir.dt.float32
BF16 = mybir.dt.bfloat16
I32 = mybir.dt.int32
U32 = mybir.dt.uint32
U16 = mybir.dt.uint16
U8 = mybir.dt.uint8
FP8X4 = mybir.dt.float8_e4m3fn_x4
MULT = mybir.AluOpType.mult
ADD = mybir.AluOpType.add
COPY = mybir.ActivationFunctionType.Copy
GELU = mybir.ActivationFunctionType.Gelu_apprx_tanh

P = 128
PACK = 4
K_PASS = P * PACK
PASSES = K // K_PASS
BANK = 512
STRIPE = 16
QUADRANT = 32
SCALE_ROWS = 4
CHUNKS = V // P
HALF = P // 2
PAIR = 2
GROUP = V // 2
PIECE = 256
OWN = D

GATE_SCALE = 0.9 / 0.1
Z_SHARE = 0.6
SUM_TO_PART = Z_SHARE * 0.1
Y_SHARE = 0.4


def tile_picked_zgcnii_gelu_po_kernel(
    tc, x_words, x_scales, w1, w2, gate, turn, offs, cen, pos1, pos2, pos3, out_0, out_1, out_2
):
    nc = tc.nc
    with ExitStack() as ctx:
        keep = ctx.enter_context(tc.tile_pool(name="keep", bufs=1))
        banks = ctx.enter_context(tc.psum_pool(name="banks", bufs=1))

        def bank_tile(number, shape, name):
            return banks.tile(shape, F32, tag="bank_%d" % number, name=name)

        def load_list(name, dram):
            tile = keep.tile(list(dram.shape), U16, name=name)
            nc.sync.dma_start(tile[:], dram)
            return tile

        w1_raw, w1_bytes = {}, {}

        def load_w1(side):
            for g in range(PASSES):
                raw = keep.tile([P, PACK, H // 2], F32, tag="w1_raw_%d_%d" % (side, g), name="w1_raw", align_bytes=64)
                rows = w1[g * K_PASS : (g + 1) * K_PASS, side * H // 2 : (side + 1) * H // 2]
                nc.sync.dma_start(out=raw[:], in_=rows.rearrange("(p j) c -> p j c", j=PACK))
                w1_bytes[side, g] = raw[:].rearrange("p j c -> p (j c)")
                w1_raw[side, g] = raw[:].rearrange("p j (m t) -> p m j t", t=PACK)

        def load_words(g):
            tile = keep.tile([P, T], I32, name="word_table_%d" % g, align_bytes=64)
            nc.sync.dma_start(out=tile[:], in_=x_words[g].rearrange("p n r -> p (n r)").bitcast(I32))
            return tile

        scale_table = keep.tile([P, T], U8, align_bytes=64)
        nc.vector.memset(scale_table[QUADRANT : 2 * QUADRANT, :].bitcast(I32), 0)
        nc.vector.memset(scale_table[2 * QUADRANT : P, :].bitcast(I32), 0)
        picked_scales = keep.tile([P, PASSES, S], U8, align_bytes=64)
        nc.vector.memset(picked_scales[:].rearrange("p g s -> p (g s)").bitcast(I32), 0)

        offs_list = load_list("offs_list", offs)
        for g in range(PASSES):
            nc.sync.dma_start(out=scale_table[g:QUADRANT:PASSES, :].bitcast(I32), in_=x_scales[g].bitcast(I32))
        word_table = [load_words(0)]
        gate_rows = keep.tile([P, P], F32)
        nc.gpsimd.memset(gate_rows[:], 0.0)
        nc.sync.dma_start(out=gate_rows[0 : D * CHUNKS, :], in_=gate[:, 0, :].rearrange("d (c v) -> d c v", v=P))
        word_table.append(load_words(1))
        load_w1(0)
        load_w1(1)
        pos_lists = [load_list("pos1_list", pos1), load_list("pos2_list", pos2)]
        cen_list = load_list("cen_list", cen)
        pos_lists.append(load_list("pos3_list", pos3))
        w2_raw = keep.tile([P, PACK, H], F32)
        nc.sync.dma_start(out=w2_raw[:], in_=w2.rearrange("(p j) c -> p j c", j=PACK))
        turn_raw = keep.tile([P, PACK], F32)
        nc.sync.dma_start(out=turn_raw[:], in_=turn.rearrange("(p t) o -> p (t o)", t=PACK))

        ident = keep.tile([P, P], F32)
        make_identity(nc, ident[:])
        table_warm_up = keep.tile([P, 1], F32)
        nc.scalar.activation(out=table_warm_up[:], in_=ident[:, 0:1], func=GELU)

        def quantize(name, values):
            width = values.shape[1] // PACK
            codes = keep.tile([P, width], U32, name=name + "_codes", align_bytes=64)
            scales = keep.tile([P, width], U8, name=name + "_scales", align_bytes=64)
            nc.vector.quantize_mx(out=codes[:].bitcast(FP8X4), scales=scales[:], in_=values)
            return codes, scales

        early, late = slice(0, GROUP), slice(GROUP, V)
        gate_turned = bank_tile(4, [P, P], "gate_turned")
        nc.tensor.transpose(gate_turned[:], gate_rows[:], ident[:])
        gate_cols = keep.tile([P, D * CHUNKS], F32)
        nc.scalar.copy(out=gate_cols[:], in_=gate_turned[:, 0 : D * CHUNKS])
        sum_gates, part_gates = [], {}
        for d in range(D):
            spread = bank_tile(5 + d, [P, V], "spread")
            for c in range(CHUNKS):
                column = gate_cols[:, CHUNKS * d + c : CHUNKS * d + c + 1]
                nc.tensor.transpose(spread[:, c * P : (c + 1) * P], column.to_broadcast([P, P]), ident[:])
            sum_gate = keep.tile([P, V], F32, name="sum_gate_%d" % d)
            nc.scalar.activation(out=sum_gate[:], in_=spread[:], func=COPY, scale=GATE_SCALE)
            sum_gates.append(sum_gate[:])
            if d == D - 1:
                part_gate = keep.tile([P, V], F32, name="part_gate_%d" % d)
                nc.scalar.activation(out=part_gate[:], in_=spread[:], func=COPY, scale=GATE_SCALE * SUM_TO_PART)
                part_gates[d] = part_gate[:]

        loose_scales = keep.tile([P, S], U8, align_bytes=64)
        nc.vector.tensor_copy(loose_scales[:], scale_table[:].indirect(offs_list[:]))
        for q in range(P // QUADRANT):
            placed = picked_scales[QUADRANT * q : QUADRANT * q + SCALE_ROWS, :, :]
            nc.scalar.dma_start(
                out=placed.rearrange("p g s -> p (g s)").bitcast(I32),
                in_=loose_scales[PASSES * SCALE_ROWS * q : PASSES * SCALE_ROWS * (q + 1), :].bitcast(I32),
            )

        def entries_of(index_list, cols):
            return index_list[:, cols.start // STRIPE : cols.stop // STRIPE]

        halves = [slice(0, BANK), slice(BANK, S)]
        first_pass = keep.tile([P, S], U32, align_bytes=64)
        nc.vector.tensor_copy(first_pass[:], word_table[0][:].bitcast(U32).indirect(offs_list[:]))
        picked_words = {(0, half): first_pass[:, cols] for half, cols in enumerate(halves)}

        def gather_last_pass(half, slot):
            last_pass = keep.tile([P, BANK], U32, tag=slot, name="last_pass", align_bytes=64)
            entries = entries_of(offs_list, halves[half])
            nc.vector.tensor_copy(last_pass[:], word_table[1][:].bitcast(U32).indirect(entries))
            picked_words[1, half] = last_pass[:]

        gather_last_pass(0, "last_pass")

        w1_mx = {}
        later_w1 = keep.tile([P, (PACK - 1) * PASSES, P, PACK], BF16, tag="later_w1", align_bytes=64)
        later_flat = later_w1[:].rearrange("p r m j -> p (r m j)")
        row_of = {(block, g): (PACK - 1) * g + n for g in range(PASSES) for n, block in enumerate((2, 3, 1))}

        def quantize_first_block(g, rounded, copies):
            by_row = rounded.rearrange("p (t m j) -> p m j t", t=PAIR, j=PACK)
            for n, copy in enumerate(copies):
                share = slice(n * HALF // len(copies), (n + 1) * HALF // len(copies))
                copy(out=by_row[:, share, :, :], in_=w1_raw[0, g][:, share, :, 0:PAIR])
            codes, scales = quantize("w1_first_%d" % g, rounded)
            w1_mx[0, g] = (codes[:], scales[:])

        first_rounded = keep.tile([P, K_PASS], BF16, tag="first_rounded", align_bytes=64)
        quantize_first_block(0, first_rounded[:], (nc.scalar.copy, nc.vector.tensor_copy))
        gather_last_pass(1, "first_rounded")
        borrowed = row_of[1, 0] * K_PASS - 3 * K_PASS // 4
        quantize_first_block(1, later_flat[:, borrowed : borrowed + K_PASS], (nc.scalar.copy,))

        h = {}

        def multiply_w1(block, g, cols, acc):
            codes, scales = w1_mx[block, g]
            half, start = divmod(cols.start, BANK)
            nc.tensor.matmul_mx(
                out=acc[:],
                lhsT=codes.bitcast(FP8X4),
                lhsT_scale=scales,
                rhs=picked_words[g, half][:, start : start + cols.stop - cols.start].bitcast(FP8X4),
                rhs_scale=picked_scales[:, g, cols],
                start=(g == 0),
                stop=(g == PASSES - 1),
            )

        def make_h(block):
            h[block] = keep.tile([P, S], F32, name="h_%d" % block)
            for half, cols in enumerate(halves):
                acc = bank_tile(4 + (2 * (block - 1) + half) % 4, [P, BANK], "h_acc")
                for g in range(PASSES):
                    multiply_w1(block, g, cols, acc)
                nc.scalar.activation(out=h[block][:, cols], in_=acc[:], func=GELU)

        def look_up(block, d, cols, term=None):
            if term is None:
                slot = "term_%d_%d_%d" % (block, d, cols.start)
                term = keep.tile([P, cols.stop - cols.start], F32, tag=slot, name="term", align_bytes=64)[:]
            nc.vector.tensor_tensor(term, h[block][:].indirect(entries_of(pos_lists[d], cols)), sum_gates[d][:, cols], MULT)
            return term

        z_sum = [bank_tile(c, [P, PAIR * P], "z_sum") for c in range(CHUNKS)]

        owns = {}

        def own_features(block, slot=None, own=None):
            if own is None:
                own = keep.tile([P, V], F32, tag=slot or "own_%d" % block, name="own", align_bytes=64)[:]
            nc.scalar.activation(out=own, in_=h[block][:].indirect(cen_list[:]), func=COPY)
            owns[block] = own

        def sum_by_transposes(summands, sums):
            for n, summand in enumerate(summands):
                for c, total in enumerate(sums):
                    nc.tensor.matmul(
                        out=total,
                        lhsT=summand[:, c * P : (c + 1) * P],
                        rhs=ident[:],
                        start=(n == 0),
                        stop=(n == len(summands) - 1),
                        is_transpose=True,
                    )

        def look_up_terms(block, cols, neighbours=D, last_term=None):
            terms = [look_up(block, d, cols, last_term if d == D - 1 else None) for d in range(neighbours)]
            return terms[:1] + [owns[block][:, cols]] + terms[1:]

        def mix_by_transposes(block, cols, sums, neighbours=D):
            sum_by_transposes(look_up_terms(block, cols, neighbours), sums)

        z_part = keep.tile([P, PACK, V], F32)

        h[0] = keep.tile([P, S], F32, name="h_0")
        pieces = [slice(start, start + PIECE) for start in range(0, S, PIECE)]
        accs = [bank_tile(4 + n, [P, PIECE], "first_acc") for n in range(len(pieces))]
        for g in range(PASSES):
            for cols, acc in zip(pieces, accs):
                multiply_w1(0, g, cols, acc)
                if g == PASSES - 1:
                    nc.scalar.activation(out=h[0][:, cols], in_=acc[:], func=GELU)

        every = slice(0, V)
        for g, copy in enumerate((nc.vector.tensor_copy, nc.scalar.copy)):
            copy(
                out=later_w1[:, row_of[1, g], :, :].rearrange("p (t m) j -> p m j t", t=PAIR),
                in_=w1_raw[1, g][:, :, :, 0:PAIR],
            )
            for side in (1, 0):
                upper = later_w1[:, row_of[2, g] : row_of[3, g] + 1, side * HALF : (side + 1) * HALF, :]
                copy(out=upper.rearrange("p t m j -> p m j t"), in_=w1_raw[side, g][:, :, :, PAIR:PACK])
            low_row, high_row = row_of[1, g] * K_PASS, row_of[2, g] * K_PASS
            codes, scales = quantize("w1_low_%d" % g, later_flat[:, low_row : low_row + K_PASS])
            w1_mx[1, g] = (codes[:], scales[:])
            codes, scales = quantize("w1_high_%d" % g, later_flat[:, high_row : high_row + PAIR * K_PASS])
            for t in range(PAIR):
                w1_mx[PAIR + t, g] = (codes[:, t * P : (t + 1) * P], scales[:, t * P : (t + 1) * P])
        own_features(0, own=w1_bytes[1, 1][:, 0:V])
        make_h(1)
        first_terms = look_up_terms(0, every, last_term=w1_bytes[1, 1][:, V:])
        own_features(1)
        make_h(2)
        own_features(2)
        make_h(3)
        sum_by_transposes(first_terms, [total[:, 0:P] for total in z_sum])
        mix_by_transposes(1, every, [total[:, P:] for total in z_sum])
        turn_share = keep.tile([P, PACK], F32)
        nc.scalar.activation(out=turn_share[:], in_=turn_raw[:], func=COPY, scale=Y_SHARE)

        low_rows = []
        for c in range(CHUNKS):
            rows = keep.tile([P, PAIR, 2, HALF], F32, tag="low_rows_%d" % c, name="low_rows", align_bytes=64)
            nc.scalar.copy(out=rows[:], in_=z_sum[c][:].rearrange("v (s t m) -> v t s m", s=2, t=PAIR))
            low_rows.append(rows)
        own_features(3, "term_1_2_0")

        low_backs = [bank_tile(4 + t, [P, V], "low_back") for t in range(PAIR)]
        for c in range(CHUNKS):
            for t in range(PAIR):
                plane_rows = low_rows[c][:, t, :, :].rearrange("v s m -> v (s m)")
                nc.tensor.transpose(low_backs[t][:, c * P : (c + 1) * P], plane_rows, ident[:])
        for t in range(PAIR):
            nc.scalar.activation(out=z_part[:, t, :], in_=low_backs[t][:], func=COPY, scale=SUM_TO_PART)
        high_sums = [bank_tile(c, [P, PAIR * P], "high_sum") for c in range(CHUNKS)]
        for t in range(PAIR):
            mix_by_transposes(PAIR + t, every, [total[:, t * P : (t + 1) * P] for total in high_sums], neighbours=D - 1)

        w2_codes = keep.tile([P, H], U32, align_bytes=64)
        w2_scales = keep.tile([P, H], U8, align_bytes=64)

        def quantize_w2(t0, slot, copy):
            rounded = keep.tile([P, PAIR, P, PACK], BF16, tag=slot, name="w2_bf", align_bytes=64)
            copy(
                out=rounded[:].rearrange("p t m j -> p m j t"),
                in_=w2_raw[:].rearrange("p j (m t) -> p m j t", t=PACK)[:, :, :, t0 : t0 + PAIR],
            )
            cols = slice(t0 * P, (t0 + PAIR) * P)
            nc.vector.quantize_mx(
                out=w2_codes[:, cols].bitcast(FP8X4),
                scales=w2_scales[:, cols],
                in_=rounded[:].rearrange("p t m j -> p (t m j)"),
            )

        quantize_w2(0, "low_rows_3", nc.scalar.copy)
        high_backs = [bank_tile(6 + half, [P, PAIR, GROUP], "high_back") for half in range(2)]
        for c, total in enumerate(high_sums):
            rows = keep.tile([P, PAIR * P], F32, tag="high_rows_%d" % c, name="high_rows", align_bytes=64)
            nc.scalar.copy(out=rows[:], in_=total[:])
            for t in range(PAIR):
                back = high_backs[c // 2][:, t, (c % 2) * P : (c % 2 + 1) * P]
                nc.tensor.transpose(back, rows[:, t * P : (t + 1) * P], ident[:])
        quantize_w2(PAIR, "high_rows_1", nc.scalar.copy)
        last_terms = keep.tile([P, PAIR, V], F32, tag="term_2_0_0", align_bytes=64)
        for t in range(PAIR):
            nc.vector.tensor_tensor(last_terms[:, t, :], h[PAIR + t][:].indirect(pos_lists[D - 1][:]), part_gates[D - 1], MULT)

        out_codes = keep.tile([P, V], U32, align_bytes=64)
        out_scales = keep.tile([P, V], U8, align_bytes=64)
        z_bf, y, result = {}, {}, {}
        groups = [early, slice(GROUP, GROUP + P), slice(GROUP + P, V)]

        def width_of(group):
            return groups[group].stop - groups[group].start

        def interleave(copy, out, in_):
            copy(out=out.rearrange("p (v i) t -> p v t i", i=PACK), in_=in_.rearrange("p t (v i) -> p v t i", i=PACK))

        def part_to_z(out, in_):
            nc.scalar.activation(out=out, in_=in_, func=COPY, scale=1.0 / Z_SHARE)

        z_slots = ("z_bf_0", "z_bf_1", "z_bf_2")
        for group, cols in enumerate(groups):
            z_bf[group] = keep.tile(
                [P, width_of(group), PACK], BF16, tag=z_slots[group], name="z_bf", align_bytes=64
            )

        def part_to_z_on_vector(out, in_):
            nc.vector.tensor_scalar(out=out, in0=in_, scalar1=1.0 / Z_SHARE, scalar2=None, op0=MULT)

        def round_z(group):
            start = groups[group].start
            for n, copy in enumerate((part_to_z, part_to_z_on_vector)[: width_of(group) // P]):
                interleave(copy, z_bf[group][:, n * P : (n + 1) * P, :], z_part[:, :, start + n * P : start + (n + 1) * P])

        def second_product(group):
            z_codes, z_scales = quantize("z_%d" % group, z_bf[group][:].rearrange("p v t -> p (v t)"))
            for t in range(PACK):
                if t % 2 == 0:
                    bank = bank_tile((4, 0, 2)[group] + t // 2, [P, BANK], "y_bank")
                y[group, t] = bank[:, (t % 2) * width_of(group) : (t % 2 + 1) * width_of(group)]
                nc.tensor.matmul_mx(
                    out=y[group, t],
                    lhsT=w2_codes[:, t * P : (t + 1) * P].bitcast(FP8X4),
                    lhsT_scale=w2_scales[:, t * P : (t + 1) * P],
                    rhs=z_codes[:].bitcast(FP8X4),
                    rhs_scale=z_scales[:],
                    start=True,
                    stop=True,
                )

        def combine(group, planes_a_store):
            result[group] = keep.tile([P, PACK, width_of(group)], F32, name="result_%d" % group)
            rows = out_0[:, groups[group]].rearrange("(p t) v -> p t v", t=PACK)
            for t in range(PACK):
                nc.vector.scalar_tensor_tensor(
                    out=result[group][:, t, :],
                    in0=y[group, t],
                    scalar=turn_share[:, t : t + 1],
                    in1=z_part[:, t, groups[group]],
                    op0=MULT,
                    op1=ADD,
                )
                if (t + 1) % planes_a_store == 0:
                    planes = slice(t + 1 - planes_a_store, t + 1)
                    nc.sync.dma_start(out=rows[:, planes, :], in_=result[group][:, planes, :])

        def round_results(name, shares):
            cols = slice(groups[shares[0][0]].start, groups[shares[-1][0]].stop)
            out_bf = keep.tile([P, cols.stop - cols.start, PACK], BF16, name=name, align_bytes=64)
            for group, copy in shares:
                own_cols = slice(groups[group].start - cols.start, groups[group].stop - cols.start)
                interleave(copy, out_bf[:, own_cols, :], result[group][:])
            return cols, out_bf

        def hand_on(cols, out_bf):
            nc.vector.quantize_mx(
                out=out_codes[:, cols].bitcast(FP8X4),
                scales=out_scales[:, cols],
                in_=out_bf[:].rearrange("p v t -> p (v t)"),
            )
            nc.sync.dma_start(
                out=out_1[0].rearrange("p n r -> p (n r)").bitcast(I32)[:, cols], in_=out_codes[:, cols].bitcast(I32)
            )

        for group, half, cols in ((0, 0, early), (1, 1, slice(0, P)), (2, 1, slice(P, GROUP))):
            nc.vector.scalar_tensor_tensor(
                out=z_part[:, PAIR:PACK, groups[group]],
                in0=high_backs[half][:, :, cols],
                scalar=SUM_TO_PART,
                in1=last_terms[:, :, groups[group]],
                op0=MULT,
                op1=ADD,
            )
            round_z(group)
        second_product(0)
        second_product(1)
        second_product(2)
        combine(0, PAIR)
        combine(1, PACK)
        combine(2, PACK)
        first_rounded_out = round_results("out_bf_first", [(0, nc.scalar.copy)])
        last_rounded_out = round_results("out_bf_last", [(1, nc.scalar.copy), (2, nc.vector.tensor_copy)])
        hand_on(*first_rounded_out)
        hand_on(*last_rounded_out)

        for q in range(P // QUADRANT):
            queue = nc.sync if q % 2 == 0 else nc.scalar
            queue.dma_start(
                out=out_2[0, SCALE_ROWS * q : SCALE_ROWS * (q + 1), :].bitcast(I32),
                in_=out_scales[QUADRANT * q : QUADRANT * q + SCALE_ROWS, :].bitcast(I32),
            )
